import numpy as np
import ml_dtypes


def mxq(x, axis, fmt="e4m3"):
    dtype, down = {"e4m3": (ml_dtypes.float8_e4m3fn, 7), "e5m2": (ml_dtypes.float8_e5m2, 14)}[fmt]
    v = np.moveaxis(np.asarray(x, np.float32).astype(ml_dtypes.bfloat16).astype(np.float64), axis, -1)
    blocks = v.reshape(v.shape[:-1] + (-1, 32))
    amax = np.abs(blocks).max(-1, keepdims=True)
    byte = np.maximum(np.where(amax > 0, np.frexp(amax)[1] - 1 + 127, 0) - down, 1)
    scale = np.exp2(byte - 127.0)
    codes = (blocks / scale).astype(np.float32).astype(dtype).astype(np.float64)
    return np.moveaxis((codes * scale).reshape(v.shape), -1, axis)


WIDE = False


def mx_kscale(k):
    if not WIDE:
        return np.ones(k)
    levels = np.array([10, -10, 5, -5, 0])
    if k % 512:
        return np.exp2(np.random.permutation(np.resize(levels, k // 32))).repeat(32)
    a = np.empty((k // 512, 16))
    for p in range(k // 512):
        a[p, :8] = np.random.permutation(np.resize(levels, 8))
        for g in range(8):
            far = levels[np.abs(levels - a[p, g]) >= 10]
            a[p, g + 8] = far[np.random.randint(len(far))]
    return np.exp2(a.ravel()).repeat(32)


def f64(x):
    return np.asarray(x).astype(np.float64)


def striped8(idx):
    return np.concatenate([x.reshape(-1, 16).T for x in idx]).astype(np.uint16)


def runs(offs, k):
    lists = np.stack([offs[16 * r : 16 * r + 16].T.reshape(-1) for r in range(8)]).astype(np.int64)
    return lists[np.arange(k) % 512 // 64]


def pack_weight(w):
    k, n = w.shape
    w = f64(np.asarray(w, np.float32).astype(ml_dtypes.bfloat16)).reshape(k // 32, 32, n)
    amax = np.abs(w).max(1)
    byte = np.clip(np.where(amax > 0, np.frexp(amax)[1] - 1 + 127 - 7, 1), 1, 254)
    scaled = (w * np.exp2(127.0 - byte)[:, None, :]).reshape(k, n).astype(np.float32)
    words = np.ascontiguousarray(scaled.reshape(k // 512, 128, 4, n).transpose(0, 1, 3, 2)).astype(ml_dtypes.float8_e4m3fn).view(np.uint8)
    return words, np.ascontiguousarray(byte.astype(np.uint8).reshape(k // 512, 16, n))


def unpack_weight(words, scales):
    g, p, n, _ = words.shape
    vals = np.ascontiguousarray(words).view(ml_dtypes.float8_e4m3fn).astype(np.float64) * np.repeat(np.exp2(scales.astype(np.float64) - 127.0), 8, axis=1)[..., None]
    return vals.transpose(0, 1, 3, 2).reshape(g * 512, n)


def silu(v):
    return v / (1.0 + np.exp(-np.maximum(v, -700.0)))

def planes(y):
    n, m = y.shape
    v = y.astype(np.float32).astype(ml_dtypes.bfloat16).astype(np.float64).reshape(n // 32, 32, m)
    top = np.abs(v).max(1)
    byte = np.clip(np.where(top > 0, np.frexp(top)[1] - 1 + 127 - 7, 1), 1, 254)
    codes = (v * np.exp2(127.0 - byte)[:, None, :]).reshape(n, m).astype(np.float32).astype(ml_dtypes.float8_e4m3fn).view(np.uint8)
    words = codes.reshape(n // 512, 128, 4, m).transpose(0, 1, 3, 2)
    return np.ascontiguousarray(words), np.ascontiguousarray(byte.astype(np.uint8).reshape(n // 512, 16, m))


K, T, S, V, N, H = 512, 2048, 1024, 512, 512, 512


def setup_inputs():
    n = np.random.standard_normal
    s = mx_kscale(K)[:, None]
    u = mx_kscale(H)
    packed_xT = pack_weight(n((K, T)) * s)
    packed_w2 = pack_weight(n((H, N)) / np.sqrt(2 * H) / u[:, None])
    packed_w3 = pack_weight(n((H, N)) / np.sqrt(2 * H) / u[:, None])
    return {
        "x_words": packed_xT[0],
        "x_scales": packed_xT[1],
        "w1": (n((K, H)) / np.sqrt(K) / s * u).astype(np.float32),
        "w2_words": packed_w2[0],
        "w2_scales": packed_w2[1],
        "w3_words": packed_w3[0],
        "w3_scales": packed_w3[1],
        "offs": striped8(np.stack([np.random.permutation(T)[:S] for _ in range(8)])),
        "order": striped8(np.stack([np.random.permutation(S) for _ in range(8)])),
    }


def reference(x_words, x_scales, w1, w2_words, w2_scales, w3_words, w3_scales, offs, order):
    xq = unpack_weight(x_words, x_scales)[np.arange(K)[:, None], runs(offs, K)]
    y = mxq(f64(w1), 0, "e4m3").T @ xq
    o = y[np.arange(H)[:, None], runs(order, H)]
    mx = o.reshape(H, V, 2).max(axis=2)
    z = silu(mx)
    mn = o.reshape(H, V, 2).min(axis=2)
    z2 = silu(mn)
    out_0 = unpack_weight(w2_words, w2_scales).T @ mxq(z, 0, "e4m3") + unpack_weight(w3_words, w3_scales).T @ mxq(z2, 0, "e4m3")
    return (out_0,) + planes(out_0)

@@ -1,0 +1,198 @@
+from contextlib import ExitStack
+
+import concourse.mybir as mybir
+
+K, T, S, V, N, H = 512, 2048, 1024, 512, 512, 512
+FLOPS = 2 * K * H * S + 2 * 2 * H * N * V
+
+F32 = mybir.dt.float32
+BF16 = mybir.dt.bfloat16
+I32 = mybir.dt.int32
+U32 = mybir.dt.uint32
+U16 = mybir.dt.uint16
+U8 = mybir.dt.uint8
+FP8X4 = mybir.dt.float8_e4m3fn_x4
+SILU = mybir.ActivationFunctionType.Silu
+MAX = mybir.AluOpType.max
+MIN = mybir.AluOpType.min
+
+P = 128
+PACK = 4
+BANK = 512
+CHUNK = 128
+W1_SCALAR_TAIL = 24
+
+
+def tile_picked_winmax_silu_po_kernel(
+    tc, x_words, x_scales, w1, w2_words, w2_scales, w3_words, w3_scales, offs, order, out_0, out_1, out_2
+):
+    nc = tc.nc
+    with ExitStack() as ctx:
+        held = ctx.enter_context(tc.tile_pool(name="held", bufs=1))
+        ring = ctx.enter_context(tc.tile_pool(name="ring", bufs=2))
+        psum = ctx.enter_context(tc.psum_pool(name="psum", bufs=8))
+
+        offs_sb = held.tile([P, S // 16], U16)
+        order_sb = held.tile([P, S // 16], U16)
+        xs_window = held.tile([P, T], U8, tag="xs_then_w23", align_bytes=64)
+        xw_window = held.tile([P, T], U32, align_bytes=64)
+        w1_raw = [held.tile([P, PACK, H // 2], F32, name=f"w1_raw{half}") for half in range(2)]
+
+        nc.sync.dma_start(offs_sb[:], offs)
+        nc.sync.dma_start(
+            xs_window[:].bitcast(I32),
+            x_scales[0].bitcast(I32).rearrange("q (one c) -> q one c", one=1).to_broadcast([16, 8, T // 4]),
+        )
+        nc.sync.dma_start(xw_window[:].bitcast(I32), x_words[0].rearrange("p c r -> p (c r)").bitcast(I32))
+        w1_rows = w1.rearrange("(p j) h -> p j h", j=PACK)
+        for half in range(2):
+            nc.sync.dma_start(w1_raw[half][:], w1_rows[:, :, half * (H // 2) : (half + 1) * (H // 2)])
+        nc.sync.dma_start(order_sb[:], order)
+
+        warm = held.tile([P, 2], F32)
+        nc.vector.memset(warm[:, 0:1], 0.0)
+        nc.scalar.activation(warm[:, 1:2], warm[:, 0:1], SILU)
+
+        xq_scales = held.tile([P, S], U8, align_bytes=64)
+        nc.gpsimd.memset(xq_scales[:].bitcast(I32), 0)
+
+        xs_picked = held.tile([P, S], U8, tag="picked_then_ws", align_bytes=64)
+        nc.vector.tensor_copy(xs_picked[:], xs_window[:].indirect(offs_sb[:]))
+        for b in range(4):
+            nc.scalar.dma_start(xq_scales[b:P:32, :].bitcast(I32), xs_picked[8 * b : P : 32, :].bitcast(I32))
+        xq_words = held.tile([P, S], U32, align_bytes=64)
+        nc.vector.tensor_copy(xq_words[:], xw_window[:].indirect(offs_sb[:]))
+
+        w23_raw = held.tile([P, 2, N], I32, tag="xs_then_w23", align_bytes=64)
+        for which, words in enumerate((w2_words, w3_words)):
+            nc.sync.dma_start(w23_raw[:, which, :], words[0].rearrange("p c r -> p (c r)").bitcast(I32))
+
+        ws_raw = held.tile([P, N], U8, tag="picked_then_ws", align_bytes=64)
+        nc.gpsimd.memset(ws_raw[:].bitcast(I32), 0)
+        for which, scales in enumerate((w2_scales, w3_scales)):
+            rows = scales[0].bitcast(I32)
+            for q in range(4):
+                first = 32 * q + 4 * which
+                nc.sync.dma_start(ws_raw[first : first + 4, :].bitcast(I32), rows[4 * q : 4 * q + 4, :])
+
+        w1_bf = held.tile([P, PACK, P, PACK], BF16, align_bytes=64)
+        w1_dealt = w1_bf[:].rearrange("p t m j -> p m j t")
+
+        def w1_source(half, first, last):
+            return w1_raw[half][:].rearrange("p j (m t) -> p m j t", t=PACK)[:, first:last]
+
+        split = 64 - W1_SCALAR_TAIL
+        nc.scalar.copy(w1_dealt[:, 0:64], w1_source(0, 0, 64))
+        nc.vector.tensor_copy(w1_dealt[:, 64 : 64 + split], w1_source(1, 0, split))
+        nc.scalar.copy(w1_dealt[:, 64 + split : 128], w1_source(1, split, 64))
+        w1_codes = held.tile([P, H], U32, align_bytes=64)
+        w1_scales = held.tile([P, H], U8, align_bytes=64)
+        for t in range(PACK):
+            cols = slice(t * P, (t + 1) * P)
+            nc.vector.quantize_mx(
+                out=w1_codes[:, cols].bitcast(FP8X4),
+                scales=w1_scales[:, cols],
+                in_=w1_bf[:, t].rearrange("p m j -> p (m j)"),
+            )
+
+        y = [held.tile([P, S], F32, name=f"y{t}") for t in range(PACK)]
+        for t in range(PACK):
+            cols = slice(t * P, (t + 1) * P)
+            for half in range(S // BANK):
+                places = slice(half * BANK, (half + 1) * BANK)
+                bank = psum.tile([P, BANK], F32, tag="bank")
+                nc.tensor.matmul_mx(
+                    out=bank[:],
+                    lhsT=w1_codes[:, cols].bitcast(FP8X4),
+                    lhsT_scale=w1_scales[:, cols],
+                    rhs=xq_words[:, places].bitcast(FP8X4),
+                    rhs_scale=xq_scales[:, places],
+                    start=True,
+                    stop=True,
+                )
+                if (t, half) == (0, 1):
+                    nc.vector.tensor_copy(y[t][:, places], bank[:])
+                else:
+                    nc.scalar.copy(y[t][:, places], bank[:])
+
+        w23_codes = held.tile([P, 2, PACK, P], I32, align_bytes=64)
+        nc.vector.tensor_copy(
+            w23_codes[:].rearrange("p w t m -> p w m t"), w23_raw[:].rearrange("p w (m t) -> p w m t", t=PACK)
+        )
+        w23_scales = held.tile([P, PACK, P], U8, align_bytes=64)
+        nc.vector.tensor_copy(
+            w23_scales[:].rearrange("p t m -> p m t"), ws_raw[:].rearrange("p (m t) -> p m t", t=PACK)
+        )
+
+        out_codes = held.tile([P, V], U32, align_bytes=64)
+        out_scales = held.tile([P, V], U8, align_bytes=64)
+        out_rows = out_0.rearrange("(p t) v -> p t v", t=PACK)
+        out_words = out_1[0].rearrange("p v r -> p (v r)").bitcast(I32)
+        z = {}
+
+        def pool_pairs(c, u):
+            picked = ring.tile([P, 2, 2 * CHUNK], F32, tag="picked")
+            entries = order_sb[:, c * (2 * CHUNK // 16) : (c + 1) * (2 * CHUNK // 16)]
+            for i in range(2):
+                nc.vector.tensor_copy(picked[:, i, :], y[2 * u + i][:].indirect(entries))
+            pairs = picked[:].rearrange("p i (v e) -> p i v e", e=2)
+            pooled = ring.tile([P, 2, 2, CHUNK], F32, tag="pooled", bufs=3)
+            nc.vector.tensor_tensor(pooled[:, 0], pairs[:, :, :, 0], pairs[:, :, :, 1], MAX)
+            nc.vector.tensor_tensor(pooled[:, 1], pairs[:, :, :, 0], pairs[:, :, :, 1], MIN)
+            if u == 0:
+                z[c] = ring.tile([P, 2, CHUNK, PACK], BF16, tag="z", bufs=3, align_bytes=64, name="z")
+            nc.scalar.activation(
+                z[c][:, :, :, 2 * u : 2 * u + 2], pooled[:].rearrange("p w i v -> p w v i"), SILU
+            )
+
+        def second_product(c):
+            cols = slice(c * CHUNK, (c + 1) * CHUNK)
+            z_codes = ring.tile([P, 2, CHUNK], U32, tag="z_codes", align_bytes=64)
+            z_scales = ring.tile([P, 2, CHUNK], U8, tag="z_scales", align_bytes=64)
+            nc.vector.quantize_mx(
+                out=z_codes[:].rearrange("p w v -> p (w v)").bitcast(FP8X4),
+                scales=z_scales[:].rearrange("p w v -> p (w v)"),
+                in_=z[c][:].rearrange("p w v t -> p (w v t)"),
+            )
+            bank = psum.tile([P, PACK, CHUNK], F32, tag="bank")
+            for t in range(PACK):
+                for w in range(2):
+                    nc.tensor.matmul_mx(
+                        out=bank[:, t, :],
+                        lhsT=w23_codes[:, w, t, :].bitcast(FP8X4),
+                        lhsT_scale=w23_scales[4 * w : P, t, :],
+                        rhs=z_codes[:, w, :].bitcast(FP8X4),
+                        rhs_scale=z_scales[:, w, :],
+                        start=(w == 0),
+                        stop=(w == 1),
+                    )
+            rounded = ring.tile([P, CHUNK, PACK], BF16, tag="rounded", align_bytes=64)
+            result = ring.tile([P, PACK, CHUNK], F32, tag="result")
+            if c == V // CHUNK - 1:
+                nc.vector.tensor_copy(rounded[:], bank[:].rearrange("p t v -> p v t"))
+            else:
+                nc.scalar.copy(rounded[:], bank[:].rearrange("p t v -> p v t"))
+            nc.scalar.copy(result[:], bank[:])
+            nc.sync.dma_start(out_rows[:, :, cols], result[:])
+            nc.vector.quantize_mx(
+                out=out_codes[:, cols].bitcast(FP8X4),
+                scales=out_scales[:, cols],
+                in_=rounded[:].rearrange("p v t -> p (v t)"),
+            )
+            nc.sync.dma_start(out_words[:, cols], out_codes[:, cols].bitcast(I32))
+
+        pool_pairs(0, 0)
+        pool_pairs(1, 0)
+        pool_pairs(0, 1)
+        second_product(0)
+        pool_pairs(1, 1)
+        second_product(1)
+        for c in range(2, V // CHUNK):
+            pool_pairs(c, 0)
+            pool_pairs(c, 1)
+            second_product(c)
+
+        scale_rows = out_2[0].bitcast(I32)
+        for q in range(4):
+            queue = nc.scalar if q % 2 else nc.sync
+            queue.dma_start(scale_rows[4 * q : 4 * q + 4, :], out_scales[32 * q : 32 * q + 4, :].bitcast(I32))

@@ -20,7 +20,7 @@ P = 128
 PACK = 4
 BANK = 512
 CHUNK = 128
-W1_SCALAR_TAIL = 24
+W1_SCALAR_TAIL = 44
 
 
 def tile_picked_winmax_silu_po_kernel(
@@ -35,7 +35,7 @@ def tile_picked_winmax_silu_po_kernel(
         offs_sb = held.tile([P, S // 16], U16)
         order_sb = held.tile([P, S // 16], U16)
         xs_window = held.tile([P, T], U8, tag="xs_then_w23", align_bytes=64)
-        xw_window = held.tile([P, T], U32, align_bytes=64)
+        xw_window = held.tile([P, T], U32, tag="xw_then_ws", align_bytes=64)
         w1_raw = [held.tile([P, PACK, H // 2], F32, name=f"w1_raw{half}") for half in range(2)]
 
         nc.sync.dma_start(offs_sb[:], offs)
@@ -56,10 +56,10 @@ def tile_picked_winmax_silu_po_kernel(
         xq_scales = held.tile([P, S], U8, align_bytes=64)
         nc.gpsimd.memset(xq_scales[:].bitcast(I32), 0)
 
-        xs_picked = held.tile([P, S], U8, tag="picked_then_ws", align_bytes=64)
+        xs_picked = held.tile([P, S], U8, align_bytes=64)
         nc.vector.tensor_copy(xs_picked[:], xs_window[:].indirect(offs_sb[:]))
         for b in range(4):
-            nc.scalar.dma_start(xq_scales[b:P:32, :].bitcast(I32), xs_picked[8 * b : P : 32, :].bitcast(I32))
+            nc.sync.dma_start(xq_scales[b:P:32, :].bitcast(I32), xs_picked[8 * b : P : 32, :].bitcast(I32))
         xq_words = held.tile([P, S], U32, align_bytes=64)
         nc.vector.tensor_copy(xq_words[:], xw_window[:].indirect(offs_sb[:]))
 
@@ -67,7 +67,7 @@ def tile_picked_winmax_silu_po_kernel(
         for which, words in enumerate((w2_words, w3_words)):
             nc.sync.dma_start(w23_raw[:, which, :], words[0].rearrange("p c r -> p (c r)").bitcast(I32))
 
-        ws_raw = held.tile([P, N], U8, tag="picked_then_ws", align_bytes=64)
+        ws_raw = held.tile([P, N], U8, tag="xw_then_ws", align_bytes=64)
         nc.gpsimd.memset(ws_raw[:].bitcast(I32), 0)
         for which, scales in enumerate((w2_scales, w3_scales)):
             rows = scales[0].bitcast(I32)
@@ -98,9 +98,10 @@ def tile_picked_winmax_silu_po_kernel(
         y = [held.tile([P, S], F32, name=f"y{t}") for t in range(PACK)]
         for t in range(PACK):
             cols = slice(t * P, (t + 1) * P)
-            for half in range(S // BANK):
-                places = slice(half * BANK, (half + 1) * BANK)
-                bank = psum.tile([P, BANK], F32, tag="bank")
+            width = BANK // 2 if t == 0 else BANK
+            for part in range(S // width):
+                places = slice(part * width, (part + 1) * width)
+                bank = psum.tile([P, width], F32, tag="bank")
                 nc.tensor.matmul_mx(
                     out=bank[:],
                     lhsT=w1_codes[:, cols].bitcast(FP8X4),
@@ -110,10 +111,7 @@ def tile_picked_winmax_silu_po_kernel(
                     start=True,
                     stop=True,
                 )
-                if (t, half) == (0, 1):
-                    nc.vector.tensor_copy(y[t][:, places], bank[:])
-                else:
-                    nc.scalar.copy(y[t][:, places], bank[:])
+                nc.scalar.copy(y[t][:, places], bank[:])
 
         w23_codes = held.tile([P, 2, PACK, P], I32, align_bytes=64)
         nc.vector.tensor_copy(
@@ -130,50 +128,70 @@ def tile_picked_winmax_silu_po_kernel(
         out_words = out_1[0].rearrange("p v r -> p (v r)").bitcast(I32)
         z = {}
 
-        def pool_pairs(c, u):
-            picked = ring.tile([P, 2, 2 * CHUNK], F32, tag="picked")
+        chunks = V // CHUNK
+        banks = {}
+        result = held.tile([P, chunks, PACK, CHUNK], F32)
+
+        def gather(c, tiles, tag):
+            picked = ring.tile([P, len(tiles), CHUNK, 2], F32, tag=tag, align_bytes=64, name="picked")
             entries = order_sb[:, c * (2 * CHUNK // 16) : (c + 1) * (2 * CHUNK // 16)]
-            for i in range(2):
-                nc.vector.tensor_copy(picked[:, i, :], y[2 * u + i][:].indirect(entries))
-            pairs = picked[:].rearrange("p i (v e) -> p i v e", e=2)
-            pooled = ring.tile([P, 2, 2, CHUNK], F32, tag="pooled", bufs=3)
-            nc.vector.tensor_tensor(pooled[:, 0], pairs[:, :, :, 0], pairs[:, :, :, 1], MAX)
-            nc.vector.tensor_tensor(pooled[:, 1], pairs[:, :, :, 0], pairs[:, :, :, 1], MIN)
+            for i, t in enumerate(tiles):
+                nc.vector.tensor_copy(picked[:, i].rearrange("p v e -> p (v e)"), y[t][:].indirect(entries))
+            return picked
+
+        def pool_pairs(c, u):
+            pooled = ring.tile([P, 2, 2, CHUNK], F32, tag="pooled")
+            if (c, u) == (chunks - 1, 1):
+                parts = [((2,), "picked"), ((3,), "z")]
+            else:
+                parts = [((2 * u, 2 * u + 1), "picked")]
+            for tiles, tag in parts:
+                picked = gather(c, tiles, tag)
+                rows = slice(tiles[0] % 2, tiles[-1] % 2 + 1)
+                for w, op in enumerate((MAX, MIN)):
+                    nc.vector.tensor_tensor(pooled[:, w, rows], picked[:, :, :, 0], picked[:, :, :, 1], op)
             if u == 0:
-                z[c] = ring.tile([P, 2, CHUNK, PACK], BF16, tag="z", bufs=3, align_bytes=64, name="z")
-            nc.scalar.activation(
-                z[c][:, :, :, 2 * u : 2 * u + 2], pooled[:].rearrange("p w i v -> p w v i"), SILU
-            )
+                z[c] = ring.tile([P, 2, CHUNK, PACK], BF16, tag="z", align_bytes=64, name="z")
+            for w in range(2):
+                nc.scalar.activation(z[c][:, w, :, 2 * u : 2 * u + 2], pooled[:, w].rearrange("p i v -> p v i"), SILU)
 
         def second_product(c):
-            cols = slice(c * CHUNK, (c + 1) * CHUNK)
             z_codes = ring.tile([P, 2, CHUNK], U32, tag="z_codes", align_bytes=64)
             z_scales = ring.tile([P, 2, CHUNK], U8, tag="z_scales", align_bytes=64)
-            nc.vector.quantize_mx(
-                out=z_codes[:].rearrange("p w v -> p (w v)").bitcast(FP8X4),
-                scales=z_scales[:].rearrange("p w v -> p (w v)"),
-                in_=z[c][:].rearrange("p w v t -> p (w v t)"),
-            )
-            bank = psum.tile([P, PACK, CHUNK], F32, tag="bank")
-            for t in range(PACK):
-                for w in range(2):
-                    nc.tensor.matmul_mx(
-                        out=bank[:, t, :],
-                        lhsT=w23_codes[:, w, t, :].bitcast(FP8X4),
-                        lhsT_scale=w23_scales[4 * w : P, t, :],
-                        rhs=z_codes[:, w, :].bitcast(FP8X4),
-                        rhs_scale=z_scales[:, w, :],
-                        start=(w == 0),
-                        stop=(w == 1),
-                    )
+            for w in range(2):
+                nc.vector.quantize_mx(
+                    out=z_codes[:, w].bitcast(FP8X4),
+                    scales=z_scales[:, w],
+                    in_=z[c][:, w].rearrange("p v t -> p (v t)"),
+                )
+            per_bank = 2 if c == chunks - 1 else PACK
+            banks[c] = []
+            for first in range(0, PACK, per_bank):
+                bank = psum.tile([P, per_bank, CHUNK], F32, tag="bank")
+                banks[c].append((slice(first, first + per_bank), bank))
+                for i in range(per_bank):
+                    for w in range(2):
+                        nc.tensor.matmul_mx(
+                            out=bank[:, i, :],
+                            lhsT=w23_codes[:, w, first + i, :].bitcast(FP8X4),
+                            lhsT_scale=w23_scales[4 * w : P, first + i, :],
+                            rhs=z_codes[:, w, :].bitcast(FP8X4),
+                            rhs_scale=z_scales[:, w, :],
+                            start=(w == 0),
+                            stop=(w == 1),
+                        )
+
+        def hand_out(c):
+            cols = slice(c * CHUNK, (c + 1) * CHUNK)
             rounded = ring.tile([P, CHUNK, PACK], BF16, tag="rounded", align_bytes=64)
-            result = ring.tile([P, PACK, CHUNK], F32, tag="result")
-            if c == V // CHUNK - 1:
-                nc.vector.tensor_copy(rounded[:], bank[:].rearrange("p t v -> p v t"))
-            else:
-                nc.scalar.copy(rounded[:], bank[:].rearrange("p t v -> p v t"))
-            nc.scalar.copy(result[:], bank[:])
-            nc.sync.dma_start(out_rows[:, :, cols], result[:])
+            for tiles, bank in banks[c]:
+                if c == chunks - 1:
+                    nc.vector.tensor_copy(rounded[:, :, tiles], bank[:].rearrange("p t v -> p v t"))
+                else:
+                    nc.scalar.copy(rounded[:, :, tiles], bank[:].rearrange("p t v -> p v t"))
+                nc.scalar.copy(result[:, c, tiles], bank[:])
+                queue = nc.scalar if c == chunks - 1 else nc.sync
+                queue.dma_start(out_rows[:, tiles, cols], result[:, c, tiles])
             nc.vector.quantize_mx(
                 out=out_codes[:, cols].bitcast(FP8X4),
                 scales=out_scales[:, cols],
@@ -181,18 +199,18 @@ def tile_picked_winmax_silu_po_kernel(
             )
             nc.sync.dma_start(out_words[:, cols], out_codes[:, cols].bitcast(I32))
 
-        pool_pairs(0, 0)
-        pool_pairs(1, 0)
-        pool_pairs(0, 1)
-        second_product(0)
-        pool_pairs(1, 1)
-        second_product(1)
-        for c in range(2, V // CHUNK):
+        for c in range(2):
             pool_pairs(c, 0)
+        for c in range(chunks):
+            if c >= 2:
+                pool_pairs(c, 0)
             pool_pairs(c, 1)
             second_product(c)
+            if c >= 1:
+                hand_out(c - 1)
+        hand_out(chunks - 1)
 
         scale_rows = out_2[0].bitcast(I32)
         for q in range(4):
-            queue = nc.scalar if q % 2 else nc.sync
+            queue = nc.scalar if q == 3 else nc.sync
             queue.dma_start(scale_rows[4 * q : 4 * q + 4, :], out_scales[32 * q : 32 * q + 4, :].bitcast(I32))

@@ -20,7 +20,7 @@ P = 128
 PACK = 4
 BANK = 512
 CHUNK = 128
-W1_SCALAR_TAIL = 44
+W1_SCALAR_TAIL = 22
 
 
 def tile_picked_winmax_silu_po_kernel(
@@ -59,7 +59,7 @@ def tile_picked_winmax_silu_po_kernel(
         xs_picked = held.tile([P, S], U8, align_bytes=64)
         nc.vector.tensor_copy(xs_picked[:], xs_window[:].indirect(offs_sb[:]))
         for b in range(4):
-            nc.sync.dma_start(xq_scales[b:P:32, :].bitcast(I32), xs_picked[8 * b : P : 32, :].bitcast(I32))
+            nc.scalar.dma_start(xq_scales[b:P:32, :].bitcast(I32), xs_picked[8 * b : P : 32, :].bitcast(I32))
         xq_words = held.tile([P, S], U32, align_bytes=64)
         nc.vector.tensor_copy(xq_words[:], xw_window[:].indirect(offs_sb[:]))
 
@@ -76,10 +76,10 @@ def tile_picked_winmax_silu_po_kernel(
                 nc.sync.dma_start(ws_raw[first : first + 4, :].bitcast(I32), rows[4 * q : 4 * q + 4, :])
 
         w1_bf = held.tile([P, PACK, P, PACK], BF16, align_bytes=64)
-        w1_dealt = w1_bf[:].rearrange("p t m j -> p m j t")
+        w1_dealt = w1_bf[:].rearrange("p t m j -> p m t j")
 
         def w1_source(half, first, last):
-            return w1_raw[half][:].rearrange("p j (m t) -> p m j t", t=PACK)[:, first:last]
+            return w1_raw[half][:].rearrange("p j (m t) -> p m t j", t=PACK)[:, first:last]
 
         split = 64 - W1_SCALAR_TAIL
         nc.scalar.copy(w1_dealt[:, 0:64], w1_source(0, 0, 64))
@@ -115,11 +115,12 @@ def tile_picked_winmax_silu_po_kernel(
 
         w23_codes = held.tile([P, 2, PACK, P], I32, align_bytes=64)
         nc.vector.tensor_copy(
-            w23_codes[:].rearrange("p w t m -> p w m t"), w23_raw[:].rearrange("p w (m t) -> p w m t", t=PACK)
+            w23_codes[:].rearrange("p w t (g i) -> p w g t i", i=PACK),
+            w23_raw[:].rearrange("p w (g i t) -> p w g t i", i=PACK, t=PACK),
         )
         w23_scales = held.tile([P, PACK, P], U8, align_bytes=64)
         nc.vector.tensor_copy(
-            w23_scales[:].rearrange("p t m -> p m t"), ws_raw[:].rearrange("p (m t) -> p m t", t=PACK)
+            w23_scales[:], ws_raw[:].rearrange("p (m t) -> p t m", t=PACK)
         )
 
         out_codes = held.tile([P, V], U32, align_bytes=64)

@@ -35,7 +35,7 @@ def tile_picked_winmax_silu_po_kernel(
         offs_sb = held.tile([P, S // 16], U16)
         order_sb = held.tile([P, S // 16], U16)
         xs_window = held.tile([P, T], U8, tag="xs_then_w23", align_bytes=64)
-        xw_window = held.tile([P, T], U32, tag="xw_then_ws", align_bytes=64)
+        xw_window = held.tile([P, T], U32, align_bytes=64)
         w1_raw = [held.tile([P, PACK, H // 2], F32, name=f"w1_raw{half}") for half in range(2)]
 
         nc.sync.dma_start(offs_sb[:], offs)
@@ -53,7 +53,7 @@ def tile_picked_winmax_silu_po_kernel(
         nc.vector.memset(warm[:, 0:1], 0.0)
         nc.scalar.activation(warm[:, 1:2], warm[:, 0:1], SILU)
 
-        xq_scales = held.tile([P, S], U8, align_bytes=64)
+        xq_scales = held.tile([P, S], U8, tag="xq_then_w23_scales", align_bytes=64)
         nc.gpsimd.memset(xq_scales[:].bitcast(I32), 0)
 
         xs_picked = held.tile([P, S], U8, align_bytes=64)
@@ -67,15 +67,7 @@ def tile_picked_winmax_silu_po_kernel(
         for which, words in enumerate((w2_words, w3_words)):
             nc.sync.dma_start(w23_raw[:, which, :], words[0].rearrange("p c r -> p (c r)").bitcast(I32))
 
-        ws_raw = held.tile([P, N], U8, tag="xw_then_ws", align_bytes=64)
-        nc.gpsimd.memset(ws_raw[:].bitcast(I32), 0)
-        for which, scales in enumerate((w2_scales, w3_scales)):
-            rows = scales[0].bitcast(I32)
-            for q in range(4):
-                first = 32 * q + 4 * which
-                nc.sync.dma_start(ws_raw[first : first + 4, :].bitcast(I32), rows[4 * q : 4 * q + 4, :])
-
-        w1_bf = held.tile([P, PACK, P, PACK], BF16, align_bytes=64)
+        w1_bf = held.tile([P, PACK, P, PACK], BF16, tag="w1_bf_then_ws", align_bytes=64)
         w1_dealt = w1_bf[:].rearrange("p t m j -> p m t j")
 
         def w1_source(half, first, last):
@@ -94,6 +86,14 @@ def tile_picked_winmax_silu_po_kernel(
                 scales=w1_scales[:, cols],
                 in_=w1_bf[:, t].rearrange("p m j -> p (m j)"),
             )
+
+        ws_raw = held.tile([P, N], U8, tag="w1_bf_then_ws", align_bytes=64)
+        nc.vector.memset(ws_raw[:].bitcast(I32), 0)
+        for which, scales in enumerate((w2_scales, w3_scales)):
+            rows = scales[0].bitcast(I32)
+            for q in range(4):
+                first = 32 * q + 4 * which
+                nc.sync.dma_start(ws_raw[first : first + 4, :].bitcast(I32), rows[4 * q : 4 * q + 4, :])
 
         y = [held.tile([P, S], F32, name=f"y{t}") for t in range(PACK)]
         for t in range(PACK):
@@ -118,7 +118,7 @@ def tile_picked_winmax_silu_po_kernel(
             w23_codes[:].rearrange("p w t (g i) -> p w g t i", i=PACK),
             w23_raw[:].rearrange("p w (g i t) -> p w g t i", i=PACK, t=PACK),
         )
-        w23_scales = held.tile([P, PACK, P], U8, align_bytes=64)
+        w23_scales = held.tile([P, PACK, P], U8, tag="xq_then_w23_scales", align_bytes=64)
         nc.vector.tensor_copy(
             w23_scales[:], ws_raw[:].rearrange("p (m t) -> p t m", t=PACK)
         )
@@ -133,39 +133,37 @@ def tile_picked_winmax_silu_po_kernel(
         banks = {}
         result = held.tile([P, chunks, PACK, CHUNK], F32)
 
-        def gather(c, tiles, tag):
-            picked = ring.tile([P, len(tiles), CHUNK, 2], F32, tag=tag, align_bytes=64, name="picked")
+        last = chunks - 1
+        pooled = {}
+
+        def pool_pairs(c, tiles):
+            picked = ring.tile([P, len(tiles), CHUNK, 2], F32, tag="picked")
             entries = order_sb[:, c * (2 * CHUNK // 16) : (c + 1) * (2 * CHUNK // 16)]
             for i, t in enumerate(tiles):
                 nc.vector.tensor_copy(picked[:, i].rearrange("p v e -> p (v e)"), y[t][:].indirect(entries))
-            return picked
-
-        def pool_pairs(c, u):
-            pooled = ring.tile([P, 2, 2, CHUNK], F32, tag="pooled")
-            if (c, u) == (chunks - 1, 1):
-                parts = [((2,), "picked"), ((3,), "z")]
-            else:
-                parts = [((2 * u, 2 * u + 1), "picked")]
-            for tiles, tag in parts:
-                picked = gather(c, tiles, tag)
-                rows = slice(tiles[0] % 2, tiles[-1] % 2 + 1)
-                for w, op in enumerate((MAX, MIN)):
-                    nc.vector.tensor_tensor(pooled[:, w, rows], picked[:, :, :, 0], picked[:, :, :, 1], op)
-            if u == 0:
+            if tiles[0] == 0:
+                pooled[c] = ring.tile([P, 2, PACK, CHUNK], F32, tag="pooled", name="pooled")
                 z[c] = ring.tile([P, 2, CHUNK, PACK], BF16, tag="z", align_bytes=64, name="z")
-            for w in range(2):
-                nc.scalar.activation(z[c][:, w, :, 2 * u : 2 * u + 2], pooled[:, w].rearrange("p i v -> p v i"), SILU)
+            for w, op in enumerate((MAX, MIN)):
+                nc.vector.tensor_tensor(
+                    pooled[c][:, w, tiles[0] : tiles[-1] + 1], picked[:, :, :, 0], picked[:, :, :, 1], op
+                )
+
+        def silu(c, kinds, tiles):
+            nc.scalar.activation(
+                z[c][:, kinds, :, tiles], pooled[c][:, kinds, tiles].rearrange("p w t v -> p w v t"), SILU
+            )
 
         def second_product(c):
             z_codes = ring.tile([P, 2, CHUNK], U32, tag="z_codes", align_bytes=64)
             z_scales = ring.tile([P, 2, CHUNK], U8, tag="z_scales", align_bytes=64)
-            for w in range(2):
+            for kinds in (slice(0, 1), slice(1, 2)) if c == last else (slice(0, 2),):
                 nc.vector.quantize_mx(
-                    out=z_codes[:, w].bitcast(FP8X4),
-                    scales=z_scales[:, w],
-                    in_=z[c][:, w].rearrange("p v t -> p (v t)"),
+                    out=z_codes[:, kinds].rearrange("p w v -> p (w v)").bitcast(FP8X4),
+                    scales=z_scales[:, kinds].rearrange("p w v -> p (w v)"),
+                    in_=z[c][:, kinds].rearrange("p w v t -> p (w v t)"),
                 )
-            per_bank = 2 if c == chunks - 1 else PACK
+            per_bank = 2 if c == last else PACK
             banks[c] = []
             for first in range(0, PACK, per_bank):
                 bank = psum.tile([P, per_bank, CHUNK], F32, tag="bank")
@@ -186,12 +184,12 @@ def tile_picked_winmax_silu_po_kernel(
             cols = slice(c * CHUNK, (c + 1) * CHUNK)
             rounded = ring.tile([P, CHUNK, PACK], BF16, tag="rounded", align_bytes=64)
             for tiles, bank in banks[c]:
-                if c == chunks - 1:
+                if c == last:
                     nc.vector.tensor_copy(rounded[:, :, tiles], bank[:].rearrange("p t v -> p v t"))
                 else:
                     nc.scalar.copy(rounded[:, :, tiles], bank[:].rearrange("p t v -> p v t"))
                 nc.scalar.copy(result[:, c, tiles], bank[:])
-                queue = nc.scalar if c == chunks - 1 else nc.sync
+                queue = nc.scalar if c == last and tiles.stop == PACK else nc.sync
                 queue.dma_start(out_rows[:, tiles, cols], result[:, c, tiles])
             nc.vector.quantize_mx(
                 out=out_codes[:, cols].bitcast(FP8X4),
@@ -200,16 +198,30 @@ def tile_picked_winmax_silu_po_kernel(
             )
             nc.sync.dma_start(out_words[:, cols], out_codes[:, cols].bitcast(I32))
 
+        both, low, high = slice(0, 2), slice(0, 2), slice(2, 4)
         for c in range(2):
-            pool_pairs(c, 0)
-        for c in range(chunks):
-            if c >= 2:
-                pool_pairs(c, 0)
-            pool_pairs(c, 1)
+            pool_pairs(c, (0, 1))
+            silu(c, both, low)
+        for c in range(2):
+            pool_pairs(c, (2, 3))
+            silu(c, both, high)
             second_product(c)
-            if c >= 1:
-                hand_out(c - 1)
-        hand_out(chunks - 1)
+        hand_out(0)
+        for c in range(2, last):
+            pool_pairs(c, (0, 1))
+            pool_pairs(c, (2, 3))
+            silu(c, both, slice(0, PACK))
+            second_product(c)
+            hand_out(c - 1)
+        pool_pairs(last, (0, 1))
+        silu(last, both, low)
+        pool_pairs(last, (2,))
+        pool_pairs(last, (3,))
+        for w in range(2):
+            silu(last, slice(w, w + 1), high)
+        second_product(last)
+        hand_out(last - 1)
+        hand_out(last)
 
         scale_rows = out_2[0].bitcast(I32)
         for q in range(4):

@@ -20,7 +20,6 @@ P = 128
 PACK = 4
 BANK = 512
 CHUNK = 128
-W1_SCALAR_TAIL = 22
 
 
 def tile_picked_winmax_silu_po_kernel(
@@ -29,12 +28,13 @@ def tile_picked_winmax_silu_po_kernel(
     nc = tc.nc
     with ExitStack() as ctx:
         held = ctx.enter_context(tc.tile_pool(name="held", bufs=1))
-        ring = ctx.enter_context(tc.tile_pool(name="ring", bufs=2))
+        late = ctx.enter_context(tc.tile_pool(name="late", bufs=1))
+        early = ctx.enter_context(tc.tile_pool(name="early", bufs=1))
         psum = ctx.enter_context(tc.psum_pool(name="psum", bufs=8))
 
         offs_sb = held.tile([P, S // 16], U16)
         order_sb = held.tile([P, S // 16], U16)
-        xs_window = held.tile([P, T], U8, tag="xs_then_w23", align_bytes=64)
+        xs_window = early.tile([P, T], U8, offset=2048, align_bytes=64)
         xw_window = held.tile([P, T], U32, align_bytes=64)
         w1_raw = [held.tile([P, PACK, H // 2], F32, name=f"w1_raw{half}") for half in range(2)]
 
@@ -44,56 +44,67 @@ def tile_picked_winmax_silu_po_kernel(
             x_scales[0].bitcast(I32).rearrange("q (one c) -> q one c", one=1).to_broadcast([16, 8, T // 4]),
         )
         nc.sync.dma_start(xw_window[:].bitcast(I32), x_words[0].rearrange("p c r -> p (c r)").bitcast(I32))
+        nc.sync.dma_start(order_sb[:], order)
         w1_rows = w1.rearrange("(p j) h -> p j h", j=PACK)
         for half in range(2):
             nc.sync.dma_start(w1_raw[half][:], w1_rows[:, :, half * (H // 2) : (half + 1) * (H // 2)])
-        nc.sync.dma_start(order_sb[:], order)
 
         warm = held.tile([P, 2], F32)
         nc.vector.memset(warm[:, 0:1], 0.0)
         nc.scalar.activation(warm[:, 1:2], warm[:, 0:1], SILU)
 
-        xq_scales = held.tile([P, S], U8, tag="xq_then_w23_scales", align_bytes=64)
+        xq_scales = held.tile([P, S], U8, align_bytes=64)
         nc.gpsimd.memset(xq_scales[:].bitcast(I32), 0)
 
         xs_picked = held.tile([P, S], U8, align_bytes=64)
         nc.vector.tensor_copy(xs_picked[:], xs_window[:].indirect(offs_sb[:]))
         for b in range(4):
-            nc.scalar.dma_start(xq_scales[b:P:32, :].bitcast(I32), xs_picked[8 * b : P : 32, :].bitcast(I32))
+            queue = nc.sync if b % 2 == 0 else nc.scalar
+            queue.dma_start(xq_scales[b:P:32, :].bitcast(I32), xs_picked[8 * b : P : 32, :].bitcast(I32))
         xq_words = held.tile([P, S], U32, align_bytes=64)
         nc.vector.tensor_copy(xq_words[:], xw_window[:].indirect(offs_sb[:]))
 
-        w23_raw = held.tile([P, 2, N], I32, tag="xs_then_w23", align_bytes=64)
-        for which, words in enumerate((w2_words, w3_words)):
-            nc.sync.dma_start(w23_raw[:, which, :], words[0].rearrange("p c r -> p (c r)").bitcast(I32))
-
-        w1_bf = held.tile([P, PACK, P, PACK], BF16, tag="w1_bf_then_ws", align_bytes=64)
-        w1_dealt = w1_bf[:].rearrange("p t m j -> p m t j")
-
-        def w1_source(half, first, last):
-            return w1_raw[half][:].rearrange("p j (m t) -> p m t j", t=PACK)[:, first:last]
-
-        split = 64 - W1_SCALAR_TAIL
-        nc.scalar.copy(w1_dealt[:, 0:64], w1_source(0, 0, 64))
-        nc.vector.tensor_copy(w1_dealt[:, 64 : 64 + split], w1_source(1, 0, split))
-        nc.scalar.copy(w1_dealt[:, 64 + split : 128], w1_source(1, split, 64))
-        w1_codes = held.tile([P, H], U32, align_bytes=64)
-        w1_scales = held.tile([P, H], U8, align_bytes=64)
-        for t in range(PACK):
-            cols = slice(t * P, (t + 1) * P)
-            nc.vector.quantize_mx(
-                out=w1_codes[:, cols].bitcast(FP8X4),
-                scales=w1_scales[:, cols],
-                in_=w1_bf[:, t].rearrange("p m j -> p (m j)"),
-            )
-
-        ws_raw = held.tile([P, N], U8, tag="w1_bf_then_ws", align_bytes=64)
-        nc.vector.memset(ws_raw[:].bitcast(I32), 0)
+        w23_raw = [early.tile([P, N], I32, name=f"w23_raw{w}", offset=256 + 2560 * w) for w in range(2)]
+        for w, words in enumerate((w2_words, w3_words)):
+            nc.sync.dma_start(w23_raw[w][:], words[0].rearrange("p c r -> p (c r)").bitcast(I32))
+        ws_raw = early.tile([P, N], U8, offset=2304, align_bytes=64)
+        nc.gpsimd.memset(ws_raw[:].bitcast(I32), 0)
         for which, scales in enumerate((w2_scales, w3_scales)):
             rows = scales[0].bitcast(I32)
             for q in range(4):
                 first = 32 * q + 4 * which
                 nc.sync.dma_start(ws_raw[first : first + 4, :].bitcast(I32), rows[4 * q : 4 * q + 4, :])
+
+        w1_bf = held.tile([P, PACK, P, PACK], BF16, align_bytes=64)
+        w1_dealt = w1_bf[:].rearrange("p t m j -> p m t j")
+
+        def round_w1(half, tiles):
+            source = w1_raw[half][:].rearrange("p j (m t) -> p m t j", t=PACK)
+            nc.scalar.copy(w1_dealt[:, 64 * half : 64 * half + 64, tiles], source[:, :, tiles])
+
+        w1_codes = held.tile([P, H], U32, align_bytes=64)
+        w1_scales = held.tile([P, H], U8, align_bytes=64)
+
+        def quantise_w1(tiles):
+            cols = slice(tiles.start * P, tiles.stop * P)
+            nc.vector.quantize_mx(
+                out=w1_codes[:, cols].bitcast(FP8X4),
+                scales=w1_scales[:, cols],
+                in_=w1_bf[:, tiles].rearrange("p t m j -> p (t m j)"),
+            )
+
+        round_w1(0, slice(0, 4))
+        round_w1(1, slice(0, 2))
+        round_w1(1, slice(2, 4))
+        for tiles in (slice(0, 1), slice(1, 2), slice(2, 4)):
+            quantise_w1(tiles)
+
+        w23_codes = held.tile([P, 2, PACK, P], I32, align_bytes=64)
+        for w in range(2):
+            nc.vector.tensor_copy(
+                w23_codes[:, w].rearrange("p t (g i) -> p g t i", i=PACK),
+                w23_raw[w][:].rearrange("p (g i t) -> p g t i", i=PACK, t=PACK),
+            )
 
         y = [held.tile([P, S], F32, name=f"y{t}") for t in range(PACK)]
         for t in range(PACK):
@@ -113,117 +124,158 @@ def tile_picked_winmax_silu_po_kernel(
                 )
                 nc.scalar.copy(y[t][:, places], bank[:])
 
-        w23_codes = held.tile([P, 2, PACK, P], I32, align_bytes=64)
-        nc.vector.tensor_copy(
-            w23_codes[:].rearrange("p w t (g i) -> p w g t i", i=PACK),
-            w23_raw[:].rearrange("p w (g i t) -> p w g t i", i=PACK, t=PACK),
-        )
-        w23_scales = held.tile([P, PACK, P], U8, tag="xq_then_w23_scales", align_bytes=64)
-        nc.vector.tensor_copy(
-            w23_scales[:], ws_raw[:].rearrange("p (m t) -> p t m", t=PACK)
-        )
+        w23_scales = held.tile([P, PACK, P], U8, align_bytes=64)
+        nc.gpsimd.tensor_copy(w23_scales[:], ws_raw[:].rearrange("p (m t) -> p t m", t=PACK))
 
         out_codes = held.tile([P, V], U32, align_bytes=64)
         out_scales = held.tile([P, V], U8, align_bytes=64)
         out_rows = out_0.rearrange("(p t) v -> p t v", t=PACK)
         out_words = out_1[0].rearrange("p v r -> p (v r)").bitcast(I32)
-        z = {}
 
         chunks = V // CHUNK
-        banks = {}
-        result = held.tile([P, chunks, PACK, CHUNK], F32)
-
         last = chunks - 1
-        pooled = {}
+        result = {}
+        z = {}
+        z_codes = {}
+        z_scales = {}
+        banks = {}
 
-        def pool_pairs(c, tiles):
-            picked = ring.tile([P, len(tiles), CHUNK, 2], F32, tag="picked")
-            entries = order_sb[:, c * (2 * CHUNK // 16) : (c + 1) * (2 * CHUNK // 16)]
-            for i, t in enumerate(tiles):
-                nc.vector.tensor_copy(picked[:, i].rearrange("p v e -> p (v e)"), y[t][:].indirect(entries))
-            if tiles[0] == 0:
-                pooled[c] = ring.tile([P, 2, PACK, CHUNK], F32, tag="pooled", name="pooled")
-                z[c] = ring.tile([P, 2, CHUNK, PACK], BF16, tag="z", align_bytes=64, name="z")
+        def fetch(first, count, t, into):
+            entries = order_sb[:, first * (2 * CHUNK // 16) : (first + count) * (2 * CHUNK // 16)]
+            nc.vector.tensor_copy(into, y[t][:].indirect(entries))
+
+        def pool_pairs(pooled, pairs):
             for w, op in enumerate((MAX, MIN)):
-                nc.vector.tensor_tensor(
-                    pooled[c][:, w, tiles[0] : tiles[-1] + 1], picked[:, :, :, 0], picked[:, :, :, 1], op
-                )
+                nc.vector.tensor_tensor(pooled[:, :, w], pairs[:, :, :, 0], pairs[:, :, :, 1], op)
 
-        def silu(c, kinds, tiles):
+        def silu(c, kinds, tiles, pooled):
             nc.scalar.activation(
-                z[c][:, kinds, :, tiles], pooled[c][:, kinds, tiles].rearrange("p w t v -> p w v t"), SILU
+                z[c][:, kinds, :, tiles].rearrange("p w (g i) t -> p (w g) t i", i=PACK),
+                pooled[:, :, kinds].rearrange("p t w (g i) -> p (w g) t i", i=PACK),
+                SILU,
+            )
+
+        def quantise_z(c, kinds):
+            nc.vector.quantize_mx(
+                out=z_codes[c][:, kinds].rearrange("p w v -> p (w v)").bitcast(FP8X4),
+                scales=z_scales[c][:, kinds].rearrange("p w v -> p (w v)"),
+                in_=z[c][:, kinds].rearrange("p w v t -> p (w v t)"),
+            )
+
+        def multiply(c, t, w, into):
+            nc.tensor.matmul_mx(
+                out=into,
+                lhsT=w23_codes[:, w, t, :].bitcast(FP8X4),
+                lhsT_scale=w23_scales[4 * w : P, t, :],
+                rhs=z_codes[c][:, w, :].bitcast(FP8X4),
+                rhs_scale=z_scales[c][:, w, :],
+                start=(w == 0),
+                stop=(w == 1),
             )
 
         def second_product(c):
-            z_codes = ring.tile([P, 2, CHUNK], U32, tag="z_codes", align_bytes=64)
-            z_scales = ring.tile([P, 2, CHUNK], U8, tag="z_scales", align_bytes=64)
-            for kinds in (slice(0, 1), slice(1, 2)) if c == last else (slice(0, 2),):
-                nc.vector.quantize_mx(
-                    out=z_codes[:, kinds].rearrange("p w v -> p (w v)").bitcast(FP8X4),
-                    scales=z_scales[:, kinds].rearrange("p w v -> p (w v)"),
-                    in_=z[c][:, kinds].rearrange("p w v t -> p (w v t)"),
-                )
-            per_bank = 2 if c == last else PACK
-            banks[c] = []
-            for first in range(0, PACK, per_bank):
-                bank = psum.tile([P, per_bank, CHUNK], F32, tag="bank")
-                banks[c].append((slice(first, first + per_bank), bank))
-                for i in range(per_bank):
-                    for w in range(2):
-                        nc.tensor.matmul_mx(
-                            out=bank[:, i, :],
-                            lhsT=w23_codes[:, w, first + i, :].bitcast(FP8X4),
-                            lhsT_scale=w23_scales[4 * w : P, first + i, :],
-                            rhs=z_codes[:, w, :].bitcast(FP8X4),
-                            rhs_scale=z_scales[:, w, :],
-                            start=(w == 0),
-                            stop=(w == 1),
-                        )
+            quantise_z(c, both)
+            banks[c] = psum.tile([P, PACK, CHUNK], F32, tag="bank", name="bank")
+            for t in range(PACK):
+                for w in range(2):
+                    multiply(c, t, w, banks[c][:, t, :])
 
-        def hand_out(c):
+        def store_result(c):
             cols = slice(c * CHUNK, (c + 1) * CHUNK)
-            rounded = ring.tile([P, CHUNK, PACK], BF16, tag="rounded", align_bytes=64)
-            for tiles, bank in banks[c]:
-                if c == last:
-                    nc.vector.tensor_copy(rounded[:, :, tiles], bank[:].rearrange("p t v -> p v t"))
-                else:
-                    nc.scalar.copy(rounded[:, :, tiles], bank[:].rearrange("p t v -> p v t"))
-                nc.scalar.copy(result[:, c, tiles], bank[:])
-                queue = nc.scalar if c == last and tiles.stop == PACK else nc.sync
-                queue.dma_start(out_rows[:, tiles, cols], result[:, c, tiles])
+            nc.sync.dma_start(out_rows[:, :, cols], result[c][:])
+
+        def quantise_result(cols, rounded):
             nc.vector.quantize_mx(
                 out=out_codes[:, cols].bitcast(FP8X4),
                 scales=out_scales[:, cols],
-                in_=rounded[:].rearrange("p v t -> p (v t)"),
+                in_=rounded.rearrange("p v t -> p (v t)"),
             )
-            nc.sync.dma_start(out_words[:, cols], out_codes[:, cols].bitcast(I32))
 
-        both, low, high = slice(0, 2), slice(0, 2), slice(2, 4)
+        both, every = slice(0, 2), slice(0, PACK)
+        for c in range(chunks):
+            z[c] = held.tile([P, 2, CHUNK, PACK], BF16, align_bytes=64, name=f"z{c}")
+            z_codes[c] = held.tile([P, 2, CHUNK], U32, align_bytes=64, name=f"z_codes{c}")
+            z_scales[c] = held.tile([P, 2, CHUNK], U8, align_bytes=64, name=f"z_scales{c}")
+
+        picked = held.tile([P, PACK * 4 * CHUNK], F32)
+
+        def slot(t, first, count):
+            start = (2 * t + first) * 2 * CHUNK
+            return picked[:, start : start + count * 2 * CHUNK]
+
+        def pairs_of(which, tiles):
+            return picked[:].rearrange("p (t s v e) -> p t s v e", t=PACK, s=2, e=2)[:, 0:tiles, which]
+
+        for t in range(PACK - 1):
+            fetch(0, 2, t, slot(t, 0, 2))
         for c in range(2):
-            pool_pairs(c, (0, 1))
-            silu(c, both, low)
-        for c in range(2):
-            pool_pairs(c, (2, 3))
-            silu(c, both, high)
-            second_product(c)
+            fetch(c, 1, PACK - 1, slot(PACK - 1, c, 1))
+        pooled0 = late.tile([P, PACK, 2, CHUNK], F32, offset=0)
+        pooled1 = held.tile([P, PACK, 2, CHUNK], F32)
+        for c, pooled in enumerate((pooled0, pooled1)):
+            pool_pairs(pooled[:], pairs_of(c, PACK))
+            silu(c, both, every, pooled[:])
+        second_product(0)
+        second_product(1)
+
+        for t in range(PACK):
+            fetch(2, 1, t, slot(t, 0, 1))
+        pooled2 = late.tile([P, PACK, 2, CHUNK], F32, offset=0)
+        pool_pairs(pooled2[:], pairs_of(0, PACK))
+        silu(2, both, every, pooled2[:])
+        rounded01 = held.tile([P, 2 * CHUNK, PACK], BF16, align_bytes=64)
+
+        def hand_out(c):
+            result[c] = held.tile([P, PACK, CHUNK], F32, name=f"result{c}")
+            nc.scalar.copy(result[c][:], banks[c][:])
+            nc.scalar.copy(rounded01[:, c * CHUNK : (c + 1) * CHUNK], banks[c][:].rearrange("p t v -> p v t"))
+            store_result(c)
+
         hand_out(0)
-        for c in range(2, last):
-            pool_pairs(c, (0, 1))
-            pool_pairs(c, (2, 3))
-            silu(c, both, slice(0, PACK))
-            second_product(c)
-            hand_out(c - 1)
-        pool_pairs(last, (0, 1))
-        silu(last, both, low)
-        pool_pairs(last, (2,))
-        pool_pairs(last, (3,))
+        for t in range(PACK - 1):
+            fetch(last, 1, t, slot(t, 1, 1))
+        second_product(2)
+
+        pooled3 = late.tile([P, PACK - 1, 2, CHUNK], F32, offset=0)
+        pool_pairs(pooled3[:], pairs_of(1, PACK - 1))
+        silu(last, both, slice(0, PACK - 1), pooled3[:])
+        picked_end = late.tile([P, 1, CHUNK, 2], F32, offset=3072)
+        fetch(last, 1, PACK - 1, picked_end[:].rearrange("p t v e -> p (t v e)"))
+        pooled_end = late.tile([P, 1, 2, CHUNK], F32, offset=5120)
+        pool_pairs(pooled_end[:], picked_end[:])
+        end_banks = [psum.tile([P, CHUNK], F32, tag="bank", name="bank") for t in range(PACK)]
         for w in range(2):
-            silu(last, slice(w, w + 1), high)
-        second_product(last)
-        hand_out(last - 1)
-        hand_out(last)
+            silu(last, slice(w, w + 1), slice(PACK - 1, PACK), pooled_end[:])
+            quantise_z(last, slice(w, w + 1))
+            for t in range(PACK):
+                multiply(last, t, w, end_banks[t][:])
+        hand_out(1)
+        quantise_result(slice(0, 2 * CHUNK), rounded01[:])
+        nc.sync.dma_start(out_words[:, 0 : 2 * CHUNK], out_codes[:, 0 : 2 * CHUNK].bitcast(I32))
+
+        rounded2 = late.tile([P, CHUNK, PACK], BF16, offset=4608, align_bytes=64)
+        nc.scalar.copy(rounded2[:], banks[2][:].rearrange("p t v -> p v t"))
+        result[2] = late.tile([P, PACK, CHUNK], F32, offset=5632, name="result2")
+        nc.scalar.copy(result[2][:], banks[2][:])
+        store_result(2)
+        quantise_result(slice(2 * CHUNK, 3 * CHUNK), rounded2[:])
+
+        result[last] = held.tile([P, PACK, CHUNK], F32, name="result3")
+        for t in range(PACK):
+            if t == PACK - 1:
+                nc.scalar.copy(result[last][:, t], end_banks[t][:])
+            else:
+                nc.vector.tensor_copy(result[last][:, t], end_banks[t][:])
+        store_result(last)
+        rounded3 = held.tile([P, CHUNK, PACK], BF16, align_bytes=64)
+        nc.vector.tensor_copy(
+            rounded3[:].rearrange("p (g i) t -> p g t i", i=PACK),
+            result[last][:].rearrange("p t (g i) -> p g t i", i=PACK),
+        )
+        quantise_result(slice(last * CHUNK, V), rounded3[:])
+        nc.sync.dma_start(out_words[:, 2 * CHUNK : V], out_codes[:, 2 * CHUNK : V].bitcast(I32))
 
         scale_rows = out_2[0].bitcast(I32)
         for q in range(4):
-            queue = nc.scalar if q == 3 else nc.sync
+            queue = nc.scalar if q % 2 == 0 else nc.sync
             queue.dma_start(scale_rows[4 * q : 4 * q + 4, :], out_scales[32 * q : 32 * q + 4, :].bitcast(I32))

@@ -15,11 +15,14 @@ FP8X4 = mybir.dt.float8_e4m3fn_x4
 SILU = mybir.ActivationFunctionType.Silu
 MAX = mybir.AluOpType.max
 MIN = mybir.AluOpType.min
+ADD = mybir.AluOpType.add
+SUBTRACT = mybir.AluOpType.subtract
 
 P = 128
 PACK = 4
 BANK = 512
 CHUNK = 128
+W1_PIECES = ((0, 64), (64, 128))
 
 
 def tile_picked_winmax_silu_po_kernel(
@@ -36,7 +39,7 @@ def tile_picked_winmax_silu_po_kernel(
         order_sb = held.tile([P, S // 16], U16)
         xs_window = early.tile([P, T], U8, offset=2048, align_bytes=64)
         xw_window = held.tile([P, T], U32, align_bytes=64)
-        w1_raw = [held.tile([P, PACK, H // 2], F32, name=f"w1_raw{half}") for half in range(2)]
+        w1_raw = [held.tile([P, PACK, PACK * (b - a)], F32, name=f"w1_raw{a}") for a, b in W1_PIECES]
 
         nc.sync.dma_start(offs_sb[:], offs)
         nc.sync.dma_start(
@@ -46,8 +49,8 @@ def tile_picked_winmax_silu_po_kernel(
         nc.sync.dma_start(xw_window[:].bitcast(I32), x_words[0].rearrange("p c r -> p (c r)").bitcast(I32))
         nc.sync.dma_start(order_sb[:], order)
         w1_rows = w1.rearrange("(p j) h -> p j h", j=PACK)
-        for half in range(2):
-            nc.sync.dma_start(w1_raw[half][:], w1_rows[:, :, half * (H // 2) : (half + 1) * (H // 2)])
+        for piece, (a, b) in enumerate(W1_PIECES):
+            nc.sync.dma_start(w1_raw[piece][:], w1_rows[:, :, PACK * a : PACK * b])
 
         warm = held.tile([P, 2], F32)
         nc.vector.memset(warm[:, 0:1], 0.0)
@@ -80,7 +83,7 @@ def tile_picked_winmax_silu_po_kernel(
 
         def round_w1(half, tiles):
             source = w1_raw[half][:].rearrange("p j (m t) -> p m t j", t=PACK)
-            nc.scalar.copy(w1_dealt[:, 64 * half : 64 * half + 64, tiles], source[:, :, tiles])
+            nc.scalar.copy(w1_dealt[:, W1_PIECES[half][0] : W1_PIECES[half][1], tiles], source[:, :, tiles])
 
         w1_codes = held.tile([P, H], U32, align_bytes=64)
         w1_scales = held.tile([P, H], U8, align_bytes=64)
@@ -128,7 +131,6 @@ def tile_picked_winmax_silu_po_kernel(
         nc.gpsimd.tensor_copy(w23_scales[:], ws_raw[:].rearrange("p (m t) -> p t m", t=PACK))
 
         out_codes = held.tile([P, V], U32, align_bytes=64)
-        out_scales = held.tile([P, V], U8, align_bytes=64)
         out_rows = out_0.rearrange("(p t) v -> p t v", t=PACK)
         out_words = out_1[0].rearrange("p v r -> p (v r)").bitcast(I32)
 
@@ -148,12 +150,15 @@ def tile_picked_winmax_silu_po_kernel(
             for w, op in enumerate((MAX, MIN)):
                 nc.vector.tensor_tensor(pooled[:, :, w], pairs[:, :, :, 0], pairs[:, :, :, 1], op)
 
-        def silu(c, kinds, tiles, pooled):
+        def silu_of(c, kinds, tiles, values):
             nc.scalar.activation(
                 z[c][:, kinds, :, tiles].rearrange("p w (g i) t -> p (w g) t i", i=PACK),
-                pooled[:, :, kinds].rearrange("p t w (g i) -> p (w g) t i", i=PACK),
+                values.rearrange("p t w (g i) -> p (w g) t i", i=PACK),
                 SILU,
             )
+
+        def silu(c, kinds, tiles, pooled):
+            silu_of(c, kinds, tiles, pooled[:, :, kinds])
 
         def quantise_z(c, kinds):
             nc.vector.quantize_mx(
@@ -206,15 +211,27 @@ def tile_picked_winmax_silu_po_kernel(
         def pairs_of(which, tiles):
             return picked[:].rearrange("p (t s v e) -> p t s v e", t=PACK, s=2, e=2)[:, 0:tiles, which]
 
+        sums = held.tile([P, PACK - 1, 2, CHUNK], F32)
         for t in range(PACK - 1):
             fetch(0, 2, t, slot(t, 0, 2))
+            pairs = slot(t, 0, 2).rearrange("p (v e) -> p v e", e=2)
+            nc.gpsimd.tensor_tensor(sums[:, t].rearrange("p c v -> p (c v)"), pairs[:, :, 0], pairs[:, :, 1], ADD)
         for c in range(2):
             fetch(c, 1, PACK - 1, slot(PACK - 1, c, 1))
-        pooled0 = late.tile([P, PACK, 2, CHUNK], F32, offset=0)
-        pooled1 = held.tile([P, PACK, 2, CHUNK], F32)
-        for c, pooled in enumerate((pooled0, pooled1)):
-            pool_pairs(pooled[:], pairs_of(c, PACK))
-            silu(c, both, every, pooled[:])
+        larger = [held.tile([P, PACK, 1, CHUNK], F32, name=f"larger{c}") for c in range(2)]
+        smaller0 = late.tile([P, PACK, 1, CHUNK], F32, offset=3072)
+        smaller1 = held.tile([P, PACK, 1, CHUNK], F32)
+        smaller = [smaller0, smaller1]
+        for c in range(2):
+            pairs = pairs_of(c, PACK)
+            nc.vector.tensor_tensor(larger[c][:, :, 0], pairs[:, :, :, 0], pairs[:, :, :, 1], MAX)
+            silu_of(c, slice(0, 1), every, larger[c][:])
+        for c in range(2):
+            pairs = pairs_of(c, PACK)[:, PACK - 1]
+            nc.vector.tensor_tensor(smaller[c][:, PACK - 1, 0], pairs[:, :, 0], pairs[:, :, 1], MIN)
+        for c in range(2):
+            nc.gpsimd.tensor_tensor(smaller[c][:, 0 : PACK - 1, 0], sums[:, :, c], larger[c][:, 0 : PACK - 1, 0], SUBTRACT)
+            silu_of(c, slice(1, 2), every, smaller[c][:])
         second_product(0)
         second_product(1)
 
@@ -232,16 +249,17 @@ def tile_picked_winmax_silu_po_kernel(
             store_result(c)
 
         hand_out(0)
+        picked3 = late.tile([P, PACK - 1, CHUNK, 2], F32, offset=4096)
         for t in range(PACK - 1):
-            fetch(last, 1, t, slot(t, 1, 1))
+            fetch(last, 1, t, picked3[:, t].rearrange("p v e -> p (v e)"))
         second_product(2)
 
         pooled3 = late.tile([P, PACK - 1, 2, CHUNK], F32, offset=0)
-        pool_pairs(pooled3[:], pairs_of(1, PACK - 1))
+        pool_pairs(pooled3[:], picked3[:])
         silu(last, both, slice(0, PACK - 1), pooled3[:])
         picked_end = late.tile([P, 1, CHUNK, 2], F32, offset=3072)
         fetch(last, 1, PACK - 1, picked_end[:].rearrange("p t v e -> p (t v e)"))
-        pooled_end = late.tile([P, 1, 2, CHUNK], F32, offset=5120)
+        pooled_end = late.tile([P, 1, 2, CHUNK], F32, offset=8192)
         pool_pairs(pooled_end[:], picked_end[:])
         end_banks = [psum.tile([P, CHUNK], F32, tag="bank", name="bank") for t in range(PACK)]
         for w in range(2):
@@ -250,28 +268,29 @@ def tile_picked_winmax_silu_po_kernel(
             for t in range(PACK):
                 multiply(last, t, w, end_banks[t][:])
         hand_out(1)
+        out_scales = late.tile([P, V], U8, offset=3072, align_bytes=64)
         quantise_result(slice(0, 2 * CHUNK), rounded01[:])
         nc.sync.dma_start(out_words[:, 0 : 2 * CHUNK], out_codes[:, 0 : 2 * CHUNK].bitcast(I32))
 
-        rounded2 = late.tile([P, CHUNK, PACK], BF16, offset=4608, align_bytes=64)
-        nc.scalar.copy(rounded2[:], banks[2][:].rearrange("p t v -> p v t"))
-        result[2] = late.tile([P, PACK, CHUNK], F32, offset=5632, name="result2")
+        result[2] = late.tile([P, PACK, CHUNK], F32, offset=8704, name="result2")
         nc.scalar.copy(result[2][:], banks[2][:])
         store_result(2)
+        rounded2 = held.tile([P, CHUNK, PACK], BF16, align_bytes=64)
+        nc.vector.tensor_copy(
+            rounded2[:].rearrange("p (g i) t -> p g t i", i=PACK),
+            result[2][:].rearrange("p t (g i) -> p g t i", i=PACK),
+        )
         quantise_result(slice(2 * CHUNK, 3 * CHUNK), rounded2[:])
 
         result[last] = held.tile([P, PACK, CHUNK], F32, name="result3")
-        for t in range(PACK):
-            if t == PACK - 1:
-                nc.scalar.copy(result[last][:, t], end_banks[t][:])
-            else:
-                nc.vector.tensor_copy(result[last][:, t], end_banks[t][:])
-        store_result(last)
         rounded3 = held.tile([P, CHUNK, PACK], BF16, align_bytes=64)
-        nc.vector.tensor_copy(
-            rounded3[:].rearrange("p (g i) t -> p g t i", i=PACK),
-            result[last][:].rearrange("p t (g i) -> p g t i", i=PACK),
-        )
+        for t in range(PACK):
+            nc.scalar.copy(result[last][:, t], end_banks[t][:])
+            if t % 2 == 1:
+                nc.sync.dma_start(out_rows[:, t - 1 : t + 1, last * CHUNK : V], result[last][:, t - 1 : t + 1])
+                nc.vector.tensor_copy(
+                    rounded3[:, :, t - 1 : t + 1], result[last][:, t - 1 : t + 1].rearrange("p t v -> p v t")
+                )
         quantise_result(slice(last * CHUNK, V), rounded3[:])
         nc.sync.dma_start(out_words[:, 2 * CHUNK : V], out_codes[:, 2 * CHUNK : V].bitcast(I32))
 

@@ -22,6 +22,7 @@ P = 128
 PACK = 4
 BANK = 512
 CHUNK = 128
+GPSIMD_TILES = (3, 2)
 W1_PIECES = ((0, 64), (64, 128))
 
 
@@ -202,43 +203,52 @@ def tile_picked_winmax_silu_po_kernel(
             z_codes[c] = held.tile([P, 2, CHUNK], U32, align_bytes=64, name=f"z_codes{c}")
             z_scales[c] = held.tile([P, 2, CHUNK], U8, align_bytes=64, name=f"z_scales{c}")
 
-        picked = held.tile([P, PACK * 4 * CHUNK], F32)
+        span = 2 * CHUNK
+        row = held.tile([P, 10 * span], F32)
 
-        def slot(t, first, count):
-            start = (2 * t + first) * 2 * CHUNK
-            return picked[:, start : start + count * 2 * CHUNK]
+        def slot(c, t, count=1):
+            start = (7 + t) * span if c == last else (2 * t + c % 2) * span
+            return row[:, start : start + count * span]
 
-        def pairs_of(which, tiles):
-            return picked[:].rearrange("p (t s v e) -> p t s v e", t=PACK, s=2, e=2)[:, 0:tiles, which]
+        def pairs_of(c, tiles):
+            if c == last:
+                return row[:, 7 * span : 10 * span].rearrange("p (t v e) -> p t v e", t=tiles, e=2)
+            return row[:, 0 : 8 * span].rearrange("p (t s v e) -> p t s v e", t=PACK, s=2, e=2)[:, :, c % 2]
 
         sums = held.tile([P, PACK - 1, 2, CHUNK], F32)
         for t in range(PACK - 1):
-            fetch(0, 2, t, slot(t, 0, 2))
-            pairs = slot(t, 0, 2).rearrange("p (v e) -> p v e", e=2)
-            nc.gpsimd.tensor_tensor(sums[:, t].rearrange("p c v -> p (c v)"), pairs[:, :, 0], pairs[:, :, 1], ADD)
+            fetch(0, 2, t, slot(0, t, 2))
+            count = len([c for c in range(2) if t < GPSIMD_TILES[c]])
+            pairs = slot(0, t, count).rearrange("p (v e) -> p v e", e=2)
+            nc.gpsimd.tensor_tensor(
+                sums[:, t, 0:count].rearrange("p c v -> p (c v)"), pairs[:, :, 0], pairs[:, :, 1], ADD
+            )
         for c in range(2):
-            fetch(c, 1, PACK - 1, slot(PACK - 1, c, 1))
-        larger = [held.tile([P, PACK, 1, CHUNK], F32, name=f"larger{c}") for c in range(2)]
-        smaller0 = late.tile([P, PACK, 1, CHUNK], F32, offset=3072)
-        smaller1 = held.tile([P, PACK, 1, CHUNK], F32)
-        smaller = [smaller0, smaller1]
-        for c in range(2):
-            pairs = pairs_of(c, PACK)
-            nc.vector.tensor_tensor(larger[c][:, :, 0], pairs[:, :, :, 0], pairs[:, :, :, 1], MAX)
-            silu_of(c, slice(0, 1), every, larger[c][:])
-        for c in range(2):
-            pairs = pairs_of(c, PACK)[:, PACK - 1]
-            nc.vector.tensor_tensor(smaller[c][:, PACK - 1, 0], pairs[:, :, 0], pairs[:, :, 1], MIN)
-        for c in range(2):
-            nc.gpsimd.tensor_tensor(smaller[c][:, 0 : PACK - 1, 0], sums[:, :, c], larger[c][:, 0 : PACK - 1, 0], SUBTRACT)
-            silu_of(c, slice(1, 2), every, smaller[c][:])
-        second_product(0)
-        second_product(1)
+            fetch(c, 1, PACK - 1, slot(c, PACK - 1))
 
-        for t in range(PACK):
-            fetch(2, 1, t, slot(t, 0, 1))
+        def split_pool(c, larger, smaller):
+            pairs = pairs_of(c, PACK)
+            nc.vector.tensor_tensor(larger[:, :, 0], pairs[:, :, :, 0], pairs[:, :, :, 1], MAX)
+            silu_of(c, slice(0, 1), every, larger)
+            n = GPSIMD_TILES[c]
+            nc.vector.tensor_tensor(smaller[:, n:PACK, 0], pairs[:, n:PACK, :, 0], pairs[:, n:PACK, :, 1], MIN)
+            nc.gpsimd.tensor_tensor(smaller[:, 0:n, 0], sums[:, 0:n, c], larger[:, 0:n, 0], SUBTRACT)
+            silu_of(c, slice(1, 2), every, smaller)
+
+        larger0 = held.tile([P, PACK, 1, CHUNK], F32)
+        smaller0 = late.tile([P, PACK, 1, CHUNK], F32, offset=4096)
+        split_pool(0, larger0[:], smaller0[:])
+        for t in range(PACK - 1):
+            fetch(2, 1, t, slot(2, t))
+        second_product(0)
+        larger1 = late.tile([P, PACK, 1, CHUNK], F32, offset=4096)
+        smaller1 = row[:, 8 * span : 10 * span].rearrange("p (t w v) -> p t w v", t=PACK, w=1)
+        split_pool(1, larger1[:], smaller1)
+        fetch(2, 1, PACK - 1, slot(2, PACK - 1))
+        fetch(last, 1, 0, slot(last, 0))
         pooled2 = late.tile([P, PACK, 2, CHUNK], F32, offset=0)
-        pool_pairs(pooled2[:], pairs_of(0, PACK))
+        pool_pairs(pooled2[:], pairs_of(2, PACK))
+        second_product(1)
         silu(2, both, every, pooled2[:])
         rounded01 = held.tile([P, 2 * CHUNK, PACK], BF16, align_bytes=64)
 
@@ -249,13 +259,12 @@ def tile_picked_winmax_silu_po_kernel(
             store_result(c)
 
         hand_out(0)
-        picked3 = late.tile([P, PACK - 1, CHUNK, 2], F32, offset=4096)
-        for t in range(PACK - 1):
-            fetch(last, 1, t, picked3[:, t].rearrange("p v e -> p (v e)"))
+        for t in range(1, PACK - 1):
+            fetch(last, 1, t, slot(last, t))
         second_product(2)
 
         pooled3 = late.tile([P, PACK - 1, 2, CHUNK], F32, offset=0)
-        pool_pairs(pooled3[:], picked3[:])
+        pool_pairs(pooled3[:], pairs_of(last, PACK - 1))
         silu(last, both, slice(0, PACK - 1), pooled3[:])
         picked_end = late.tile([P, 1, CHUNK, 2], F32, offset=3072)
         fetch(last, 1, PACK - 1, picked_end[:].rearrange("p t v e -> p (t v e)"))

@@ -48,10 +48,10 @@ def tile_picked_winmax_silu_po_kernel(
             x_scales[0].bitcast(I32).rearrange("q (one c) -> q one c", one=1).to_broadcast([16, 8, T // 4]),
         )
         nc.sync.dma_start(xw_window[:].bitcast(I32), x_words[0].rearrange("p c r -> p (c r)").bitcast(I32))
-        nc.sync.dma_start(order_sb[:], order)
         w1_rows = w1.rearrange("(p j) h -> p j h", j=PACK)
         for piece, (a, b) in enumerate(W1_PIECES):
             nc.sync.dma_start(w1_raw[piece][:], w1_rows[:, :, PACK * a : PACK * b])
+        nc.sync.dma_start(order_sb[:], order)
 
         warm = held.tile([P, 2], F32)
         nc.vector.memset(warm[:, 0:1], 0.0)
@@ -80,11 +80,11 @@ def tile_picked_winmax_silu_po_kernel(
                 nc.sync.dma_start(ws_raw[first : first + 4, :].bitcast(I32), rows[4 * q : 4 * q + 4, :])
 
         w1_bf = held.tile([P, PACK, P, PACK], BF16, align_bytes=64)
-        w1_dealt = w1_bf[:].rearrange("p t m j -> p m t j")
+        w1_dealt = w1_bf[:].rearrange("p t m j -> p m j t")
 
         def round_w1(half, tiles):
-            source = w1_raw[half][:].rearrange("p j (m t) -> p m t j", t=PACK)
-            nc.scalar.copy(w1_dealt[:, W1_PIECES[half][0] : W1_PIECES[half][1], tiles], source[:, :, tiles])
+            source = w1_raw[half][:].rearrange("p j (m t) -> p m j t", t=PACK)
+            nc.scalar.copy(w1_dealt[:, W1_PIECES[half][0] : W1_PIECES[half][1], :, tiles], source[:, :, :, tiles])
 
         w1_codes = held.tile([P, H], U32, align_bytes=64)
         w1_scales = held.tile([P, H], U8, align_bytes=64)
@@ -226,24 +226,36 @@ def tile_picked_winmax_silu_po_kernel(
         for c in range(2):
             fetch(c, 1, PACK - 1, slot(c, PACK - 1))
 
-        def split_pool(c, larger, smaller):
+        def pool_larger(c, larger):
             pairs = pairs_of(c, PACK)
-            nc.vector.tensor_tensor(larger[:, :, 0], pairs[:, :, :, 0], pairs[:, :, :, 1], MAX)
+            halves = (every,) if c == 0 else (slice(2, 4), slice(0, 2))
+            for half in halves:
+                nc.vector.tensor_tensor(larger[:, half, 0], pairs[:, half, :, 0], pairs[:, half, :, 1], MAX)
             silu_of(c, slice(0, 1), every, larger)
+
+        def smaller_on_vector(c, smaller):
             n = GPSIMD_TILES[c]
+            pairs = pairs_of(c, PACK)
             nc.vector.tensor_tensor(smaller[:, n:PACK, 0], pairs[:, n:PACK, :, 0], pairs[:, n:PACK, :, 1], MIN)
+
+        def smaller_on_gpsimd(c, larger, smaller):
+            n = GPSIMD_TILES[c]
             nc.gpsimd.tensor_tensor(smaller[:, 0:n, 0], sums[:, 0:n, c], larger[:, 0:n, 0], SUBTRACT)
             silu_of(c, slice(1, 2), every, smaller)
 
-        larger0 = held.tile([P, PACK, 1, CHUNK], F32)
+        larger0 = row[:, 8 * span : 10 * span].rearrange("p (t w v) -> p t w v", t=PACK, w=1)
         smaller0 = late.tile([P, PACK, 1, CHUNK], F32, offset=4096)
-        split_pool(0, larger0[:], smaller0[:])
+        pool_larger(0, larger0)
+        smaller_on_vector(0, smaller0[:])
+        smaller_on_gpsimd(0, larger0, smaller0[:])
         for t in range(PACK - 1):
             fetch(2, 1, t, slot(2, t))
+        smaller1 = larger0
+        smaller_on_vector(1, smaller1)
         second_product(0)
         larger1 = late.tile([P, PACK, 1, CHUNK], F32, offset=4096)
-        smaller1 = row[:, 8 * span : 10 * span].rearrange("p (t w v) -> p t w v", t=PACK, w=1)
-        split_pool(1, larger1[:], smaller1)
+        pool_larger(1, larger1[:])
+        smaller_on_gpsimd(1, larger1[:], smaller1)
         fetch(2, 1, PACK - 1, slot(2, PACK - 1))
         fetch(last, 1, 0, slot(last, 0))
         pooled2 = late.tile([P, PACK, 2, CHUNK], F32, offset=0)
@@ -281,24 +293,20 @@ def tile_picked_winmax_silu_po_kernel(
         quantise_result(slice(0, 2 * CHUNK), rounded01[:])
         nc.sync.dma_start(out_words[:, 0 : 2 * CHUNK], out_codes[:, 0 : 2 * CHUNK].bitcast(I32))
 
-        result[2] = late.tile([P, PACK, CHUNK], F32, offset=8704, name="result2")
-        nc.scalar.copy(result[2][:], banks[2][:])
-        store_result(2)
+        result23 = late.tile([P, PACK, 2 * CHUNK], F32, offset=8704)
+        nc.scalar.copy(result23[:, :, 0:CHUNK], banks[2][:])
         rounded2 = held.tile([P, CHUNK, PACK], BF16, align_bytes=64)
-        nc.vector.tensor_copy(
-            rounded2[:].rearrange("p (g i) t -> p g t i", i=PACK),
-            result[2][:].rearrange("p t (g i) -> p g t i", i=PACK),
-        )
+        nc.vector.tensor_copy(rounded2[:], banks[2][:].rearrange("p t v -> p v t"))
         quantise_result(slice(2 * CHUNK, 3 * CHUNK), rounded2[:])
 
-        result[last] = held.tile([P, PACK, CHUNK], F32, name="result3")
         rounded3 = held.tile([P, CHUNK, PACK], BF16, align_bytes=64)
         for t in range(PACK):
-            nc.scalar.copy(result[last][:, t], end_banks[t][:])
+            nc.scalar.copy(result23[:, t, CHUNK : 2 * CHUNK], end_banks[t][:])
             if t % 2 == 1:
-                nc.sync.dma_start(out_rows[:, t - 1 : t + 1, last * CHUNK : V], result[last][:, t - 1 : t + 1])
+                pair = slice(t - 1, t + 1)
+                nc.sync.dma_start(out_rows[:, pair, 2 * CHUNK : V], result23[:, pair])
                 nc.vector.tensor_copy(
-                    rounded3[:, :, t - 1 : t + 1], result[last][:, t - 1 : t + 1].rearrange("p t v -> p v t")
+                    rounded3[:, :, pair], result23[:, pair, CHUNK : 2 * CHUNK].rearrange("p t v -> p v t")
                 )
         quantise_result(slice(last * CHUNK, V), rounded3[:])
         nc.sync.dma_start(out_words[:, 2 * CHUNK : V], out_codes[:, 2 * CHUNK : V].bitcast(I32))

@@ -289,26 +289,26 @@ def tile_picked_winmax_silu_po_kernel(
             for t in range(PACK):
                 multiply(last, t, w, end_banks[t][:])
         hand_out(1)
-        out_scales = late.tile([P, V], U8, offset=3072, align_bytes=64)
+        out_scales = late.tile([P, V], U8, offset=8192, align_bytes=64)
         quantise_result(slice(0, 2 * CHUNK), rounded01[:])
         nc.sync.dma_start(out_words[:, 0 : 2 * CHUNK], out_codes[:, 0 : 2 * CHUNK].bitcast(I32))
 
         result23 = late.tile([P, PACK, 2 * CHUNK], F32, offset=8704)
         nc.scalar.copy(result23[:, :, 0:CHUNK], banks[2][:])
-        rounded2 = held.tile([P, CHUNK, PACK], BF16, align_bytes=64)
-        nc.vector.tensor_copy(rounded2[:], banks[2][:].rearrange("p t v -> p v t"))
-        quantise_result(slice(2 * CHUNK, 3 * CHUNK), rounded2[:])
+        rounded23 = held.tile([P, 2 * CHUNK, PACK], BF16, align_bytes=64)
 
-        rounded3 = held.tile([P, CHUNK, PACK], BF16, align_bytes=64)
-        for t in range(PACK):
-            nc.scalar.copy(result23[:, t, CHUNK : 2 * CHUNK], end_banks[t][:])
-            if t % 2 == 1:
-                pair = slice(t - 1, t + 1)
-                nc.sync.dma_start(out_rows[:, pair, 2 * CHUNK : V], result23[:, pair])
-                nc.vector.tensor_copy(
-                    rounded3[:, :, pair], result23[:, pair, CHUNK : 2 * CHUNK].rearrange("p t v -> p v t")
-                )
-        quantise_result(slice(last * CHUNK, V), rounded3[:])
+        def round_out(cols, pair):
+            nc.vector.tensor_copy(rounded23[:, cols, pair], result23[:, pair, cols].rearrange("p t v -> p v t"))
+
+        low, high = slice(0, 2), slice(2, 4)
+        round_out(slice(0, CHUNK), high)
+        for pair, cols in ((low, slice(0, 2 * CHUNK)), (high, slice(CHUNK, 2 * CHUNK))):
+            for t in range(pair.start, pair.stop):
+                nc.scalar.copy(result23[:, t, CHUNK : 2 * CHUNK], end_banks[t][:])
+            nc.sync.dma_start(out_rows[:, pair, 2 * CHUNK : V], result23[:, pair])
+            round_out(cols, pair)
+        for c in (2, 3):
+            quantise_result(slice(c * CHUNK, (c + 1) * CHUNK), rounded23[:, (c - 2) * CHUNK : (c - 1) * CHUNK])
         nc.sync.dma_start(out_words[:, 2 * CHUNK : V], out_codes[:, 2 * CHUNK : V].bitcast(I32))
 
         scale_rows = out_2[0].bitcast(I32)

@@ -22,8 +22,17 @@ P = 128
 PACK = 4
 BANK = 512
 CHUNK = 128
-GPSIMD_TILES = (3, 2)
-W1_PIECES = ((0, 64), (64, 128))
+SPAN = 2 * CHUNK
+LAST = V // CHUNK - 1
+GPSIMD_TILES = 3
+
+XS_WINDOW_AT = 2048
+W2_RAW_AT, WS_RAW_AT, W3_RAW_AT = 256, 2304, 2816
+POOLED_AT = 0
+LAST_SMALLER_AT = 2048
+OUT_SCALES_AT = 2048
+RESULT23_AT = 3072
+SMALLER0_AT = 4096
 
 
 def tile_picked_winmax_silu_po_kernel(
@@ -38,9 +47,9 @@ def tile_picked_winmax_silu_po_kernel(
 
         offs_sb = held.tile([P, S // 16], U16)
         order_sb = held.tile([P, S // 16], U16)
-        xs_window = early.tile([P, T], U8, offset=2048, align_bytes=64)
+        xs_window = early.tile([P, T], U8, offset=XS_WINDOW_AT, align_bytes=64)
         xw_window = held.tile([P, T], U32, align_bytes=64)
-        w1_raw = [held.tile([P, PACK, PACK * (b - a)], F32, name=f"w1_raw{a}") for a, b in W1_PIECES]
+        w1_raw = [held.tile([P, PACK, H // 2], F32, name=f"w1_raw{half}") for half in range(2)]
 
         nc.sync.dma_start(offs_sb[:], offs)
         nc.sync.dma_start(
@@ -49,8 +58,8 @@ def tile_picked_winmax_silu_po_kernel(
         )
         nc.sync.dma_start(xw_window[:].bitcast(I32), x_words[0].rearrange("p c r -> p (c r)").bitcast(I32))
         w1_rows = w1.rearrange("(p j) h -> p j h", j=PACK)
-        for piece, (a, b) in enumerate(W1_PIECES):
-            nc.sync.dma_start(w1_raw[piece][:], w1_rows[:, :, PACK * a : PACK * b])
+        for half in range(2):
+            nc.sync.dma_start(w1_raw[half][:], w1_rows[:, :, half * (H // 2) : (half + 1) * (H // 2)])
         nc.sync.dma_start(order_sb[:], order)
 
         warm = held.tile([P, 2], F32)
@@ -68,15 +77,17 @@ def tile_picked_winmax_silu_po_kernel(
         xq_words = held.tile([P, S], U32, align_bytes=64)
         nc.vector.tensor_copy(xq_words[:], xw_window[:].indirect(offs_sb[:]))
 
-        w23_raw = [early.tile([P, N], I32, name=f"w23_raw{w}", offset=256 + 2560 * w) for w in range(2)]
+        w23_raw = [
+            early.tile([P, N], I32, name=f"w23_raw{w}", offset=at) for w, at in enumerate((W2_RAW_AT, W3_RAW_AT))
+        ]
         for w, words in enumerate((w2_words, w3_words)):
             nc.sync.dma_start(w23_raw[w][:], words[0].rearrange("p c r -> p (c r)").bitcast(I32))
-        ws_raw = early.tile([P, N], U8, offset=2304, align_bytes=64)
+        ws_raw = early.tile([P, N], U8, offset=WS_RAW_AT, align_bytes=64)
         nc.gpsimd.memset(ws_raw[:].bitcast(I32), 0)
-        for which, scales in enumerate((w2_scales, w3_scales)):
+        for w, scales in enumerate((w2_scales, w3_scales)):
             rows = scales[0].bitcast(I32)
             for q in range(4):
-                first = 32 * q + 4 * which
+                first = 32 * q + 4 * w
                 nc.sync.dma_start(ws_raw[first : first + 4, :].bitcast(I32), rows[4 * q : 4 * q + 4, :])
 
         w1_bf = held.tile([P, PACK, P, PACK], BF16, align_bytes=64)
@@ -84,7 +95,8 @@ def tile_picked_winmax_silu_po_kernel(
 
         def round_w1(half, tiles):
             source = w1_raw[half][:].rearrange("p j (m t) -> p m j t", t=PACK)
-            nc.scalar.copy(w1_dealt[:, W1_PIECES[half][0] : W1_PIECES[half][1], :, tiles], source[:, :, :, tiles])
+            places = slice(half * (P // 2), (half + 1) * (P // 2))
+            nc.scalar.copy(w1_dealt[:, places, :, tiles], source[:, :, :, tiles])
 
         w1_codes = held.tile([P, H], U32, align_bytes=64)
         w1_scales = held.tile([P, H], U8, align_bytes=64)
@@ -97,10 +109,11 @@ def tile_picked_winmax_silu_po_kernel(
                 in_=w1_bf[:, tiles].rearrange("p t m j -> p (t m j)"),
             )
 
-        round_w1(0, slice(0, 4))
-        round_w1(1, slice(0, 2))
-        round_w1(1, slice(2, 4))
-        for tiles in (slice(0, 1), slice(1, 2), slice(2, 4)):
+        low, high, every = slice(0, 2), slice(2, PACK), slice(0, PACK)
+        round_w1(0, every)
+        round_w1(1, low)
+        round_w1(1, high)
+        for tiles in (slice(0, 1), slice(1, 2), high):
             quantise_w1(tiles)
 
         w23_codes = held.tile([P, 2, PACK, P], I32, align_bytes=64)
@@ -135,31 +148,44 @@ def tile_picked_winmax_silu_po_kernel(
         out_rows = out_0.rearrange("(p t) v -> p t v", t=PACK)
         out_words = out_1[0].rearrange("p v r -> p (v r)").bitcast(I32)
 
-        chunks = V // CHUNK
-        last = chunks - 1
-        result = {}
-        z = {}
-        z_codes = {}
-        z_scales = {}
-        banks = {}
+        z, z_codes, z_scales, banks = [], [], [], []
+        for c in range(LAST + 1):
+            z.append(held.tile([P, 2, CHUNK, PACK], BF16, align_bytes=64, name=f"z{c}"))
+            z_codes.append(held.tile([P, 2, CHUNK], U32, align_bytes=64, name=f"z_codes{c}"))
+            z_scales.append(held.tile([P, 2, CHUNK], U8, align_bytes=64, name=f"z_scales{c}"))
+        larger_kind, smaller_kind, both_kinds = slice(0, 1), slice(1, 2), slice(0, 2)
 
-        def fetch(first, count, t, into):
-            entries = order_sb[:, first * (2 * CHUNK // 16) : (first + count) * (2 * CHUNK // 16)]
-            nc.vector.tensor_copy(into, y[t][:].indirect(entries))
+        row = held.tile([P, 11 * SPAN], F32)
+        stretch = row[:, 8 * SPAN + CHUNK : 10 * SPAN + CHUNK].rearrange("p (t w v) -> p t w v", t=PACK, w=1)
 
-        def pool_pairs(pooled, pairs):
-            for w, op in enumerate((MAX, MIN)):
-                nc.vector.tensor_tensor(pooled[:, :, w], pairs[:, :, :, 0], pairs[:, :, :, 1], op)
+        def slot(c, t, count=1):
+            start = (7 + t) * SPAN if c == LAST else (2 * t + c % 2) * SPAN
+            return row[:, start : start + count * SPAN]
 
-        def silu_of(c, kinds, tiles, values):
+        def pairs_of(c):
+            if c == LAST:
+                return row[:, 7 * SPAN : 11 * SPAN].rearrange("p (t v e) -> p t v e", t=PACK, e=2)
+            return row[:, 0 : 8 * SPAN].rearrange("p (t s v e) -> p t s v e", t=PACK, s=2, e=2)[:, :, c % 2]
+
+        def fetch(c, t, count=1):
+            entries = order_sb[:, c * (SPAN // 16) : (c + count) * (SPAN // 16)]
+            nc.vector.tensor_copy(slot(c, t, count), y[t][:].indirect(entries))
+
+        def pool(into, c, tiles, op):
+            pairs = pairs_of(c)
+            nc.vector.tensor_tensor(into, pairs[:, tiles, :, 0], pairs[:, tiles, :, 1], op)
+
+        def silu(c, kinds, values):
             nc.scalar.activation(
-                z[c][:, kinds, :, tiles].rearrange("p w (g i) t -> p (w g) t i", i=PACK),
+                z[c][:, kinds].rearrange("p w (g i) t -> p (w g) t i", i=PACK),
                 values.rearrange("p t w (g i) -> p (w g) t i", i=PACK),
                 SILU,
             )
 
-        def silu(c, kinds, tiles, pooled):
-            silu_of(c, kinds, tiles, pooled[:, :, kinds])
+        def smaller_from_sums(c, larger, smaller):
+            tiles = slice(0, GPSIMD_TILES)
+            nc.gpsimd.tensor_tensor(smaller[:, tiles, 0], sums[:, :, c], larger[:, tiles, 0], SUBTRACT)
+            silu(c, smaller_kind, smaller)
 
         def quantise_z(c, kinds):
             nc.vector.quantize_mx(
@@ -180,15 +206,18 @@ def tile_picked_winmax_silu_po_kernel(
             )
 
         def second_product(c):
-            quantise_z(c, both)
-            banks[c] = psum.tile([P, PACK, CHUNK], F32, tag="bank", name="bank")
+            quantise_z(c, both_kinds)
+            banks.append(psum.tile([P, PACK, CHUNK], F32, tag="bank", name="bank"))
             for t in range(PACK):
                 for w in range(2):
                     multiply(c, t, w, banks[c][:, t, :])
 
         def store_result(c):
             cols = slice(c * CHUNK, (c + 1) * CHUNK)
-            nc.sync.dma_start(out_rows[:, :, cols], result[c][:])
+            result = held.tile([P, PACK, CHUNK], F32, name=f"result{c}")
+            nc.scalar.copy(result[:], banks[c][:])
+            nc.sync.dma_start(out_rows[:, :, cols], result[:])
+            return result
 
         def quantise_result(cols, rounded):
             nc.vector.quantize_mx(
@@ -197,118 +226,87 @@ def tile_picked_winmax_silu_po_kernel(
                 in_=rounded.rearrange("p v t -> p (v t)"),
             )
 
-        both, every = slice(0, 2), slice(0, PACK)
-        for c in range(chunks):
-            z[c] = held.tile([P, 2, CHUNK, PACK], BF16, align_bytes=64, name=f"z{c}")
-            z_codes[c] = held.tile([P, 2, CHUNK], U32, align_bytes=64, name=f"z_codes{c}")
-            z_scales[c] = held.tile([P, 2, CHUNK], U8, align_bytes=64, name=f"z_scales{c}")
-
-        span = 2 * CHUNK
-        row = held.tile([P, 10 * span], F32)
-
-        def slot(c, t, count=1):
-            start = (7 + t) * span if c == last else (2 * t + c % 2) * span
-            return row[:, start : start + count * span]
-
-        def pairs_of(c, tiles):
-            if c == last:
-                return row[:, 7 * span : 10 * span].rearrange("p (t v e) -> p t v e", t=tiles, e=2)
-            return row[:, 0 : 8 * span].rearrange("p (t s v e) -> p t s v e", t=PACK, s=2, e=2)[:, :, c % 2]
-
-        sums = held.tile([P, PACK - 1, 2, CHUNK], F32)
-        for t in range(PACK - 1):
-            fetch(0, 2, t, slot(0, t, 2))
-            count = len([c for c in range(2) if t < GPSIMD_TILES[c]])
-            pairs = slot(0, t, count).rearrange("p (v e) -> p v e", e=2)
-            nc.gpsimd.tensor_tensor(
-                sums[:, t, 0:count].rearrange("p c v -> p (c v)"), pairs[:, :, 0], pairs[:, :, 1], ADD
-            )
+        sums = held.tile([P, GPSIMD_TILES, 2, CHUNK], F32)
+        for t in range(GPSIMD_TILES):
+            fetch(0, t, count=2)
+            pairs = slot(0, t, count=2).rearrange("p (v e) -> p v e", e=2)
+            nc.gpsimd.tensor_tensor(sums[:, t].rearrange("p c v -> p (c v)"), pairs[:, :, 0], pairs[:, :, 1], ADD)
+        vector_tiles = slice(GPSIMD_TILES, PACK)
         for c in range(2):
-            fetch(c, 1, PACK - 1, slot(c, PACK - 1))
+            fetch(c, PACK - 1)
 
-        def pool_larger(c, larger):
-            pairs = pairs_of(c, PACK)
-            halves = (every,) if c == 0 else (slice(2, 4), slice(0, 2))
-            for half in halves:
-                nc.vector.tensor_tensor(larger[:, half, 0], pairs[:, half, :, 0], pairs[:, half, :, 1], MAX)
-            silu_of(c, slice(0, 1), every, larger)
-
-        def smaller_on_vector(c, smaller):
-            n = GPSIMD_TILES[c]
-            pairs = pairs_of(c, PACK)
-            nc.vector.tensor_tensor(smaller[:, n:PACK, 0], pairs[:, n:PACK, :, 0], pairs[:, n:PACK, :, 1], MIN)
-
-        def smaller_on_gpsimd(c, larger, smaller):
-            n = GPSIMD_TILES[c]
-            nc.gpsimd.tensor_tensor(smaller[:, 0:n, 0], sums[:, 0:n, c], larger[:, 0:n, 0], SUBTRACT)
-            silu_of(c, slice(1, 2), every, smaller)
-
-        larger0 = row[:, 8 * span : 10 * span].rearrange("p (t w v) -> p t w v", t=PACK, w=1)
-        smaller0 = late.tile([P, PACK, 1, CHUNK], F32, offset=4096)
-        pool_larger(0, larger0)
-        smaller_on_vector(0, smaller0[:])
-        smaller_on_gpsimd(0, larger0, smaller0[:])
+        larger0 = stretch
+        smaller0 = late.tile([P, PACK, 1, CHUNK], F32, offset=SMALLER0_AT)
+        pool(larger0[:, :, 0], 0, every, MAX)
+        silu(0, larger_kind, larger0)
+        pool(smaller0[:, vector_tiles, 0], 0, vector_tiles, MIN)
+        smaller_from_sums(0, larger0, smaller0[:])
         for t in range(PACK - 1):
-            fetch(2, 1, t, slot(2, t))
-        smaller1 = larger0
-        smaller_on_vector(1, smaller1)
+            fetch(2, t)
+
+        smaller1 = stretch
+        pool(smaller1[:, vector_tiles, 0], 1, vector_tiles, MIN)
         second_product(0)
-        larger1 = late.tile([P, PACK, 1, CHUNK], F32, offset=4096)
-        pool_larger(1, larger1[:])
-        smaller_on_gpsimd(1, larger1[:], smaller1)
-        fetch(2, 1, PACK - 1, slot(2, PACK - 1))
-        fetch(last, 1, 0, slot(last, 0))
-        pooled2 = late.tile([P, PACK, 2, CHUNK], F32, offset=0)
-        pool_pairs(pooled2[:], pairs_of(2, PACK))
+        larger1 = late.tile([P, PACK, 1, CHUNK], F32, offset=SMALLER0_AT)
+        for tiles in (high, low):
+            pool(larger1[:, tiles, 0], 1, tiles, MAX)
+        silu(1, larger_kind, larger1[:])
+        smaller_from_sums(1, larger1[:], smaller1)
+        fetch(2, PACK - 1)
+        fetch(LAST, 0)
+
+        pooled2 = late.tile([P, PACK, 2, CHUNK], F32, offset=POOLED_AT)
+        for w, op in enumerate((MAX, MIN)):
+            pool(pooled2[:, :, w], 2, every, op)
         second_product(1)
-        silu(2, both, every, pooled2[:])
-        rounded01 = held.tile([P, 2 * CHUNK, PACK], BF16, align_bytes=64)
-
-        def hand_out(c):
-            result[c] = held.tile([P, PACK, CHUNK], F32, name=f"result{c}")
-            nc.scalar.copy(result[c][:], banks[c][:])
-            nc.scalar.copy(rounded01[:, c * CHUNK : (c + 1) * CHUNK], banks[c][:].rearrange("p t v -> p v t"))
-            store_result(c)
-
-        hand_out(0)
-        for t in range(1, PACK - 1):
-            fetch(last, 1, t, slot(last, t))
+        silu(2, both_kinds, pooled2[:])
+        store_result(0)
+        rounded0 = held.tile([P, CHUNK, PACK], BF16, align_bytes=64)
+        nc.scalar.copy(rounded0[:], banks[0][:].rearrange("p t v -> p v t"))
+        for t in range(1, PACK):
+            fetch(LAST, t)
         second_product(2)
 
-        pooled3 = late.tile([P, PACK - 1, 2, CHUNK], F32, offset=0)
-        pool_pairs(pooled3[:], pairs_of(last, PACK - 1))
-        silu(last, both, slice(0, PACK - 1), pooled3[:])
-        picked_end = late.tile([P, 1, CHUNK, 2], F32, offset=3072)
-        fetch(last, 1, PACK - 1, picked_end[:].rearrange("p t v e -> p (t v e)"))
-        pooled_end = late.tile([P, 1, 2, CHUNK], F32, offset=8192)
-        pool_pairs(pooled_end[:], picked_end[:])
-        end_banks = [psum.tile([P, CHUNK], F32, tag="bank", name="bank") for t in range(PACK)]
-        for w in range(2):
-            silu(last, slice(w, w + 1), slice(PACK - 1, PACK), pooled_end[:])
-            quantise_z(last, slice(w, w + 1))
+        pooled3 = [
+            late.tile([P, PACK, 1, CHUNK], F32, offset=at, name=f"pooled3_{w}")
+            for w, at in enumerate((POOLED_AT, LAST_SMALLER_AT))
+        ]
+        for w, op in enumerate((MAX, MIN)):
+            pool(pooled3[w][:, :, 0], LAST, every, op)
+        last_banks = [psum.tile([P, CHUNK], F32, tag="bank", name="bank") for t in range(PACK)]
+        for w, kind in enumerate((larger_kind, smaller_kind)):
+            silu(LAST, kind, pooled3[w][:])
+            quantise_z(LAST, kind)
             for t in range(PACK):
-                multiply(last, t, w, end_banks[t][:])
-        hand_out(1)
-        out_scales = late.tile([P, V], U8, offset=8192, align_bytes=64)
-        quantise_result(slice(0, 2 * CHUNK), rounded01[:])
+                multiply(LAST, t, w, last_banks[t][:])
+
+        result1 = store_result(1)
+        rounded1 = late.tile([P, CHUNK, PACK], BF16, offset=POOLED_AT, align_bytes=64)
+        nc.vector.tensor_copy(
+            rounded1[:].rearrange("p (g i) t -> p g t i", i=PACK),
+            result1[:].rearrange("p t (g i) -> p g t i", i=PACK),
+        )
+        out_scales = late.tile([P, V], U8, offset=OUT_SCALES_AT, align_bytes=64)
+        for c, rounded in enumerate((rounded0, rounded1)):
+            quantise_result(slice(c * CHUNK, (c + 1) * CHUNK), rounded[:])
         nc.sync.dma_start(out_words[:, 0 : 2 * CHUNK], out_codes[:, 0 : 2 * CHUNK].bitcast(I32))
 
-        result23 = late.tile([P, PACK, 2 * CHUNK], F32, offset=8704)
-        nc.scalar.copy(result23[:, :, 0:CHUNK], banks[2][:])
+        result23 = late.tile([P, PACK, 2 * CHUNK], F32, offset=RESULT23_AT)
         rounded23 = held.tile([P, 2 * CHUNK, PACK], BF16, align_bytes=64)
+        chunk2, chunk3, chunks23 = slice(0, CHUNK), slice(CHUNK, 2 * CHUNK), slice(0, 2 * CHUNK)
 
-        def round_out(cols, pair):
-            nc.vector.tensor_copy(rounded23[:, cols, pair], result23[:, pair, cols].rearrange("p t v -> p v t"))
+        def round_result(cols, tiles):
+            nc.vector.tensor_copy(rounded23[:, cols, tiles], result23[:, tiles, cols].rearrange("p t v -> p v t"))
 
-        low, high = slice(0, 2), slice(2, 4)
-        round_out(slice(0, CHUNK), high)
-        for pair, cols in ((low, slice(0, 2 * CHUNK)), (high, slice(CHUNK, 2 * CHUNK))):
-            for t in range(pair.start, pair.stop):
-                nc.scalar.copy(result23[:, t, CHUNK : 2 * CHUNK], end_banks[t][:])
-            nc.sync.dma_start(out_rows[:, pair, 2 * CHUNK : V], result23[:, pair])
-            round_out(cols, pair)
-        for c in (2, 3):
-            quantise_result(slice(c * CHUNK, (c + 1) * CHUNK), rounded23[:, (c - 2) * CHUNK : (c - 1) * CHUNK])
+        nc.scalar.copy(result23[:, :, chunk2], banks[2][:])
+        round_result(chunk2, high)
+        for tiles, cols in ((low, chunks23), (high, chunk3)):
+            for t in range(tiles.start, tiles.stop):
+                nc.scalar.copy(result23[:, t, chunk3], last_banks[t][:])
+            nc.sync.dma_start(out_rows[:, tiles, 2 * CHUNK : V], result23[:, tiles])
+            round_result(cols, tiles)
+        for cols in (chunk2, chunk3):
+            quantise_result(slice(2 * CHUNK + cols.start, 2 * CHUNK + cols.stop), rounded23[:, cols])
         nc.sync.dma_start(out_words[:, 2 * CHUNK : V], out_codes[:, 2 * CHUNK : V].bitcast(I32))
 
         scale_rows = out_2[0].bitcast(I32)

@@ -28,11 +28,20 @@ GPSIMD_TILES = 3
 
 XS_WINDOW_AT = 2048
 W2_RAW_AT, WS_RAW_AT, W3_RAW_AT = 256, 2304, 2816
-POOLED_AT = 0
-LAST_SMALLER_AT = 2048
-OUT_SCALES_AT = 2048
-RESULT23_AT = 3072
-SMALLER0_AT = 4096
+W1_BF_AT = 5376
+LAST_LARGER_AT = 0
+LAST_SMALLER_AT = (1024, 4096)
+Z1_AT = 2048
+OUT_SCALES_AT = 4096
+RESULT23_AT = 4608
+SMALLER1 = 2304
+SMALLER2 = 2816
+LAST_LARGER_FIRST = 3072
+LARGER1 = 3200
+SMALLER0 = 3328
+LARGER2 = 3584
+LARGER0 = 3840
+ROW = 4352
 
 
 def tile_picked_winmax_silu_po_kernel(
@@ -90,7 +99,7 @@ def tile_picked_winmax_silu_po_kernel(
                 first = 32 * q + 4 * w
                 nc.sync.dma_start(ws_raw[first : first + 4, :].bitcast(I32), rows[4 * q : 4 * q + 4, :])
 
-        w1_bf = held.tile([P, PACK, P, PACK], BF16, align_bytes=64)
+        w1_bf = early.tile([P, PACK, P, PACK], BF16, offset=W1_BF_AT, align_bytes=64)
         w1_dealt = w1_bf[:].rearrange("p t m j -> p m j t")
 
         def round_w1(half, tiles):
@@ -116,10 +125,13 @@ def tile_picked_winmax_silu_po_kernel(
         for tiles in (slice(0, 1), slice(1, 2), high):
             quantise_w1(tiles)
 
-        w23_codes = held.tile([P, 2, PACK, P], I32, align_bytes=64)
+        w23_codes = [
+            early.tile([P, PACK, P], I32, offset=W1_BF_AT + w * 2048, align_bytes=64, name=f"w23_codes{w}")
+            for w in range(2)
+        ]
         for w in range(2):
-            nc.vector.tensor_copy(
-                w23_codes[:, w].rearrange("p t (g i) -> p g t i", i=PACK),
+            nc.gpsimd.tensor_copy(
+                w23_codes[w][:].rearrange("p t (g i) -> p g t i", i=PACK),
                 w23_raw[w][:].rearrange("p (g i t) -> p g t i", i=PACK, t=PACK),
             )
 
@@ -139,7 +151,10 @@ def tile_picked_winmax_silu_po_kernel(
                     start=True,
                     stop=True,
                 )
-                nc.scalar.copy(y[t][:, places], bank[:])
+                if t == 0 and part == 1:
+                    nc.vector.tensor_copy(y[t][:, places], bank[:])
+                else:
+                    nc.scalar.copy(y[t][:, places], bank[:])
 
         w23_scales = held.tile([P, PACK, P], U8, align_bytes=64)
         nc.gpsimd.tensor_copy(w23_scales[:], ws_raw[:].rearrange("p (m t) -> p t m", t=PACK))
@@ -150,34 +165,42 @@ def tile_picked_winmax_silu_po_kernel(
 
         z, z_codes, z_scales, banks = [], [], [], []
         for c in range(LAST + 1):
-            z.append(held.tile([P, 2, CHUNK, PACK], BF16, align_bytes=64, name=f"z{c}"))
+            if c == 1:
+                z.append(late.tile([P, 2, CHUNK, PACK], BF16, offset=Z1_AT, align_bytes=64, name="z1"))
+            else:
+                z.append(held.tile([P, 2, CHUNK, PACK], BF16, align_bytes=64, name=f"z{c}"))
             z_codes.append(held.tile([P, 2, CHUNK], U32, align_bytes=64, name=f"z_codes{c}"))
             z_scales.append(held.tile([P, 2, CHUNK], U8, align_bytes=64, name=f"z_scales{c}"))
         larger_kind, smaller_kind, both_kinds = slice(0, 1), slice(1, 2), slice(0, 2)
 
-        row = held.tile([P, 11 * SPAN], F32)
-        stretch = row[:, 8 * SPAN + CHUNK : 10 * SPAN + CHUNK].rearrange("p (t w v) -> p t w v", t=PACK, w=1)
+        row = held.tile([P, ROW], F32)
+        STEP = 2 * SPAN
+
+        def first_slot(c):
+            return (0, SPAN, 0, 2 * STEP + SPAN)[c]
 
         def slot(c, t, count=1):
-            start = (7 + t) * SPAN if c == LAST else (2 * t + c % 2) * SPAN
+            start = first_slot(c) + t * STEP
             return row[:, start : start + count * SPAN]
 
         def pairs_of(c):
-            if c == LAST:
-                return row[:, 7 * SPAN : 11 * SPAN].rearrange("p (t v e) -> p t v e", t=PACK, e=2)
-            return row[:, 0 : 8 * SPAN].rearrange("p (t s v e) -> p t s v e", t=PACK, s=2, e=2)[:, :, c % 2]
+            start = first_slot(c)
+            return row[:, start : start + PACK * STEP].rearrange("p (t s v e) -> p t s v e", t=PACK, s=2, e=2)[:, :, 0]
+
+        def pooled(at, width=CHUNK):
+            return row[:, at : at + PACK * width].rearrange("p (t w v) -> p t w v", t=PACK, w=1)
 
         def fetch(c, t, count=1):
             entries = order_sb[:, c * (SPAN // 16) : (c + count) * (SPAN // 16)]
             nc.vector.tensor_copy(slot(c, t, count), y[t][:].indirect(entries))
 
-        def pool(into, c, tiles, op):
+        def pool(into, c, tiles, op, cols=slice(0, CHUNK)):
             pairs = pairs_of(c)
-            nc.vector.tensor_tensor(into, pairs[:, tiles, :, 0], pairs[:, tiles, :, 1], op)
+            nc.vector.tensor_tensor(into, pairs[:, tiles, cols, 0], pairs[:, tiles, cols, 1], op)
 
-        def silu(c, kinds, values):
+        def silu(c, kinds, values, cols=slice(0, CHUNK)):
             nc.scalar.activation(
-                z[c][:, kinds].rearrange("p w (g i) t -> p (w g) t i", i=PACK),
+                z[c][:, kinds, cols].rearrange("p w (g i) t -> p (w g) t i", i=PACK),
                 values.rearrange("p t w (g i) -> p (w g) t i", i=PACK),
                 SILU,
             )
@@ -197,7 +220,7 @@ def tile_picked_winmax_silu_po_kernel(
         def multiply(c, t, w, into):
             nc.tensor.matmul_mx(
                 out=into,
-                lhsT=w23_codes[:, w, t, :].bitcast(FP8X4),
+                lhsT=w23_codes[w][:, t, :].bitcast(FP8X4),
                 lhsT_scale=w23_scales[4 * w : P, t, :],
                 rhs=z_codes[c][:, w, :].bitcast(FP8X4),
                 rhs_scale=z_scales[c][:, w, :],
@@ -207,15 +230,19 @@ def tile_picked_winmax_silu_po_kernel(
 
         def second_product(c):
             quantise_z(c, both_kinds)
-            banks.append(psum.tile([P, PACK, CHUNK], F32, tag="bank", name="bank"))
+            banks.append([psum.tile([P, 2, CHUNK], F32, tag="bank", name="bank") for half in range(2)])
             for t in range(PACK):
                 for w in range(2):
-                    multiply(c, t, w, banks[c][:, t, :])
+                    multiply(c, t, w, banks[c][t // 2][:, t % 2, :])
+
+        def empty_banks(c, into):
+            for half, tiles in enumerate((low, high)):
+                nc.scalar.copy(into[:, tiles], banks[c][half][:])
 
         def store_result(c):
             cols = slice(c * CHUNK, (c + 1) * CHUNK)
             result = held.tile([P, PACK, CHUNK], F32, name=f"result{c}")
-            nc.scalar.copy(result[:], banks[c][:])
+            empty_banks(c, result[:])
             nc.sync.dma_start(out_rows[:, :, cols], result[:])
             return result
 
@@ -226,7 +253,7 @@ def tile_picked_winmax_silu_po_kernel(
                 in_=rounded.rearrange("p v t -> p (v t)"),
             )
 
-        sums = held.tile([P, GPSIMD_TILES, 2, CHUNK], F32)
+        sums = early.tile([P, GPSIMD_TILES, 2, CHUNK], F32, offset=WS_RAW_AT)
         for t in range(GPSIMD_TILES):
             fetch(0, t, count=2)
             pairs = slot(0, t, count=2).rearrange("p (v e) -> p v e", e=2)
@@ -235,53 +262,59 @@ def tile_picked_winmax_silu_po_kernel(
         for c in range(2):
             fetch(c, PACK - 1)
 
-        larger0 = stretch
-        smaller0 = late.tile([P, PACK, 1, CHUNK], F32, offset=SMALLER0_AT)
+        larger0, smaller0 = pooled(LARGER0), pooled(SMALLER0)
         pool(larger0[:, :, 0], 0, every, MAX)
         silu(0, larger_kind, larger0)
-        pool(smaller0[:, vector_tiles, 0], 0, vector_tiles, MIN)
-        smaller_from_sums(0, larger0, smaller0[:])
-        for t in range(PACK - 1):
+        larger1, smaller1 = pooled(LARGER1), pooled(SMALLER1)
+        for c, smaller in enumerate((smaller0, smaller1)):
+            pool(smaller[:, vector_tiles, 0], c, vector_tiles, MIN)
+        smaller_from_sums(0, larger0, smaller0)
+        for t in range(PACK):
             fetch(2, t)
 
-        smaller1 = stretch
-        pool(smaller1[:, vector_tiles, 0], 1, vector_tiles, MIN)
         second_product(0)
-        larger1 = late.tile([P, PACK, 1, CHUNK], F32, offset=SMALLER0_AT)
         for tiles in (high, low):
             pool(larger1[:, tiles, 0], 1, tiles, MAX)
-        silu(1, larger_kind, larger1[:])
-        smaller_from_sums(1, larger1[:], smaller1)
-        fetch(2, PACK - 1)
-        fetch(LAST, 0)
-
-        pooled2 = late.tile([P, PACK, 2, CHUNK], F32, offset=POOLED_AT)
-        for w, op in enumerate((MAX, MIN)):
-            pool(pooled2[:, :, w], 2, every, op)
-        second_product(1)
-        silu(2, both_kinds, pooled2[:])
-        store_result(0)
-        rounded0 = held.tile([P, CHUNK, PACK], BF16, align_bytes=64)
-        nc.scalar.copy(rounded0[:], banks[0][:].rearrange("p t v -> p v t"))
-        for t in range(1, PACK):
+        silu(1, larger_kind, larger1)
+        result0 = store_result(0)
+        smaller_from_sums(1, larger1, smaller1)
+        for t in range(2):
             fetch(LAST, t)
-        second_product(2)
 
-        pooled3 = [
-            late.tile([P, PACK, 1, CHUNK], F32, offset=at, name=f"pooled3_{w}")
-            for w, at in enumerate((POOLED_AT, LAST_SMALLER_AT))
+        for at, op, kind in ((LARGER2, MAX, larger_kind), (SMALLER2, MIN, smaller_kind)):
+            pool(pooled(at)[:, :, 0], 2, every, op)
+            silu(2, kind, pooled(at))
+        second_product(1)
+        rounded0 = late.tile([P, CHUNK, PACK], BF16, offset=Z1_AT, align_bytes=64)
+        nc.scalar.copy(
+            rounded0[:].rearrange("p (g i) t -> p g t i", i=PACK),
+            result0[:].rearrange("p t (g i) -> p g t i", i=PACK),
+        )
+        result1 = store_result(1)
+        fetch(LAST, 2)
+        second_product(2)
+        fetch(LAST, 3)
+
+        HALF = CHUNK // 2
+        halves = (slice(0, HALF), slice(HALF, CHUNK))
+        larger3 = [pooled(LAST_LARGER_FIRST, HALF), late.tile([P, PACK, 1, HALF], F32, offset=LAST_LARGER_AT, name="larger3")[:]]
+        smaller3 = [
+            late.tile([P, PACK, 1, HALF], F32, offset=at, name=f"smaller3_{h}")[:] for h, at in enumerate(LAST_SMALLER_AT)
         ]
-        for w, op in enumerate((MAX, MIN)):
-            pool(pooled3[w][:, :, 0], LAST, every, op)
+        for tiles in (slice(0, PACK - 1), slice(PACK - 1, PACK)):
+            pool(larger3[0][:, tiles, 0], LAST, tiles, MAX, halves[0])
+        pool(larger3[1][:, :, 0], LAST, every, MAX, halves[1])
+        for h in range(2):
+            pool(smaller3[h][:, :, 0], LAST, every, MIN, halves[h])
         last_banks = [psum.tile([P, CHUNK], F32, tag="bank", name="bank") for t in range(PACK)]
-        for w, kind in enumerate((larger_kind, smaller_kind)):
-            silu(LAST, kind, pooled3[w][:])
+        for w, (kind, values) in enumerate(((larger_kind, larger3), (smaller_kind, smaller3))):
+            for h in range(2):
+                silu(LAST, kind, values[h], halves[h])
             quantise_z(LAST, kind)
             for t in range(PACK):
                 multiply(LAST, t, w, last_banks[t][:])
 
-        result1 = store_result(1)
-        rounded1 = late.tile([P, CHUNK, PACK], BF16, offset=POOLED_AT, align_bytes=64)
+        rounded1 = late.tile([P, CHUNK, PACK], BF16, offset=LAST_LARGER_AT, align_bytes=64)
         nc.vector.tensor_copy(
             rounded1[:].rearrange("p (g i) t -> p g t i", i=PACK),
             result1[:].rearrange("p t (g i) -> p g t i", i=PACK),
@@ -298,7 +331,7 @@ def tile_picked_winmax_silu_po_kernel(
         def round_result(cols, tiles):
             nc.vector.tensor_copy(rounded23[:, cols, tiles], result23[:, tiles, cols].rearrange("p t v -> p v t"))
 
-        nc.scalar.copy(result23[:, :, chunk2], banks[2][:])
+        empty_banks(2, result23[:, :, chunk2])
         round_result(chunk2, high)
         for tiles, cols in ((low, chunks23), (high, chunk3)):
             for t in range(tiles.start, tiles.stop):

@@ -28,6 +28,9 @@ GPSIMD_TILES = 3
 
 XS_WINDOW_AT = 2048
 W2_RAW_AT, WS_RAW_AT, W3_RAW_AT = 256, 2304, 2816
+W1_CODES_AT = (11776, 12288, 11264, 12800)
+W3_CODES_AT = 9728
+LARGER0_AT = 8704
 W1_BF_AT = 5376
 LAST_LARGER_AT = 0
 LAST_SMALLER_AT = (1024, 4096)
@@ -60,11 +63,11 @@ def tile_picked_winmax_silu_po_kernel(
         xw_window = held.tile([P, T], U32, align_bytes=64)
         w1_raw = [held.tile([P, PACK, H // 2], F32, name=f"w1_raw{half}") for half in range(2)]
 
-        nc.sync.dma_start(offs_sb[:], offs)
         nc.sync.dma_start(
             xs_window[:].bitcast(I32),
             x_scales[0].bitcast(I32).rearrange("q (one c) -> q one c", one=1).to_broadcast([16, 8, T // 4]),
         )
+        nc.sync.dma_start(offs_sb[:], offs)
         nc.sync.dma_start(xw_window[:].bitcast(I32), x_words[0].rearrange("p c r -> p (c r)").bitcast(I32))
         w1_rows = w1.rearrange("(p j) h -> p j h", j=PACK)
         for half in range(2):
@@ -107,44 +110,49 @@ def tile_picked_winmax_silu_po_kernel(
             places = slice(half * (P // 2), (half + 1) * (P // 2))
             nc.scalar.copy(w1_dealt[:, places, :, tiles], source[:, :, :, tiles])
 
-        w1_codes = held.tile([P, H], U32, align_bytes=64)
+        w1_codes = [
+            early.tile([P, P], U32, offset=W1_CODES_AT[t], align_bytes=64, name=f"w1_codes{t}")
+            for t in range(PACK)
+        ]
         w1_scales = held.tile([P, H], U8, align_bytes=64)
 
-        def quantise_w1(tiles):
-            cols = slice(tiles.start * P, tiles.stop * P)
+        def quantise_w1(t):
             nc.vector.quantize_mx(
-                out=w1_codes[:, cols].bitcast(FP8X4),
-                scales=w1_scales[:, cols],
-                in_=w1_bf[:, tiles].rearrange("p t m j -> p (t m j)"),
+                out=w1_codes[t][:].bitcast(FP8X4),
+                scales=w1_scales[:, t * P : (t + 1) * P],
+                in_=w1_bf[:, t].rearrange("p m j -> p (m j)"),
             )
 
         low, high, every = slice(0, 2), slice(2, PACK), slice(0, PACK)
         round_w1(0, every)
         round_w1(1, low)
         round_w1(1, high)
-        for tiles in (slice(0, 1), slice(1, 2), high):
-            quantise_w1(tiles)
+        for t in range(PACK):
+            quantise_w1(t)
 
         w23_codes = [
-            early.tile([P, PACK, P], I32, offset=W1_BF_AT + w * 2048, align_bytes=64, name=f"w23_codes{w}")
-            for w in range(2)
+            early.tile([P, PACK, P], I32, offset=at, align_bytes=64, name=f"w23_codes{w}")
+            for w, at in enumerate((W1_BF_AT, W3_CODES_AT))
         ]
-        for w in range(2):
+
+        def deal_words(w):
             nc.gpsimd.tensor_copy(
                 w23_codes[w][:].rearrange("p t (g i) -> p g t i", i=PACK),
                 w23_raw[w][:].rearrange("p (g i t) -> p g t i", i=PACK, t=PACK),
             )
 
+        deal_words(0)
+
         y = [held.tile([P, S], F32, name=f"y{t}") for t in range(PACK)]
         for t in range(PACK):
             cols = slice(t * P, (t + 1) * P)
-            width = BANK // 2 if t == 0 else BANK
+            width = BANK // 2 if t < 2 else BANK
             for part in range(S // width):
                 places = slice(part * width, (part + 1) * width)
                 bank = psum.tile([P, width], F32, tag="bank")
                 nc.tensor.matmul_mx(
                     out=bank[:],
-                    lhsT=w1_codes[:, cols].bitcast(FP8X4),
+                    lhsT=w1_codes[t][:].bitcast(FP8X4),
                     lhsT_scale=w1_scales[:, cols],
                     rhs=xq_words[:, places].bitcast(FP8X4),
                     rhs_scale=xq_scales[:, places],
@@ -156,8 +164,6 @@ def tile_picked_winmax_silu_po_kernel(
                 else:
                     nc.scalar.copy(y[t][:, places], bank[:])
 
-        w23_scales = held.tile([P, PACK, P], U8, align_bytes=64)
-        nc.gpsimd.tensor_copy(w23_scales[:], ws_raw[:].rearrange("p (m t) -> p t m", t=PACK))
 
         out_codes = held.tile([P, V], U32, align_bytes=64)
         out_rows = out_0.rearrange("(p t) v -> p t v", t=PACK)
@@ -253,22 +259,27 @@ def tile_picked_winmax_silu_po_kernel(
                 in_=rounded.rearrange("p v t -> p (v t)"),
             )
 
-        sums = early.tile([P, GPSIMD_TILES, 2, CHUNK], F32, offset=WS_RAW_AT)
+        sums = held.tile([P, GPSIMD_TILES, 2, CHUNK], F32)
         for t in range(GPSIMD_TILES):
             fetch(0, t, count=2)
             pairs = slot(0, t, count=2).rearrange("p (v e) -> p v e", e=2)
             nc.gpsimd.tensor_tensor(sums[:, t].rearrange("p c v -> p (c v)"), pairs[:, :, 0], pairs[:, :, 1], ADD)
+            if t == 0:
+                deal_words(1)
         vector_tiles = slice(GPSIMD_TILES, PACK)
         for c in range(2):
             fetch(c, PACK - 1)
 
-        larger0, smaller0 = pooled(LARGER0), pooled(SMALLER0)
+        larger0_tile = late.tile([P, PACK, 1, CHUNK], F32, offset=LARGER0_AT)
+        larger0, smaller0 = larger0_tile[:], pooled(SMALLER0)
         pool(larger0[:, :, 0], 0, every, MAX)
         silu(0, larger_kind, larger0)
         larger1, smaller1 = pooled(LARGER1), pooled(SMALLER1)
         for c, smaller in enumerate((smaller0, smaller1)):
             pool(smaller[:, vector_tiles, 0], c, vector_tiles, MIN)
         smaller_from_sums(0, larger0, smaller0)
+        w23_scales = late.tile([P, PACK, P], U8, offset=LARGER0_AT, align_bytes=64)
+        nc.gpsimd.tensor_copy(w23_scales[:], ws_raw[:].rearrange("p (m t) -> p t m", t=PACK))
         for t in range(PACK):
             fetch(2, t)
 
@@ -325,21 +336,22 @@ def tile_picked_winmax_silu_po_kernel(
         nc.sync.dma_start(out_words[:, 0 : 2 * CHUNK], out_codes[:, 0 : 2 * CHUNK].bitcast(I32))
 
         result23 = late.tile([P, PACK, 2 * CHUNK], F32, offset=RESULT23_AT)
-        rounded23 = held.tile([P, 2 * CHUNK, PACK], BF16, align_bytes=64)
-        chunk2, chunk3, chunks23 = slice(0, CHUNK), slice(CHUNK, 2 * CHUNK), slice(0, 2 * CHUNK)
-
-        def round_result(cols, tiles):
-            nc.vector.tensor_copy(rounded23[:, cols, tiles], result23[:, tiles, cols].rearrange("p t v -> p v t"))
-
+        chunk2, chunk3 = slice(0, CHUNK), slice(CHUNK, 2 * CHUNK)
         empty_banks(2, result23[:, :, chunk2])
-        round_result(chunk2, high)
-        for tiles, cols in ((low, chunks23), (high, chunk3)):
+        rounded2 = held.tile([P, CHUNK, PACK], BF16, align_bytes=64)
+        nc.vector.tensor_copy(
+            rounded2[:].rearrange("p (g i) t -> p g t i", i=PACK),
+            result23[:, :, chunk2].rearrange("p t (g i) -> p g t i", i=PACK),
+        )
+        rounded3 = held.tile([P, CHUNK, PACK], BF16, align_bytes=64)
+        for tiles in (low, high):
             for t in range(tiles.start, tiles.stop):
                 nc.scalar.copy(result23[:, t, chunk3], last_banks[t][:])
             nc.sync.dma_start(out_rows[:, tiles, 2 * CHUNK : V], result23[:, tiles])
-            round_result(cols, tiles)
-        for cols in (chunk2, chunk3):
-            quantise_result(slice(2 * CHUNK + cols.start, 2 * CHUNK + cols.stop), rounded23[:, cols])
+            nc.vector.tensor_copy(rounded3[:, :, tiles], result23[:, tiles, chunk3].rearrange("p t v -> p v t"))
+            if tiles == low:
+                quantise_result(slice(2 * CHUNK, 3 * CHUNK), rounded2[:])
+        quantise_result(slice(3 * CHUNK, V), rounded3[:])
         nc.sync.dma_start(out_words[:, 2 * CHUNK : V], out_codes[:, 2 * CHUNK : V].bitcast(I32))
 
         scale_rows = out_2[0].bitcast(I32)

@@ -28,20 +28,17 @@ GPSIMD_TILES = 3
 
 XS_WINDOW_AT = 2048
 W2_RAW_AT, WS_RAW_AT, W3_RAW_AT = 256, 2304, 2816
-W1_CODES_AT = (11776, 12288, 11264, 12800)
-W3_CODES_AT = 9728
-LARGER0_AT = 8704
 W1_BF_AT = 5376
-LAST_LARGER_AT = 0
-LAST_SMALLER_AT = (1024, 4096)
-Z1_AT = 2048
+ROUNDED1_AT = 2560
+LAST_SMALLER_AT = (3072, 4096)
+Z_AT = {1: 0, 2: 3072}
 OUT_SCALES_AT = 4096
 RESULT23_AT = 4608
 SMALLER1 = 2304
 SMALLER2 = 2816
-LAST_LARGER_FIRST = 3072
+LARGER3 = 2816
 LARGER1 = 3200
-SMALLER0 = 3328
+SMALLER0 = 3264
 LARGER2 = 3584
 LARGER0 = 3840
 ROW = 4352
@@ -63,11 +60,11 @@ def tile_picked_winmax_silu_po_kernel(
         xw_window = held.tile([P, T], U32, align_bytes=64)
         w1_raw = [held.tile([P, PACK, H // 2], F32, name=f"w1_raw{half}") for half in range(2)]
 
+        nc.sync.dma_start(offs_sb[:], offs)
         nc.sync.dma_start(
             xs_window[:].bitcast(I32),
             x_scales[0].bitcast(I32).rearrange("q (one c) -> q one c", one=1).to_broadcast([16, 8, T // 4]),
         )
-        nc.sync.dma_start(offs_sb[:], offs)
         nc.sync.dma_start(xw_window[:].bitcast(I32), x_words[0].rearrange("p c r -> p (c r)").bitcast(I32))
         w1_rows = w1.rearrange("(p j) h -> p j h", j=PACK)
         for half in range(2):
@@ -110,49 +107,44 @@ def tile_picked_winmax_silu_po_kernel(
             places = slice(half * (P // 2), (half + 1) * (P // 2))
             nc.scalar.copy(w1_dealt[:, places, :, tiles], source[:, :, :, tiles])
 
-        w1_codes = [
-            early.tile([P, P], U32, offset=W1_CODES_AT[t], align_bytes=64, name=f"w1_codes{t}")
-            for t in range(PACK)
-        ]
+        w1_codes = held.tile([P, H], U32, align_bytes=64)
         w1_scales = held.tile([P, H], U8, align_bytes=64)
 
-        def quantise_w1(t):
+        def quantise_w1(tiles):
+            cols = slice(tiles.start * P, tiles.stop * P)
             nc.vector.quantize_mx(
-                out=w1_codes[t][:].bitcast(FP8X4),
-                scales=w1_scales[:, t * P : (t + 1) * P],
-                in_=w1_bf[:, t].rearrange("p m j -> p (m j)"),
+                out=w1_codes[:, cols].bitcast(FP8X4),
+                scales=w1_scales[:, cols],
+                in_=w1_bf[:, tiles].rearrange("p t m j -> p (t m j)"),
             )
 
         low, high, every = slice(0, 2), slice(2, PACK), slice(0, PACK)
         round_w1(0, every)
         round_w1(1, low)
         round_w1(1, high)
-        for t in range(PACK):
-            quantise_w1(t)
+        for tiles in (slice(0, 1), slice(1, 2), high):
+            quantise_w1(tiles)
 
         w23_codes = [
-            early.tile([P, PACK, P], I32, offset=at, align_bytes=64, name=f"w23_codes{w}")
-            for w, at in enumerate((W1_BF_AT, W3_CODES_AT))
+            early.tile([P, PACK, P], I32, offset=W1_BF_AT + w * 2048, align_bytes=64, name=f"w23_codes{w}")
+            for w in range(2)
         ]
-
-        def deal_words(w):
+        for w in range(2):
             nc.gpsimd.tensor_copy(
                 w23_codes[w][:].rearrange("p t (g i) -> p g t i", i=PACK),
                 w23_raw[w][:].rearrange("p (g i t) -> p g t i", i=PACK, t=PACK),
             )
 
-        deal_words(0)
-
         y = [held.tile([P, S], F32, name=f"y{t}") for t in range(PACK)]
         for t in range(PACK):
             cols = slice(t * P, (t + 1) * P)
-            width = BANK // 2 if t < 2 else BANK
+            width = BANK // 2 if t == 0 else BANK
             for part in range(S // width):
                 places = slice(part * width, (part + 1) * width)
                 bank = psum.tile([P, width], F32, tag="bank")
                 nc.tensor.matmul_mx(
                     out=bank[:],
-                    lhsT=w1_codes[t][:].bitcast(FP8X4),
+                    lhsT=w1_codes[:, cols].bitcast(FP8X4),
                     lhsT_scale=w1_scales[:, cols],
                     rhs=xq_words[:, places].bitcast(FP8X4),
                     rhs_scale=xq_scales[:, places],
@@ -164,6 +156,8 @@ def tile_picked_winmax_silu_po_kernel(
                 else:
                     nc.scalar.copy(y[t][:, places], bank[:])
 
+        w23_scales = held.tile([P, PACK, P], U8, align_bytes=64)
+        nc.gpsimd.tensor_copy(w23_scales[:], ws_raw[:].rearrange("p (m t) -> p t m", t=PACK))
 
         out_codes = held.tile([P, V], U32, align_bytes=64)
         out_rows = out_0.rearrange("(p t) v -> p t v", t=PACK)
@@ -171,8 +165,8 @@ def tile_picked_winmax_silu_po_kernel(
 
         z, z_codes, z_scales, banks = [], [], [], []
         for c in range(LAST + 1):
-            if c == 1:
-                z.append(late.tile([P, 2, CHUNK, PACK], BF16, offset=Z1_AT, align_bytes=64, name="z1"))
+            if c in Z_AT:
+                z.append(late.tile([P, 2, CHUNK, PACK], BF16, offset=Z_AT[c], align_bytes=64, name=f"z{c}"))
             else:
                 z.append(held.tile([P, 2, CHUNK, PACK], BF16, align_bytes=64, name=f"z{c}"))
             z_codes.append(held.tile([P, 2, CHUNK], U32, align_bytes=64, name=f"z_codes{c}"))
@@ -183,7 +177,7 @@ def tile_picked_winmax_silu_po_kernel(
         STEP = 2 * SPAN
 
         def first_slot(c):
-            return (0, SPAN, 0, 2 * STEP + SPAN)[c]
+            return (0, SPAN, 0, STEP + SPAN)[c]
 
         def slot(c, t, count=1):
             start = first_slot(c) + t * STEP
@@ -259,64 +253,56 @@ def tile_picked_winmax_silu_po_kernel(
                 in_=rounded.rearrange("p v t -> p (v t)"),
             )
 
-        sums = held.tile([P, GPSIMD_TILES, 2, CHUNK], F32)
+        sums = early.tile([P, GPSIMD_TILES, 2, CHUNK], F32, offset=WS_RAW_AT)
         for t in range(GPSIMD_TILES):
             fetch(0, t, count=2)
             pairs = slot(0, t, count=2).rearrange("p (v e) -> p v e", e=2)
             nc.gpsimd.tensor_tensor(sums[:, t].rearrange("p c v -> p (c v)"), pairs[:, :, 0], pairs[:, :, 1], ADD)
-            if t == 0:
-                deal_words(1)
         vector_tiles = slice(GPSIMD_TILES, PACK)
         for c in range(2):
             fetch(c, PACK - 1)
 
-        larger0_tile = late.tile([P, PACK, 1, CHUNK], F32, offset=LARGER0_AT)
-        larger0, smaller0 = larger0_tile[:], pooled(SMALLER0)
+        larger0, smaller0 = pooled(LARGER0), pooled(SMALLER0)
         pool(larger0[:, :, 0], 0, every, MAX)
         silu(0, larger_kind, larger0)
         larger1, smaller1 = pooled(LARGER1), pooled(SMALLER1)
         for c, smaller in enumerate((smaller0, smaller1)):
             pool(smaller[:, vector_tiles, 0], c, vector_tiles, MIN)
         smaller_from_sums(0, larger0, smaller0)
-        w23_scales = late.tile([P, PACK, P], U8, offset=LARGER0_AT, align_bytes=64)
-        nc.gpsimd.tensor_copy(w23_scales[:], ws_raw[:].rearrange("p (m t) -> p t m", t=PACK))
         for t in range(PACK):
             fetch(2, t)
 
         second_product(0)
-        for tiles in (high, low):
+        for tiles in (slice(1, PACK), slice(0, 1)):
             pool(larger1[:, tiles, 0], 1, tiles, MAX)
         silu(1, larger_kind, larger1)
         result0 = store_result(0)
         smaller_from_sums(1, larger1, smaller1)
-        for t in range(2):
+        for t in range(PACK - 1):
             fetch(LAST, t)
 
         for at, op, kind in ((LARGER2, MAX, larger_kind), (SMALLER2, MIN, smaller_kind)):
             pool(pooled(at)[:, :, 0], 2, every, op)
             silu(2, kind, pooled(at))
         second_product(1)
-        rounded0 = late.tile([P, CHUNK, PACK], BF16, offset=Z1_AT, align_bytes=64)
+        rounded0 = late.tile([P, CHUNK, PACK], BF16, offset=Z_AT[1], align_bytes=64)
         nc.scalar.copy(
             rounded0[:].rearrange("p (g i) t -> p g t i", i=PACK),
             result0[:].rearrange("p t (g i) -> p g t i", i=PACK),
         )
         result1 = store_result(1)
-        fetch(LAST, 2)
+        fetch(LAST, PACK - 1)
         second_product(2)
-        fetch(LAST, 3)
 
         HALF = CHUNK // 2
         halves = (slice(0, HALF), slice(HALF, CHUNK))
-        larger3 = [pooled(LAST_LARGER_FIRST, HALF), late.tile([P, PACK, 1, HALF], F32, offset=LAST_LARGER_AT, name="larger3")[:]]
+        larger3 = [pooled(LARGER3 + h * PACK * HALF, HALF) for h in range(2)]
         smaller3 = [
             late.tile([P, PACK, 1, HALF], F32, offset=at, name=f"smaller3_{h}")[:] for h, at in enumerate(LAST_SMALLER_AT)
         ]
-        for tiles in (slice(0, PACK - 1), slice(PACK - 1, PACK)):
-            pool(larger3[0][:, tiles, 0], LAST, tiles, MAX, halves[0])
-        pool(larger3[1][:, :, 0], LAST, every, MAX, halves[1])
-        for h in range(2):
-            pool(smaller3[h][:, :, 0], LAST, every, MIN, halves[h])
+        for values, op in ((larger3, MAX), (smaller3, MIN)):
+            for h in range(2):
+                pool(values[h][:, :, 0], LAST, every, op, halves[h])
         last_banks = [psum.tile([P, CHUNK], F32, tag="bank", name="bank") for t in range(PACK)]
         for w, (kind, values) in enumerate(((larger_kind, larger3), (smaller_kind, smaller3))):
             for h in range(2):
@@ -325,7 +311,7 @@ def tile_picked_winmax_silu_po_kernel(
             for t in range(PACK):
                 multiply(LAST, t, w, last_banks[t][:])
 
-        rounded1 = late.tile([P, CHUNK, PACK], BF16, offset=LAST_LARGER_AT, align_bytes=64)
+        rounded1 = late.tile([P, CHUNK, PACK], BF16, offset=ROUNDED1_AT, align_bytes=64)
         nc.vector.tensor_copy(
             rounded1[:].rearrange("p (g i) t -> p g t i", i=PACK),
             result1[:].rearrange("p t (g i) -> p g t i", i=PACK),

@@ -99,13 +99,16 @@ def tile_picked_winmax_silu_po_kernel(
                 first = 32 * q + 4 * w
                 nc.sync.dma_start(ws_raw[first : first + 4, :].bitcast(I32), rows[4 * q : 4 * q + 4, :])
 
-        w1_bf = early.tile([P, PACK, P, PACK], BF16, offset=W1_BF_AT, align_bytes=64)
-        w1_dealt = w1_bf[:].rearrange("p t m j -> p m j t")
+        w1_bf = [
+            early.tile([P, 2, P, PACK], BF16, offset=W1_BF_AT + 1024, align_bytes=64, name=f"w1_bf{pair}")
+            for pair in range(2)
+        ]
 
-        def round_w1(half, tiles):
+        def round_w1(half, pair, copy, first=0, count=P // 2):
             source = w1_raw[half][:].rearrange("p j (m t) -> p m j t", t=PACK)
-            places = slice(half * (P // 2), (half + 1) * (P // 2))
-            nc.scalar.copy(w1_dealt[:, places, :, tiles], source[:, :, :, tiles])
+            places = slice(half * (P // 2) + first, half * (P // 2) + first + count)
+            dealt = w1_bf[pair][:].rearrange("p t m j -> p m j t")
+            copy(dealt[:, places], source[:, first : first + count, :, 2 * pair : 2 * pair + 2])
 
         w1_codes = held.tile([P, H], U32, align_bytes=64)
         w1_scales = held.tile([P, H], U8, align_bytes=64)
@@ -115,15 +118,18 @@ def tile_picked_winmax_silu_po_kernel(
             nc.vector.quantize_mx(
                 out=w1_codes[:, cols].bitcast(FP8X4),
                 scales=w1_scales[:, cols],
-                in_=w1_bf[:, tiles].rearrange("p t m j -> p (t m j)"),
+                in_=w1_bf[tiles.start // 2][:, tiles.start % 2 : (tiles.stop - 1) % 2 + 1].rearrange("p t m j -> p (t m j)"),
             )
 
         low, high, every = slice(0, 2), slice(2, PACK), slice(0, PACK)
-        round_w1(0, every)
-        round_w1(1, low)
-        round_w1(1, high)
-        for tiles in (slice(0, 1), slice(1, 2), high):
+        round_w1(0, 0, nc.scalar.copy)
+        round_w1(1, 0, nc.scalar.copy, 0, P // 4)
+        round_w1(1, 0, nc.vector.tensor_copy, P // 4, P // 4)
+        for tiles in (slice(0, 1), slice(1, 2)):
             quantise_w1(tiles)
+        round_w1(1, 1, nc.scalar.copy)
+        round_w1(0, 1, nc.vector.tensor_copy)
+        quantise_w1(high)
 
         w23_codes = [
             early.tile([P, PACK, P], I32, offset=W1_BF_AT + w * 2048, align_bytes=64, name=f"w23_codes{w}")

@@ -23,25 +23,31 @@ PACK = 4
 BANK = 512
 CHUNK = 128
 SPAN = 2 * CHUNK
+STEP = 2 * SPAN
+HALF = CHUNK // 2
 LAST = V // CHUNK - 1
+X_AHEAD = T // 8
 GPSIMD_TILES = 3
 
 XS_WINDOW_AT = 2048
 W2_RAW_AT, WS_RAW_AT, W3_RAW_AT = 256, 2304, 2816
-W1_BF_AT = 5376
-ROUNDED1_AT = 2560
-LAST_SMALLER_AT = (3072, 4096)
+SUMS_AT = WS_RAW_AT
+W1_BF_AT = 6400
+W23_CODES_AT = (5376, 7424)
 Z_AT = {1: 0, 2: 3072}
+ROUNDED0_AT = Z_AT[1]
+SMALLER3_AT = (3072, 4096)
+ROUNDED1_AT = 2560
 OUT_SCALES_AT = 4096
 RESULT23_AT = 4608
+FIRST_SLOT = (0, SPAN, 0, STEP + SPAN)
 SMALLER1 = 2304
-SMALLER2 = 2816
-LARGER3 = 2816
+SMALLER2 = LARGER3 = 2816
 LARGER1 = 3200
 SMALLER0 = 3264
 LARGER2 = 3584
 LARGER0 = 3840
-ROW = 4352
+ROW = LARGER0 + PACK * CHUNK
 
 
 def tile_picked_winmax_silu_po_kernel(
@@ -61,22 +67,22 @@ def tile_picked_winmax_silu_po_kernel(
         w1_raw = [held.tile([P, PACK, H // 2], F32, name=f"w1_raw{half}") for half in range(2)]
 
         nc.sync.dma_start(offs_sb[:], offs)
-        nc.sync.dma_start(
-            xs_window[:].bitcast(I32),
-            x_scales[0].bitcast(I32).rearrange("q (one c) -> q one c", one=1).to_broadcast([16, 8, T // 4]),
-        )
-        nc.sync.dma_start(xw_window[:].bitcast(I32), x_words[0].rearrange("p c r -> p (c r)").bitcast(I32))
+        nc.sync.dma_start(order_sb[:], order)
+        nc.vector.memset(xs_window[:].bitcast(I32), 0)
+        x_rows = x_words[0].rearrange("p c r -> p (c r)").bitcast(I32)
+        nc.sync.dma_start(xw_window[:, 0:X_AHEAD].bitcast(I32), x_rows[:, 0:X_AHEAD])
+        nc.sync.dma_start(xs_window[0:P:8, :].bitcast(I32), x_scales[0].bitcast(I32))
+        nc.sync.dma_start(xw_window[:, X_AHEAD:T].bitcast(I32), x_rows[:, X_AHEAD:T])
         w1_rows = w1.rearrange("(p j) h -> p j h", j=PACK)
         for half in range(2):
             nc.sync.dma_start(w1_raw[half][:], w1_rows[:, :, half * (H // 2) : (half + 1) * (H // 2)])
-        nc.sync.dma_start(order_sb[:], order)
 
         warm = held.tile([P, 2], F32)
         nc.vector.memset(warm[:, 0:1], 0.0)
         nc.scalar.activation(warm[:, 1:2], warm[:, 0:1], SILU)
 
         xq_scales = held.tile([P, S], U8, align_bytes=64)
-        nc.gpsimd.memset(xq_scales[:].bitcast(I32), 0)
+        nc.vector.memset(xq_scales[:].bitcast(I32), 0)
 
         xs_picked = held.tile([P, S], U8, align_bytes=64)
         nc.vector.tensor_copy(xs_picked[:], xs_window[:].indirect(offs_sb[:]))
@@ -100,40 +106,39 @@ def tile_picked_winmax_silu_po_kernel(
                 nc.sync.dma_start(ws_raw[first : first + 4, :].bitcast(I32), rows[4 * q : 4 * q + 4, :])
 
         w1_bf = [
-            early.tile([P, 2, P, PACK], BF16, offset=W1_BF_AT + 1024, align_bytes=64, name=f"w1_bf{pair}")
+            early.tile([P, 2, P, PACK], BF16, offset=W1_BF_AT, align_bytes=64, name=f"w1_bf{pair}")
             for pair in range(2)
         ]
 
         def round_w1(half, pair, copy, first=0, count=P // 2):
             source = w1_raw[half][:].rearrange("p j (m t) -> p m j t", t=PACK)
             places = slice(half * (P // 2) + first, half * (P // 2) + first + count)
-            dealt = w1_bf[pair][:].rearrange("p t m j -> p m j t")
+            dealt = w1_bf[pair][:].rearrange("p u m j -> p m j u")
             copy(dealt[:, places], source[:, first : first + count, :, 2 * pair : 2 * pair + 2])
 
         w1_codes = held.tile([P, H], U32, align_bytes=64)
         w1_scales = held.tile([P, H], U8, align_bytes=64)
 
-        def quantise_w1(tiles):
-            cols = slice(tiles.start * P, tiles.stop * P)
+        def quantise_w1(pair, first, count):
+            cols = slice((2 * pair + first) * P, (2 * pair + first + count) * P)
             nc.vector.quantize_mx(
                 out=w1_codes[:, cols].bitcast(FP8X4),
                 scales=w1_scales[:, cols],
-                in_=w1_bf[tiles.start // 2][:, tiles.start % 2 : (tiles.stop - 1) % 2 + 1].rearrange("p t m j -> p (t m j)"),
+                in_=w1_bf[pair][:, first : first + count].rearrange("p u m j -> p (u m j)"),
             )
 
-        low, high, every = slice(0, 2), slice(2, PACK), slice(0, PACK)
         round_w1(0, 0, nc.scalar.copy)
         round_w1(1, 0, nc.scalar.copy, 0, P // 4)
         round_w1(1, 0, nc.vector.tensor_copy, P // 4, P // 4)
-        for tiles in (slice(0, 1), slice(1, 2)):
-            quantise_w1(tiles)
+        for first in range(2):
+            quantise_w1(0, first, 1)
         round_w1(1, 1, nc.scalar.copy)
         round_w1(0, 1, nc.vector.tensor_copy)
-        quantise_w1(high)
+        quantise_w1(1, 0, 2)
 
         w23_codes = [
-            early.tile([P, PACK, P], I32, offset=W1_BF_AT + w * 2048, align_bytes=64, name=f"w23_codes{w}")
-            for w in range(2)
+            early.tile([P, PACK, P], I32, offset=at, align_bytes=64, name=f"w23_codes{w}")
+            for w, at in enumerate(W23_CODES_AT)
         ]
         for w in range(2):
             nc.gpsimd.tensor_copy(
@@ -179,19 +184,17 @@ def tile_picked_winmax_silu_po_kernel(
             z_scales.append(held.tile([P, 2, CHUNK], U8, align_bytes=64, name=f"z_scales{c}"))
         larger_kind, smaller_kind, both_kinds = slice(0, 1), slice(1, 2), slice(0, 2)
 
-        row = held.tile([P, ROW], F32)
-        STEP = 2 * SPAN
+        low, high, every = slice(0, 2), slice(2, PACK), slice(0, PACK)
 
-        def first_slot(c):
-            return (0, SPAN, 0, STEP + SPAN)[c]
+        row = held.tile([P, ROW], F32)
 
         def slot(c, t, count=1):
-            start = first_slot(c) + t * STEP
+            start = FIRST_SLOT[c] + t * STEP
             return row[:, start : start + count * SPAN]
 
         def pairs_of(c):
-            start = first_slot(c)
-            return row[:, start : start + PACK * STEP].rearrange("p (t s v e) -> p t s v e", t=PACK, s=2, e=2)[:, :, 0]
+            steps = row[:, FIRST_SLOT[c] : FIRST_SLOT[c] + PACK * STEP]
+            return steps.rearrange("p (t s v e) -> p t s v e", t=PACK, s=2, e=2)[:, :, 0]
 
         def pooled(at, width=CHUNK):
             return row[:, at : at + PACK * width].rearrange("p (t w v) -> p t w v", t=PACK, w=1)
@@ -252,22 +255,26 @@ def tile_picked_winmax_silu_po_kernel(
             nc.sync.dma_start(out_rows[:, :, cols], result[:])
             return result
 
-        def quantise_result(cols, rounded):
+        def round_result(copy, rounded, result):
+            copy(rounded.rearrange("p (g i) t -> p g t i", i=PACK), result.rearrange("p t (g i) -> p g t i", i=PACK))
+
+        def quantise_result(c, rounded):
+            cols = slice(c * CHUNK, (c + 1) * CHUNK)
             nc.vector.quantize_mx(
                 out=out_codes[:, cols].bitcast(FP8X4),
                 scales=out_scales[:, cols],
                 in_=rounded.rearrange("p v t -> p (v t)"),
             )
 
-        sums = early.tile([P, GPSIMD_TILES, 2, CHUNK], F32, offset=WS_RAW_AT)
+        sums = early.tile([P, GPSIMD_TILES, 2, CHUNK], F32, offset=SUMS_AT)
         for t in range(GPSIMD_TILES):
             fetch(0, t, count=2)
             pairs = slot(0, t, count=2).rearrange("p (v e) -> p v e", e=2)
             nc.gpsimd.tensor_tensor(sums[:, t].rearrange("p c v -> p (c v)"), pairs[:, :, 0], pairs[:, :, 1], ADD)
-        vector_tiles = slice(GPSIMD_TILES, PACK)
         for c in range(2):
             fetch(c, PACK - 1)
 
+        vector_tiles = slice(GPSIMD_TILES, PACK)
         larger0, smaller0 = pooled(LARGER0), pooled(SMALLER0)
         pool(larger0[:, :, 0], 0, every, MAX)
         silu(0, larger_kind, larger0)
@@ -279,6 +286,7 @@ def tile_picked_winmax_silu_po_kernel(
             fetch(2, t)
 
         second_product(0)
+
         for tiles in (slice(1, PACK), slice(0, 1)):
             pool(larger1[:, tiles, 0], 1, tiles, MAX)
         silu(1, larger_kind, larger1)
@@ -291,20 +299,16 @@ def tile_picked_winmax_silu_po_kernel(
             pool(pooled(at)[:, :, 0], 2, every, op)
             silu(2, kind, pooled(at))
         second_product(1)
-        rounded0 = late.tile([P, CHUNK, PACK], BF16, offset=Z_AT[1], align_bytes=64)
-        nc.scalar.copy(
-            rounded0[:].rearrange("p (g i) t -> p g t i", i=PACK),
-            result0[:].rearrange("p t (g i) -> p g t i", i=PACK),
-        )
+        rounded0 = late.tile([P, CHUNK, PACK], BF16, offset=ROUNDED0_AT, align_bytes=64)
+        round_result(nc.scalar.copy, rounded0[:], result0[:])
         result1 = store_result(1)
         fetch(LAST, PACK - 1)
         second_product(2)
 
-        HALF = CHUNK // 2
         halves = (slice(0, HALF), slice(HALF, CHUNK))
         larger3 = [pooled(LARGER3 + h * PACK * HALF, HALF) for h in range(2)]
         smaller3 = [
-            late.tile([P, PACK, 1, HALF], F32, offset=at, name=f"smaller3_{h}")[:] for h, at in enumerate(LAST_SMALLER_AT)
+            late.tile([P, PACK, 1, HALF], F32, offset=at, name=f"smaller3_{h}")[:] for h, at in enumerate(SMALLER3_AT)
         ]
         for values, op in ((larger3, MAX), (smaller3, MIN)):
             for h in range(2):
@@ -318,32 +322,29 @@ def tile_picked_winmax_silu_po_kernel(
                 multiply(LAST, t, w, last_banks[t][:])
 
         rounded1 = late.tile([P, CHUNK, PACK], BF16, offset=ROUNDED1_AT, align_bytes=64)
-        nc.vector.tensor_copy(
-            rounded1[:].rearrange("p (g i) t -> p g t i", i=PACK),
-            result1[:].rearrange("p t (g i) -> p g t i", i=PACK),
-        )
+        round_result(nc.vector.tensor_copy, rounded1[:], result1[:])
         out_scales = late.tile([P, V], U8, offset=OUT_SCALES_AT, align_bytes=64)
         for c, rounded in enumerate((rounded0, rounded1)):
-            quantise_result(slice(c * CHUNK, (c + 1) * CHUNK), rounded[:])
+            quantise_result(c, rounded[:])
         nc.sync.dma_start(out_words[:, 0 : 2 * CHUNK], out_codes[:, 0 : 2 * CHUNK].bitcast(I32))
 
         result23 = late.tile([P, PACK, 2 * CHUNK], F32, offset=RESULT23_AT)
         chunk2, chunk3 = slice(0, CHUNK), slice(CHUNK, 2 * CHUNK)
         empty_banks(2, result23[:, :, chunk2])
         rounded2 = held.tile([P, CHUNK, PACK], BF16, align_bytes=64)
-        nc.vector.tensor_copy(
-            rounded2[:].rearrange("p (g i) t -> p g t i", i=PACK),
-            result23[:, :, chunk2].rearrange("p t (g i) -> p g t i", i=PACK),
-        )
+        round_result(nc.vector.tensor_copy, rounded2[:], result23[:, :, chunk2])
         rounded3 = held.tile([P, CHUNK, PACK], BF16, align_bytes=64)
-        for tiles in (low, high):
+
+        def hand_out_last(tiles):
             for t in range(tiles.start, tiles.stop):
                 nc.scalar.copy(result23[:, t, chunk3], last_banks[t][:])
             nc.sync.dma_start(out_rows[:, tiles, 2 * CHUNK : V], result23[:, tiles])
             nc.vector.tensor_copy(rounded3[:, :, tiles], result23[:, tiles, chunk3].rearrange("p t v -> p v t"))
-            if tiles == low:
-                quantise_result(slice(2 * CHUNK, 3 * CHUNK), rounded2[:])
-        quantise_result(slice(3 * CHUNK, V), rounded3[:])
+
+        hand_out_last(low)
+        quantise_result(2, rounded2[:])
+        hand_out_last(high)
+        quantise_result(LAST, rounded3[:])
         nc.sync.dma_start(out_words[:, 2 * CHUNK : V], out_codes[:, 2 * CHUNK : V].bitcast(I32))
 
         scale_rows = out_2[0].bitcast(I32)

@@ -13,10 +13,9 @@ U16 = mybir.dt.uint16
 U8 = mybir.dt.uint8
 FP8X4 = mybir.dt.float8_e4m3fn_x4
 SILU = mybir.ActivationFunctionType.Silu
+COPY = mybir.ActivationFunctionType.Copy
 MAX = mybir.AluOpType.max
 MIN = mybir.AluOpType.min
-ADD = mybir.AluOpType.add
-SUBTRACT = mybir.AluOpType.subtract
 
 P = 128
 PACK = 4
@@ -27,27 +26,23 @@ STEP = 2 * SPAN
 HALF = CHUNK // 2
 LAST = V // CHUNK - 1
 X_AHEAD = T // 8
-GPSIMD_TILES = 3
 
 XS_WINDOW_AT = 2048
 W2_RAW_AT, WS_RAW_AT, W3_RAW_AT = 256, 2304, 2816
-SUMS_AT = WS_RAW_AT
 W1_BF_AT = 6400
 W23_CODES_AT = (5376, 7424)
-Z_AT = {1: 0, 2: 3072}
-ROUNDED0_AT = Z_AT[1]
-SMALLER3_AT = (3072, 4096)
-ROUNDED1_AT = 2560
-OUT_SCALES_AT = 4096
-RESULT23_AT = 4608
-FIRST_SLOT = (0, SPAN, 0, STEP + SPAN)
-SMALLER1 = 2304
-SMALLER2 = LARGER3 = 2816
-LARGER1 = 3200
-SMALLER0 = 3264
-LARGER2 = 3584
-LARGER0 = 3840
-ROW = LARGER0 + PACK * CHUNK
+Z_CODES_AT = {0: 2048, 1: 7168}
+Z_SCALES_AT = {0: 5632}
+Z_AT = {2: 7168}
+LARGER2_AT, SMALLER2_AT = 512, 2560
+LARGER3_AT = (4736, 5760)
+SMALLER3_AT = (512, 1536)
+ROUNDED_AT = (768, 1792)
+RESULT23_AT = 2816
+FIRST_SLOT = (STEP, STEP + SPAN, 0, 5 * STEP)
+SLOT_STEP = (STEP, STEP, STEP, SPAN)
+SMALLER1 = FIRST_SLOT[LAST]
+ROW = FIRST_SLOT[LAST] + PACK * SPAN
 
 
 def tile_picked_winmax_silu_po_kernel(
@@ -174,38 +169,41 @@ def tile_picked_winmax_silu_po_kernel(
         out_rows = out_0.rearrange("(p t) v -> p t v", t=PACK)
         out_words = out_1[0].rearrange("p v r -> p (v r)").bitcast(I32)
 
-        z, z_codes, z_scales, banks = [], [], [], []
-        for c in range(LAST + 1):
-            if c in Z_AT:
-                z.append(late.tile([P, 2, CHUNK, PACK], BF16, offset=Z_AT[c], align_bytes=64, name=f"z{c}"))
-            else:
-                z.append(held.tile([P, 2, CHUNK, PACK], BF16, align_bytes=64, name=f"z{c}"))
-            z_codes.append(held.tile([P, 2, CHUNK], U32, align_bytes=64, name=f"z_codes{c}"))
-            z_scales.append(held.tile([P, 2, CHUNK], U8, align_bytes=64, name=f"z_scales{c}"))
+        def placed(shape, dtype, name, at):
+            if at is None:
+                return held.tile(shape, dtype, align_bytes=64, name=name)
+            return late.tile(shape, dtype, offset=at, align_bytes=64, name=name)
+
+        z, z_codes, z_scales = {}, {}, {}
+
+        def open_chunk(c):
+            z[c] = placed([P, 2, CHUNK, PACK], BF16, f"z{c}", Z_AT.get(c))
+            z_codes[c] = placed([P, 2, CHUNK], U32, f"z_codes{c}", Z_CODES_AT.get(c))
+            z_scales[c] = placed([P, 2, CHUNK], U8, f"z_scales{c}", Z_SCALES_AT.get(c))
+
         larger_kind, smaller_kind, both_kinds = slice(0, 1), slice(1, 2), slice(0, 2)
-
-        low, high, every = slice(0, 2), slice(2, PACK), slice(0, PACK)
-
+        low, high = slice(0, 2), slice(2, PACK)
         row = held.tile([P, ROW], F32)
 
         def slot(c, t, count=1):
-            start = FIRST_SLOT[c] + t * STEP
+            start = FIRST_SLOT[c] + t * SLOT_STEP[c]
             return row[:, start : start + count * SPAN]
 
-        def pairs_of(c):
-            steps = row[:, FIRST_SLOT[c] : FIRST_SLOT[c] + PACK * STEP]
-            return steps.rearrange("p (t s v e) -> p t s v e", t=PACK, s=2, e=2)[:, :, 0]
+        def fetch(c, t, on_vector, count=1):
+            picked = y[t][:].indirect(order_sb[:, c * (SPAN // 16) : (c + count) * (SPAN // 16)])
+            if on_vector:
+                nc.vector.tensor_copy(slot(c, t, count), picked)
+            else:
+                nc.scalar.activation(slot(c, t, count), picked, COPY)
 
-        def pooled(at, width=CHUNK):
-            return row[:, at : at + PACK * width].rearrange("p (t w v) -> p t w v", t=PACK, w=1)
-
-        def fetch(c, t, count=1):
-            entries = order_sb[:, c * (SPAN // 16) : (c + count) * (SPAN // 16)]
-            nc.vector.tensor_copy(slot(c, t, count), y[t][:].indirect(entries))
-
-        def pool(into, c, tiles, op, cols=slice(0, CHUNK)):
-            pairs = pairs_of(c)
-            nc.vector.tensor_tensor(into, pairs[:, tiles, cols, 0], pairs[:, tiles, cols, 1], op)
+        def pool(into, c, op, cols=slice(0, CHUNK)):
+            first, last = FIRST_SLOT[c], FIRST_SLOT[c] + (PACK - 1) * SLOT_STEP[c] + SPAN
+            if SLOT_STEP[c] == SPAN:
+                pairs = row[:, first:last].rearrange("p (t v e) -> p t v e", t=PACK, e=2)
+            else:
+                steps = row[:, first : first + PACK * STEP]
+                pairs = steps.rearrange("p (t s v e) -> p t s v e", t=PACK, s=2, e=2)[:, :, 0]
+            nc.vector.tensor_tensor(into[:, :, 0], pairs[:, :, cols, 0], pairs[:, :, cols, 1], op)
 
         def silu(c, kinds, values, cols=slice(0, CHUNK)):
             nc.scalar.activation(
@@ -214,11 +212,6 @@ def tile_picked_winmax_silu_po_kernel(
                 SILU,
             )
 
-        def smaller_from_sums(c, larger, smaller):
-            tiles = slice(0, GPSIMD_TILES)
-            nc.gpsimd.tensor_tensor(smaller[:, tiles, 0], sums[:, :, c], larger[:, tiles, 0], SUBTRACT)
-            silu(c, smaller_kind, smaller)
-
         def quantise_z(c, kinds):
             nc.vector.quantize_mx(
                 out=z_codes[c][:, kinds].rearrange("p w v -> p (w v)").bitcast(FP8X4),
@@ -226,111 +219,111 @@ def tile_picked_winmax_silu_po_kernel(
                 in_=z[c][:, kinds].rearrange("p w v t -> p (w v t)"),
             )
 
-        def multiply(c, t, w, into):
+        def multiply(c, t, w, into, start, stop):
             nc.tensor.matmul_mx(
                 out=into,
                 lhsT=w23_codes[w][:, t, :].bitcast(FP8X4),
                 lhsT_scale=w23_scales[4 * w : P, t, :],
                 rhs=z_codes[c][:, w, :].bitcast(FP8X4),
                 rhs_scale=z_scales[c][:, w, :],
-                start=(w == 0),
-                stop=(w == 1),
+                start=start,
+                stop=stop,
             )
 
         def second_product(c):
             quantise_z(c, both_kinds)
-            banks.append([psum.tile([P, 2, CHUNK], F32, tag="bank", name="bank") for half in range(2)])
+            bank = psum.tile([P, PACK, CHUNK], F32, tag="bank", name="bank")
             for t in range(PACK):
                 for w in range(2):
-                    multiply(c, t, w, banks[c][t // 2][:, t % 2, :])
+                    multiply(c, t, w, bank[:, t, :], w == 0, w == 1)
+            return bank
 
-        def empty_banks(c, into):
-            for half, tiles in enumerate((low, high)):
-                nc.scalar.copy(into[:, tiles], banks[c][half][:])
-
-        def store_result(c):
-            cols = slice(c * CHUNK, (c + 1) * CHUNK)
+        def store_result(c, bank, copy):
             result = held.tile([P, PACK, CHUNK], F32, name=f"result{c}")
-            empty_banks(c, result[:])
-            nc.sync.dma_start(out_rows[:, :, cols], result[:])
+            copy(result[:], bank[:])
+            nc.sync.dma_start(out_rows[:, :, c * CHUNK : (c + 1) * CHUNK], result[:])
             return result
 
         def round_result(copy, rounded, result):
             copy(rounded.rearrange("p (g i) t -> p g t i", i=PACK), result.rearrange("p t (g i) -> p g t i", i=PACK))
 
-        def quantise_result(c, rounded):
-            cols = slice(c * CHUNK, (c + 1) * CHUNK)
+        def quantise_result(cols, rounded):
             nc.vector.quantize_mx(
                 out=out_codes[:, cols].bitcast(FP8X4),
                 scales=out_scales[:, cols],
                 in_=rounded.rearrange("p v t -> p (v t)"),
             )
 
-        sums = early.tile([P, GPSIMD_TILES, 2, CHUNK], F32, offset=SUMS_AT)
-        for t in range(GPSIMD_TILES):
-            fetch(0, t, count=2)
-            pairs = slot(0, t, count=2).rearrange("p (v e) -> p v e", e=2)
-            nc.gpsimd.tensor_tensor(sums[:, t].rearrange("p c v -> p (c v)"), pairs[:, :, 0], pairs[:, :, 1], ADD)
+        def pooled_tile(name, at=None, width=CHUNK):
+            return placed([P, PACK, 1, width], F32, name, at)
+
+        fetch(0, 0, True, count=2)
+        fetch(2, 0, True)
+        for t in (1, 2):
+            fetch(0, t, True, count=2)
         for c in range(2):
-            fetch(c, PACK - 1)
+            fetch(c, 3, False)
+        smaller1 = row[:, SMALLER1 : SMALLER1 + PACK * SPAN].rearrange("p (t w v) -> p t w v", t=PACK, w=2)[:, :, 0:1]
+        pooled01 = (
+            (pooled_tile("larger0")[:], pooled_tile("smaller0")[:]),
+            (pooled_tile("larger1")[:], smaller1),
+        )
+        for c in range(2):
+            open_chunk(c)
+            for values, op, kind in zip(pooled01[c], (MAX, MIN), (larger_kind, smaller_kind)):
+                pool(values, c, op)
+                silu(c, kind, values)
+        bank0 = second_product(0)
+        fetch(2, 1, True)
+        bank1 = second_product(1)
+        for c in (2, LAST):
+            for t in (2, 3):
+                fetch(c, t, False)
+        for t in (0, 1):
+            fetch(LAST, t, True)
+        result0 = store_result(0, bank0, nc.vector.tensor_copy)
+        result1 = store_result(1, bank1, nc.scalar.copy)
 
-        vector_tiles = slice(GPSIMD_TILES, PACK)
-        larger0, smaller0 = pooled(LARGER0), pooled(SMALLER0)
-        pool(larger0[:, :, 0], 0, every, MAX)
-        silu(0, larger_kind, larger0)
-        larger1, smaller1 = pooled(LARGER1), pooled(SMALLER1)
-        for c, smaller in enumerate((smaller0, smaller1)):
-            pool(smaller[:, vector_tiles, 0], c, vector_tiles, MIN)
-        smaller_from_sums(0, larger0, smaller0)
-        for t in range(PACK):
-            fetch(2, t)
-
-        second_product(0)
-
-        for tiles in (slice(1, PACK), slice(0, 1)):
-            pool(larger1[:, tiles, 0], 1, tiles, MAX)
-        silu(1, larger_kind, larger1)
-        result0 = store_result(0)
-        smaller_from_sums(1, larger1, smaller1)
-        for t in range(PACK - 1):
-            fetch(LAST, t)
-
-        for at, op, kind in ((LARGER2, MAX, larger_kind), (SMALLER2, MIN, smaller_kind)):
-            pool(pooled(at)[:, :, 0], 2, every, op)
-            silu(2, kind, pooled(at))
-        second_product(1)
-        rounded0 = late.tile([P, CHUNK, PACK], BF16, offset=ROUNDED0_AT, align_bytes=64)
-        round_result(nc.scalar.copy, rounded0[:], result0[:])
-        result1 = store_result(1)
-        fetch(LAST, PACK - 1)
-        second_product(2)
+        open_chunk(2)
+        open_chunk(LAST)
+        for name, at, op, kind in (
+            ("larger2", LARGER2_AT, MAX, larger_kind),
+            ("smaller2", SMALLER2_AT, MIN, smaller_kind),
+        ):
+            values = pooled_tile(name, at)[:]
+            pool(values, 2, op)
+            silu(2, kind, values)
 
         halves = (slice(0, HALF), slice(HALF, CHUNK))
-        larger3 = [pooled(LARGER3 + h * PACK * HALF, HALF) for h in range(2)]
-        smaller3 = [
-            late.tile([P, PACK, 1, HALF], F32, offset=at, name=f"smaller3_{h}")[:] for h, at in enumerate(SMALLER3_AT)
-        ]
-        for values, op in ((larger3, MAX), (smaller3, MIN)):
-            for h in range(2):
-                pool(values[h][:, :, 0], LAST, every, op, halves[h])
+        bank2 = psum.tile([P, PACK, CHUNK], F32, tag="bank", name="bank")
+        for h, kind in enumerate((larger_kind, smaller_kind)):
+            values = pooled_tile(f"larger3_{h}", LARGER3_AT[h], HALF)[:]
+            pool(values, LAST, MAX, halves[h])
+            silu(LAST, larger_kind, values, halves[h])
+            quantise_z(2, kind)
+            for t in range(PACK):
+                multiply(2, t, h, bank2[:, t, :], h == 0 and t == 0, h == 1 and t == PACK - 1)
+        for h in range(2):
+            values = pooled_tile(f"smaller3_{h}", SMALLER3_AT[h], HALF * (h + 1))[:, :, :, 0:HALF]
+            pool(values, LAST, MIN, halves[h])
+            silu(LAST, smaller_kind, values, halves[h])
         last_banks = [psum.tile([P, CHUNK], F32, tag="bank", name="bank") for t in range(PACK)]
-        for w, (kind, values) in enumerate(((larger_kind, larger3), (smaller_kind, smaller3))):
-            for h in range(2):
-                silu(LAST, kind, values[h], halves[h])
+        for w, kind in enumerate((larger_kind, smaller_kind)):
             quantise_z(LAST, kind)
             for t in range(PACK):
-                multiply(LAST, t, w, last_banks[t][:])
+                multiply(LAST, t, w, last_banks[t][:], w == 0, w == 1)
 
-        rounded1 = late.tile([P, CHUNK, PACK], BF16, offset=ROUNDED1_AT, align_bytes=64)
-        round_result(nc.vector.tensor_copy, rounded1[:], result1[:])
-        out_scales = late.tile([P, V], U8, offset=OUT_SCALES_AT, align_bytes=64)
-        for c, rounded in enumerate((rounded0, rounded1)):
-            quantise_result(c, rounded[:])
+        out_scales = held.tile([P, V], U8, align_bytes=64)
+        rounded01 = [placed([P, CHUNK, PACK], BF16, f"rounded{c}", ROUNDED_AT[c]) for c in range(2)]
+        round_result(nc.scalar.copy, rounded01[0][:], result0[:])
+        round_result(nc.vector.tensor_copy, rounded01[1][:], result1[:])
+        for c in (1, 0):
+            quantise_result(slice(c * CHUNK, (c + 1) * CHUNK), rounded01[c][:])
         nc.sync.dma_start(out_words[:, 0 : 2 * CHUNK], out_codes[:, 0 : 2 * CHUNK].bitcast(I32))
 
         result23 = late.tile([P, PACK, 2 * CHUNK], F32, offset=RESULT23_AT)
         chunk2, chunk3 = slice(0, CHUNK), slice(CHUNK, 2 * CHUNK)
-        empty_banks(2, result23[:, :, chunk2])
+        nc.scalar.copy(result23[:, :, chunk2], bank2[:])
         rounded2 = held.tile([P, CHUNK, PACK], BF16, align_bytes=64)
         round_result(nc.vector.tensor_copy, rounded2[:], result23[:, :, chunk2])
         rounded3 = held.tile([P, CHUNK, PACK], BF16, align_bytes=64)
@@ -342,9 +335,9 @@ def tile_picked_winmax_silu_po_kernel(
             nc.vector.tensor_copy(rounded3[:, :, tiles], result23[:, tiles, chunk3].rearrange("p t v -> p v t"))
 
         hand_out_last(low)
-        quantise_result(2, rounded2[:])
+        quantise_result(slice(2 * CHUNK, 3 * CHUNK), rounded2[:])
         hand_out_last(high)
-        quantise_result(LAST, rounded3[:])
+        quantise_result(slice(3 * CHUNK, V), rounded3[:])
         nc.sync.dma_start(out_words[:, 2 * CHUNK : V], out_codes[:, 2 * CHUNK : V].bitcast(I32))
 
         scale_rows = out_2[0].bitcast(I32)

@@ -22,27 +22,20 @@ PACK = 4
 BANK = 512
 CHUNK = 128
 SPAN = 2 * CHUNK
-STEP = 2 * SPAN
 HALF = CHUNK // 2
-LAST = V // CHUNK - 1
 X_AHEAD = T // 8
 
 XS_WINDOW_AT = 2048
 W2_RAW_AT, WS_RAW_AT, W3_RAW_AT = 256, 2304, 2816
-W1_BF_AT = 6400
-W23_CODES_AT = (5376, 7424)
-Z_CODES_AT = {0: 2048, 1: 7168}
-Z_SCALES_AT = {0: 5632}
-Z_AT = {2: 7168}
-LARGER2_AT, SMALLER2_AT = 512, 2560
-LARGER3_AT = (4736, 5760)
-SMALLER3_AT = (512, 1536)
-ROUNDED_AT = (768, 1792)
-RESULT23_AT = 2816
-FIRST_SLOT = (STEP, STEP + SPAN, 0, 5 * STEP)
-SLOT_STEP = (STEP, STEP, STEP, SPAN)
-SMALLER1 = FIRST_SLOT[LAST]
-ROW = FIRST_SLOT[LAST] + PACK * SPAN
+W1_BF_AT = (5120, 8192)
+W23_CODES_AT = (7168, 9216)
+
+SLOTS01, SLOTS2, SLOTS3 = 0, 2048, 3072
+LARGER = (5888, 3328, 4352, 4864)
+SMALLER = (2816, 4096, 5376, 6400)
+ROUNDED01 = 4352
+RESULT2 = 4864
+ARENA = 6912
 
 
 def tile_picked_winmax_silu_po_kernel(
@@ -51,7 +44,6 @@ def tile_picked_winmax_silu_po_kernel(
     nc = tc.nc
     with ExitStack() as ctx:
         held = ctx.enter_context(tc.tile_pool(name="held", bufs=1))
-        late = ctx.enter_context(tc.tile_pool(name="late", bufs=1))
         early = ctx.enter_context(tc.tile_pool(name="early", bufs=1))
         psum = ctx.enter_context(tc.psum_pool(name="psum", bufs=8))
 
@@ -78,7 +70,6 @@ def tile_picked_winmax_silu_po_kernel(
 
         xq_scales = held.tile([P, S], U8, align_bytes=64)
         nc.vector.memset(xq_scales[:].bitcast(I32), 0)
-
         xs_picked = held.tile([P, S], U8, align_bytes=64)
         nc.vector.tensor_copy(xs_picked[:], xs_window[:].indirect(offs_sb[:]))
         for b in range(4):
@@ -101,7 +92,7 @@ def tile_picked_winmax_silu_po_kernel(
                 nc.sync.dma_start(ws_raw[first : first + 4, :].bitcast(I32), rows[4 * q : 4 * q + 4, :])
 
         w1_bf = [
-            early.tile([P, 2, P, PACK], BF16, offset=W1_BF_AT, align_bytes=64, name=f"w1_bf{pair}")
+            early.tile([P, 2, P, PACK], BF16, offset=W1_BF_AT[pair], align_bytes=64, name=f"w1_bf{pair}")
             for pair in range(2)
         ]
 
@@ -122,13 +113,13 @@ def tile_picked_winmax_silu_po_kernel(
                 in_=w1_bf[pair][:, first : first + count].rearrange("p u m j -> p (u m j)"),
             )
 
-        round_w1(0, 0, nc.scalar.copy)
+        for pair in range(2):
+            round_w1(0, pair, nc.scalar.copy)
         round_w1(1, 0, nc.scalar.copy, 0, P // 4)
         round_w1(1, 0, nc.vector.tensor_copy, P // 4, P // 4)
         for first in range(2):
             quantise_w1(0, first, 1)
-        round_w1(1, 1, nc.scalar.copy)
-        round_w1(0, 1, nc.vector.tensor_copy)
+        round_w1(1, 1, nc.vector.tensor_copy)
         quantise_w1(1, 0, 2)
 
         w23_codes = [
@@ -144,7 +135,7 @@ def tile_picked_winmax_silu_po_kernel(
         y = [held.tile([P, S], F32, name=f"y{t}") for t in range(PACK)]
         for t in range(PACK):
             cols = slice(t * P, (t + 1) * P)
-            width = BANK // 2 if t == 0 else BANK
+            width = BANK // 2 if t < 2 else BANK
             for part in range(S // width):
                 places = slice(part * width, (part + 1) * width)
                 bank = psum.tile([P, width], F32, tag="bank")
@@ -157,58 +148,52 @@ def tile_picked_winmax_silu_po_kernel(
                     start=True,
                     stop=True,
                 )
-                if t == 0 and part == 1:
-                    nc.vector.tensor_copy(y[t][:, places], bank[:])
-                else:
-                    nc.scalar.copy(y[t][:, places], bank[:])
+                nc.scalar.copy(y[t][:, places], bank[:])
 
         w23_scales = held.tile([P, PACK, P], U8, align_bytes=64)
         nc.gpsimd.tensor_copy(w23_scales[:], ws_raw[:].rearrange("p (m t) -> p t m", t=PACK))
 
         out_codes = held.tile([P, V], U32, align_bytes=64)
+        out_scales = held.tile([P, V], U8, align_bytes=64)
         out_rows = out_0.rearrange("(p t) v -> p t v", t=PACK)
         out_words = out_1[0].rearrange("p v r -> p (v r)").bitcast(I32)
+        arena = held.tile([P, ARENA], F32, align_bytes=64)
 
-        def placed(shape, dtype, name, at):
-            if at is None:
-                return held.tile(shape, dtype, align_bytes=64, name=name)
-            return late.tile(shape, dtype, offset=at, align_bytes=64, name=name)
-
-        z, z_codes, z_scales = {}, {}, {}
-
-        def open_chunk(c):
-            z[c] = placed([P, 2, CHUNK, PACK], BF16, f"z{c}", Z_AT.get(c))
-            z_codes[c] = placed([P, 2, CHUNK], U32, f"z_codes{c}", Z_CODES_AT.get(c))
-            z_scales[c] = placed([P, 2, CHUNK], U8, f"z_scales{c}", Z_SCALES_AT.get(c))
-
+        z = [held.tile([P, 2, CHUNK, PACK], BF16, align_bytes=64, name=f"z{c}") for c in range(4)]
+        z_codes = [held.tile([P, 2, CHUNK], U32, align_bytes=64, name=f"z_codes{c}") for c in range(4)]
+        z_scales = [held.tile([P, 2, CHUNK], U8, align_bytes=64, name=f"z_scales{c}") for c in range(4)]
         larger_kind, smaller_kind, both_kinds = slice(0, 1), slice(1, 2), slice(0, 2)
-        low, high = slice(0, 2), slice(2, PACK)
-        row = held.tile([P, ROW], F32)
+        whole = slice(0, CHUNK)
 
-        def slot(c, t, count=1):
-            start = FIRST_SLOT[c] + t * SLOT_STEP[c]
-            return row[:, start : start + count * SPAN]
+        def slot_start(c, t):
+            if c < 2:
+                return SLOTS01 + t * 2 * SPAN + c * SPAN
+            return (SLOTS2 if c == 2 else SLOTS3) + t * SPAN
 
         def fetch(c, t, on_vector, count=1):
             picked = y[t][:].indirect(order_sb[:, c * (SPAN // 16) : (c + count) * (SPAN // 16)])
+            into = arena[:, slot_start(c, t) : slot_start(c, t) + count * SPAN]
             if on_vector:
-                nc.vector.tensor_copy(slot(c, t, count), picked)
+                nc.vector.tensor_copy(into, picked)
             else:
-                nc.scalar.activation(slot(c, t, count), picked, COPY)
+                nc.scalar.activation(into, picked, COPY)
 
-        def pool(into, c, op, cols=slice(0, CHUNK)):
-            first, last = FIRST_SLOT[c], FIRST_SLOT[c] + (PACK - 1) * SLOT_STEP[c] + SPAN
-            if SLOT_STEP[c] == SPAN:
-                pairs = row[:, first:last].rearrange("p (t v e) -> p t v e", t=PACK, e=2)
+        def pooled(at, width=CHUNK):
+            return arena[:, at : at + PACK * width].rearrange("p (t v) -> p t v", t=PACK)
+
+        def pool(into, c, op, cols=whole):
+            if c < 2:
+                both = arena[:, SLOTS01 : SLOTS01 + PACK * 2 * SPAN]
+                pairs = both.rearrange("p (t s v e) -> p t s v e", t=PACK, s=2, e=2)[:, :, c]
             else:
-                steps = row[:, first : first + PACK * STEP]
-                pairs = steps.rearrange("p (t s v e) -> p t s v e", t=PACK, s=2, e=2)[:, :, 0]
-            nc.vector.tensor_tensor(into[:, :, 0], pairs[:, :, cols, 0], pairs[:, :, cols, 1], op)
+                first = slot_start(c, 0)
+                pairs = arena[:, first : first + PACK * SPAN].rearrange("p (t v e) -> p t v e", t=PACK, e=2)
+            nc.vector.tensor_tensor(into, pairs[:, :, cols, 0], pairs[:, :, cols, 1], op)
 
-        def silu(c, kinds, values, cols=slice(0, CHUNK)):
+        def silu(c, w, values, cols=whole):
             nc.scalar.activation(
-                z[c][:, kinds, cols].rearrange("p w (g i) t -> p (w g) t i", i=PACK),
-                values.rearrange("p t w (g i) -> p (w g) t i", i=PACK),
+                z[c][:, w, cols].rearrange("p (g i) t -> p g t i", i=PACK),
+                values.rearrange("p t (g i) -> p g t i", i=PACK),
                 SILU,
             )
 
@@ -238,14 +223,14 @@ def tile_picked_winmax_silu_po_kernel(
                     multiply(c, t, w, bank[:, t, :], w == 0, w == 1)
             return bank
 
-        def store_result(c, bank, copy):
-            result = held.tile([P, PACK, CHUNK], F32, name=f"result{c}")
-            copy(result[:], bank[:])
-            nc.sync.dma_start(out_rows[:, :, c * CHUNK : (c + 1) * CHUNK], result[:])
-            return result
+        def store_result(c, result, bank):
+            nc.scalar.copy(result, bank[:])
+            nc.sync.dma_start(out_rows[:, :, c * CHUNK : (c + 1) * CHUNK], result)
 
-        def round_result(copy, rounded, result):
-            copy(rounded.rearrange("p (g i) t -> p g t i", i=PACK), result.rearrange("p t (g i) -> p g t i", i=PACK))
+        def round_result(rounded, result):
+            nc.vector.tensor_copy(
+                rounded.rearrange("p (g i) t -> p g t i", i=PACK), result.rearrange("p t (g i) -> p g t i", i=PACK)
+            )
 
         def quantise_result(cols, rounded):
             nc.vector.quantize_mx(
@@ -254,89 +239,67 @@ def tile_picked_winmax_silu_po_kernel(
                 in_=rounded.rearrange("p v t -> p (v t)"),
             )
 
-        def pooled_tile(name, at=None, width=CHUNK):
-            return placed([P, PACK, 1, width], F32, name, at)
-
         fetch(0, 0, True, count=2)
         fetch(2, 0, True)
-        for t in (1, 2):
-            fetch(0, t, True, count=2)
-        for c in range(2):
-            fetch(c, 3, False)
-        smaller1 = row[:, SMALLER1 : SMALLER1 + PACK * SPAN].rearrange("p (t w v) -> p t w v", t=PACK, w=2)[:, :, 0:1]
-        pooled01 = (
-            (pooled_tile("larger0")[:], pooled_tile("smaller0")[:]),
-            (pooled_tile("larger1")[:], smaller1),
-        )
-        for c in range(2):
-            open_chunk(c)
-            for values, op, kind in zip(pooled01[c], (MAX, MIN), (larger_kind, smaller_kind)):
-                pool(values, c, op)
-                silu(c, kind, values)
-        bank0 = second_product(0)
+        fetch(0, 1, True, count=2)
         fetch(2, 1, True)
+        for c in range(2):
+            fetch(c, 2, True)
+        fetch(2, 2, False)
+        for c in (0, 1, 3):
+            fetch(c, 3, False)
+
+        def pool_and_silu(c, w):
+            at, op = ((LARGER[c], MAX), (SMALLER[c], MIN))[w]
+            pool(pooled(at), c, op)
+            silu(c, w, pooled(at))
+
+        for c in range(2):
+            for w in range(2):
+                pool_and_silu(c, w)
+        bank0 = second_product(0)
+        fetch(2, 3, True)
+        fetch(3, 0, True)
         bank1 = second_product(1)
-        for c in (2, LAST):
-            for t in (2, 3):
-                fetch(c, t, False)
-        for t in (0, 1):
-            fetch(LAST, t, True)
-        result0 = store_result(0, bank0, nc.vector.tensor_copy)
-        result1 = store_result(1, bank1, nc.scalar.copy)
+        for t in (1, 2):
+            fetch(3, t, False)
+        result01 = [held.tile([P, PACK, CHUNK], F32, name=f"result{c}") for c in range(2)]
+        store_result(0, result01[0][:], bank0)
+        for w in range(2):
+            pool_and_silu(2, w)
+        store_result(1, result01[1][:], bank1)
 
-        open_chunk(2)
-        open_chunk(LAST)
-        for name, at, op, kind in (
-            ("larger2", LARGER2_AT, MAX, larger_kind),
-            ("smaller2", SMALLER2_AT, MIN, smaller_kind),
-        ):
-            values = pooled_tile(name, at)[:]
-            pool(values, 2, op)
-            silu(2, kind, values)
-
-        halves = (slice(0, HALF), slice(HALF, CHUNK))
         bank2 = psum.tile([P, PACK, CHUNK], F32, tag="bank", name="bank")
-        for h, kind in enumerate((larger_kind, smaller_kind)):
-            values = pooled_tile(f"larger3_{h}", LARGER3_AT[h], HALF)[:]
-            pool(values, LAST, MAX, halves[h])
-            silu(LAST, larger_kind, values, halves[h])
+        for w, kind in enumerate((larger_kind, smaller_kind)):
+            pool_and_silu(3, w)
             quantise_z(2, kind)
             for t in range(PACK):
-                multiply(2, t, h, bank2[:, t, :], h == 0 and t == 0, h == 1 and t == PACK - 1)
-        for h in range(2):
-            values = pooled_tile(f"smaller3_{h}", SMALLER3_AT[h], HALF * (h + 1))[:, :, :, 0:HALF]
-            pool(values, LAST, MIN, halves[h])
-            silu(LAST, smaller_kind, values, halves[h])
+                multiply(2, t, w, bank2[:, t, :], w == 0 and t == 0, w == 1 and t == PACK - 1)
+
+        rounded01 = arena[:, ROUNDED01 : ROUNDED01 + 2 * SPAN].bitcast(BF16).rearrange("p (v t) -> p v t", t=PACK)
         last_banks = [psum.tile([P, CHUNK], F32, tag="bank", name="bank") for t in range(PACK)]
         for w, kind in enumerate((larger_kind, smaller_kind)):
-            quantise_z(LAST, kind)
+            quantise_z(3, kind)
             for t in range(PACK):
-                multiply(LAST, t, w, last_banks[t][:], w == 0, w == 1)
+                multiply(3, t, w, last_banks[t][:], w == 0, w == 1)
+        for c in range(2):
+            round_result(rounded01[:, c * CHUNK : (c + 1) * CHUNK], result01[c][:])
 
-        out_scales = held.tile([P, V], U8, align_bytes=64)
-        rounded01 = [placed([P, CHUNK, PACK], BF16, f"rounded{c}", ROUNDED_AT[c]) for c in range(2)]
-        round_result(nc.scalar.copy, rounded01[0][:], result0[:])
-        round_result(nc.vector.tensor_copy, rounded01[1][:], result1[:])
-        for c in (1, 0):
-            quantise_result(slice(c * CHUNK, (c + 1) * CHUNK), rounded01[c][:])
+        result2 = pooled(RESULT2)
+        store_result(2, result2, bank2)
+        quantise_result(slice(0, 2 * CHUNK), rounded01)
         nc.sync.dma_start(out_words[:, 0 : 2 * CHUNK], out_codes[:, 0 : 2 * CHUNK].bitcast(I32))
-
-        result23 = late.tile([P, PACK, 2 * CHUNK], F32, offset=RESULT23_AT)
-        chunk2, chunk3 = slice(0, CHUNK), slice(CHUNK, 2 * CHUNK)
-        nc.scalar.copy(result23[:, :, chunk2], bank2[:])
         rounded2 = held.tile([P, CHUNK, PACK], BF16, align_bytes=64)
-        round_result(nc.vector.tensor_copy, rounded2[:], result23[:, :, chunk2])
-        rounded3 = held.tile([P, CHUNK, PACK], BF16, align_bytes=64)
-
-        def hand_out_last(tiles):
-            for t in range(tiles.start, tiles.stop):
-                nc.scalar.copy(result23[:, t, chunk3], last_banks[t][:])
-            nc.sync.dma_start(out_rows[:, tiles, 2 * CHUNK : V], result23[:, tiles])
-            nc.vector.tensor_copy(rounded3[:, :, tiles], result23[:, tiles, chunk3].rearrange("p t v -> p v t"))
-
-        hand_out_last(low)
+        round_result(rounded2[:], result2)
         quantise_result(slice(2 * CHUNK, 3 * CHUNK), rounded2[:])
-        hand_out_last(high)
+
+        result3 = held.tile([P, PACK, CHUNK], F32)
+        rounded3 = held.tile([P, CHUNK, PACK], BF16, align_bytes=64)
+        for tiles in (slice(0, 2), slice(2, PACK)):
+            for t in range(tiles.start, tiles.stop):
+                nc.scalar.copy(result3[:, t, :], last_banks[t][:])
+            nc.sync.dma_start(out_rows[:, tiles, 3 * CHUNK : V], result3[:, tiles])
+            nc.vector.tensor_copy(rounded3[:, :, tiles], result3[:, tiles].rearrange("p t v -> p v t"))
         quantise_result(slice(3 * CHUNK, V), rounded3[:])
         nc.sync.dma_start(out_words[:, 2 * CHUNK : V], out_codes[:, 2 * CHUNK : V].bitcast(I32))
 

@@ -27,7 +27,7 @@ X_AHEAD = T // 8
 
 XS_WINDOW_AT = 2048
 W2_RAW_AT, WS_RAW_AT, W3_RAW_AT = 256, 2304, 2816
-W1_BF_AT = (5120, 8192)
+W1_BF_AT = (8192, 8192)
 W23_CODES_AT = (7168, 9216)
 
 SLOTS01, SLOTS2, SLOTS3 = 0, 2048, 3072
@@ -113,13 +113,13 @@ def tile_picked_winmax_silu_po_kernel(
                 in_=w1_bf[pair][:, first : first + count].rearrange("p u m j -> p (u m j)"),
             )
 
-        for pair in range(2):
-            round_w1(0, pair, nc.scalar.copy)
+        round_w1(0, 0, nc.scalar.copy)
         round_w1(1, 0, nc.scalar.copy, 0, P // 4)
         round_w1(1, 0, nc.vector.tensor_copy, P // 4, P // 4)
         for first in range(2):
             quantise_w1(0, first, 1)
-        round_w1(1, 1, nc.vector.tensor_copy)
+        round_w1(1, 1, nc.scalar.copy)
+        round_w1(0, 1, nc.vector.tensor_copy)
         quantise_w1(1, 0, 2)
 
         w23_codes = [
@@ -135,7 +135,7 @@ def tile_picked_winmax_silu_po_kernel(
         y = [held.tile([P, S], F32, name=f"y{t}") for t in range(PACK)]
         for t in range(PACK):
             cols = slice(t * P, (t + 1) * P)
-            width = BANK // 2 if t < 2 else BANK
+            width = BANK // 2 if t == 0 else BANK
             for part in range(S // width):
                 places = slice(part * width, (part + 1) * width)
                 bank = psum.tile([P, width], F32, tag="bank")
@@ -148,7 +148,10 @@ def tile_picked_winmax_silu_po_kernel(
                     start=True,
                     stop=True,
                 )
-                nc.scalar.copy(y[t][:, places], bank[:])
+                if t == 0 and part == 1:
+                    nc.vector.tensor_copy(y[t][:, places], bank[:])
+                else:
+                    nc.scalar.copy(y[t][:, places], bank[:])
 
         w23_scales = held.tile([P, PACK, P], U8, align_bytes=64)
         nc.gpsimd.tensor_copy(w23_scales[:], ws_raw[:].rearrange("p (m t) -> p t m", t=PACK))

@@ -24,6 +24,7 @@ CHUNK = 128
 SPAN = 2 * CHUNK
 HALF = CHUNK // 2
 X_AHEAD = T // 8
+WARM_PASSES, WARM_ROWS = 3, 64
 
 XS_WINDOW_AT = 2048
 W2_RAW_AT, WS_RAW_AT, W3_RAW_AT = 256, 2304, 2816
@@ -76,7 +77,22 @@ def tile_picked_winmax_silu_po_kernel(
             queue = nc.sync if b % 2 == 0 else nc.scalar
             queue.dma_start(xq_scales[b:P:32, :].bitcast(I32), xs_picked[8 * b : P : 32, :].bitcast(I32))
         xq_words = held.tile([P, S], U32, align_bytes=64)
-        nc.vector.tensor_copy(xq_words[:], xw_window[:].indirect(offs_sb[:]))
+        for half in range(2):
+            nc.vector.tensor_copy(
+                xq_words[:, half * BANK : (half + 1) * BANK],
+                xw_window[:].indirect(offs_sb[:, half * (BANK // 16) : (half + 1) * (BANK // 16)]),
+            )
+        for turn in range(WARM_PASSES):
+            idle = psum.tile([WARM_ROWS, BANK], F32, tag="bank")
+            nc.tensor.matmul_mx(
+                out=idle[:],
+                lhsT=xq_words[:, 0:WARM_ROWS].bitcast(FP8X4),
+                lhsT_scale=xs_picked[:, 0:WARM_ROWS],
+                rhs=xq_words[:, 0:BANK].bitcast(FP8X4),
+                rhs_scale=xs_picked[:, 0:BANK],
+                start=True,
+                stop=True,
+            )
 
         w23_raw = [
             early.tile([P, N], I32, name=f"w23_raw{w}", offset=at) for w, at in enumerate((W2_RAW_AT, W3_RAW_AT))

@@ -134,8 +134,8 @@ def tile_picked_winmax_silu_po_kernel(
         round_w1(1, 0, nc.vector.tensor_copy, P // 4, P // 4)
         for first in range(2):
             quantise_w1(0, first, 1)
-        round_w1(1, 1, nc.scalar.copy)
-        round_w1(0, 1, nc.vector.tensor_copy)
+        for half in range(2):
+            round_w1(half, 1, nc.vector.tensor_copy)
         quantise_w1(1, 0, 2)
 
         w23_codes = [

@@ -24,7 +24,9 @@ CHUNK = 128
 SPAN = 2 * CHUNK
 HALF = CHUNK // 2
 X_AHEAD = T // 8
-WARM_PASSES, WARM_ROWS = 3, 64
+X_EDGES = (0, S // 4, S // 2, S)
+WARM_ROWS = 64
+WARM_WIDTHS = (CHUNK, CHUNK, CHUNK, BANK, BANK)
 
 XS_WINDOW_AT = 2048
 W2_RAW_AT, WS_RAW_AT, W3_RAW_AT = 256, 2304, 2816
@@ -32,11 +34,12 @@ W1_BF_AT = (8192, 8192)
 W23_CODES_AT = (7168, 9216)
 
 SLOTS01, SLOTS2, SLOTS3 = 0, 2048, 3072
-LARGER = (5888, 3328, 4352, 4864)
-SMALLER = (2816, 4096, 5376, 6400)
+LARGER = (6144, 3328, 4352, 4864)
+SMALLER = (2816, 4096, 5632, 6656)
+RESULT1 = 5376
 ROUNDED01 = 4352
 RESULT2 = 4864
-ARENA = 6912
+ARENA = 7168
 
 
 def tile_picked_winmax_silu_po_kernel(
@@ -77,19 +80,16 @@ def tile_picked_winmax_silu_po_kernel(
             queue = nc.sync if b % 2 == 0 else nc.scalar
             queue.dma_start(xq_scales[b:P:32, :].bitcast(I32), xs_picked[8 * b : P : 32, :].bitcast(I32))
         xq_words = held.tile([P, S], U32, align_bytes=64)
-        for half in range(2):
-            nc.vector.tensor_copy(
-                xq_words[:, half * BANK : (half + 1) * BANK],
-                xw_window[:].indirect(offs_sb[:, half * (BANK // 16) : (half + 1) * (BANK // 16)]),
-            )
-        for turn in range(WARM_PASSES):
-            idle = psum.tile([WARM_ROWS, BANK], F32, tag="bank")
+        for first, last in zip(X_EDGES, X_EDGES[1:]):
+            nc.vector.tensor_copy(xq_words[:, first:last], xw_window[:].indirect(offs_sb[:, first // 16 : last // 16]))
+        for width in WARM_WIDTHS:
+            idle = psum.tile([WARM_ROWS, width], F32, tag="bank")
             nc.tensor.matmul_mx(
                 out=idle[:],
                 lhsT=xq_words[:, 0:WARM_ROWS].bitcast(FP8X4),
                 lhsT_scale=xs_picked[:, 0:WARM_ROWS],
-                rhs=xq_words[:, 0:BANK].bitcast(FP8X4),
-                rhs_scale=xs_picked[:, 0:BANK],
+                rhs=xq_words[:, 0:width].bitcast(FP8X4),
+                rhs_scale=xs_picked[:, 0:width],
                 start=True,
                 stop=True,
             )
@@ -282,11 +282,14 @@ def tile_picked_winmax_silu_po_kernel(
         bank1 = second_product(1)
         for t in (1, 2):
             fetch(3, t, False)
-        result01 = [held.tile([P, PACK, CHUNK], F32, name=f"result{c}") for c in range(2)]
-        store_result(0, result01[0][:], bank0)
+        result0 = held.tile([P, PACK, CHUNK], F32)
+        result1 = arena[:, RESULT1 : RESULT1 + PACK * CHUNK].rearrange("p (t v) -> p t v", t=PACK)
+        result01 = (result0[:], result1)
+        low, high = slice(0, 2), slice(2, PACK)
+        store_result(0, result0[:], bank0)
         for w in range(2):
             pool_and_silu(2, w)
-        store_result(1, result01[1][:], bank1)
+        nc.scalar.copy(result1[:, low], bank1[:, low])
 
         bank2 = psum.tile([P, PACK, CHUNK], F32, tag="bank", name="bank")
         for w, kind in enumerate((larger_kind, smaller_kind)):
@@ -294,6 +297,8 @@ def tile_picked_winmax_silu_po_kernel(
             quantise_z(2, kind)
             for t in range(PACK):
                 multiply(2, t, w, bank2[:, t, :], w == 0 and t == 0, w == 1 and t == PACK - 1)
+        nc.vector.tensor_copy(result1[:, high], bank1[:, high])
+        nc.sync.dma_start(out_rows[:, :, CHUNK : 2 * CHUNK], result1)
 
         rounded01 = arena[:, ROUNDED01 : ROUNDED01 + 2 * SPAN].bitcast(BF16).rearrange("p (v t) -> p v t", t=PACK)
         last_banks = [psum.tile([P, CHUNK], F32, tag="bank", name="bank") for t in range(PACK)]
@@ -302,7 +307,7 @@ def tile_picked_winmax_silu_po_kernel(
             for t in range(PACK):
                 multiply(3, t, w, last_banks[t][:], w == 0, w == 1)
         for c in range(2):
-            round_result(rounded01[:, c * CHUNK : (c + 1) * CHUNK], result01[c][:])
+            round_result(rounded01[:, c * CHUNK : (c + 1) * CHUNK], result01[c])
 
         result2 = pooled(RESULT2)
         store_result(2, result2, bank2)
@@ -314,7 +319,7 @@ def tile_picked_winmax_silu_po_kernel(
 
         result3 = held.tile([P, PACK, CHUNK], F32)
         rounded3 = held.tile([P, CHUNK, PACK], BF16, align_bytes=64)
-        for tiles in (slice(0, 2), slice(2, PACK)):
+        for tiles in (low, high):
             for t in range(tiles.start, tiles.stop):
                 nc.scalar.copy(result3[:, t, :], last_banks[t][:])
             nc.sync.dma_start(out_rows[:, tiles, 3 * CHUNK : V], result3[:, tiles])

@@ -25,8 +25,7 @@ SPAN = 2 * CHUNK
 HALF = CHUNK // 2
 X_AHEAD = T // 8
 X_EDGES = (0, S // 4, S // 2, S)
-WARM_ROWS = 64
-WARM_WIDTHS = (CHUNK, CHUNK, CHUNK, BANK, BANK)
+WARM_SHAPES = ((64, CHUNK), (64, CHUNK), (64, BANK), (64, BANK), (32, BANK))
 
 XS_WINDOW_AT = 2048
 W2_RAW_AT, WS_RAW_AT, W3_RAW_AT = 256, 2304, 2816
@@ -82,12 +81,12 @@ def tile_picked_winmax_silu_po_kernel(
         xq_words = held.tile([P, S], U32, align_bytes=64)
         for first, last in zip(X_EDGES, X_EDGES[1:]):
             nc.vector.tensor_copy(xq_words[:, first:last], xw_window[:].indirect(offs_sb[:, first // 16 : last // 16]))
-        for width in WARM_WIDTHS:
-            idle = psum.tile([WARM_ROWS, width], F32, tag="bank")
+        for rows, width in WARM_SHAPES:
+            idle = psum.tile([rows, width], F32, tag="bank")
             nc.tensor.matmul_mx(
                 out=idle[:],
-                lhsT=xq_words[:, 0:WARM_ROWS].bitcast(FP8X4),
-                lhsT_scale=xs_picked[:, 0:WARM_ROWS],
+                lhsT=xq_words[:, 0:rows].bitcast(FP8X4),
+                lhsT_scale=xs_picked[:, 0:rows],
                 rhs=xq_words[:, 0:width].bitcast(FP8X4),
                 rhs_scale=xs_picked[:, 0:width],
                 start=True,

@@ -25,7 +25,8 @@ SPAN = 2 * CHUNK
 HALF = CHUNK // 2
 X_AHEAD = T // 8
 X_EDGES = (0, S // 4, S // 2, S)
-WARM_SHAPES = ((64, CHUNK), (64, CHUNK), (64, BANK), (64, BANK), (32, BANK))
+WARM_ROWS = 32
+WARM_WIDTHS = (CHUNK, CHUNK, BANK, BANK, BANK)
 
 XS_WINDOW_AT = 2048
 W2_RAW_AT, WS_RAW_AT, W3_RAW_AT = 256, 2304, 2816
@@ -81,17 +82,21 @@ def tile_picked_winmax_silu_po_kernel(
         xq_words = held.tile([P, S], U32, align_bytes=64)
         for first, last in zip(X_EDGES, X_EDGES[1:]):
             nc.vector.tensor_copy(xq_words[:, first:last], xw_window[:].indirect(offs_sb[:, first // 16 : last // 16]))
-        for rows, width in WARM_SHAPES:
-            idle = psum.tile([rows, width], F32, tag="bank")
+
+        def warm_pass(codes, scales, width, moving_scales):
+            idle = psum.tile([WARM_ROWS, width], F32, tag="bank", name="idle")
             nc.tensor.matmul_mx(
                 out=idle[:],
-                lhsT=xq_words[:, 0:rows].bitcast(FP8X4),
-                lhsT_scale=xs_picked[:, 0:rows],
+                lhsT=codes.bitcast(FP8X4),
+                lhsT_scale=scales,
                 rhs=xq_words[:, 0:width].bitcast(FP8X4),
-                rhs_scale=xs_picked[:, 0:width],
+                rhs_scale=moving_scales[:, 0:width],
                 start=True,
                 stop=True,
             )
+
+        for width in WARM_WIDTHS:
+            warm_pass(xq_words[:, 0:WARM_ROWS], xs_picked[:, 0:WARM_ROWS], width, xs_picked)
 
         w23_raw = [
             early.tile([P, N], I32, name=f"w23_raw{w}", offset=at) for w, at in enumerate((W2_RAW_AT, W3_RAW_AT))
@@ -182,6 +187,7 @@ def tile_picked_winmax_silu_po_kernel(
         z_scales = [held.tile([P, 2, CHUNK], U8, align_bytes=64, name=f"z_scales{c}") for c in range(4)]
         larger_kind, smaller_kind, both_kinds = slice(0, 1), slice(1, 2), slice(0, 2)
         whole = slice(0, CHUNK)
+        halves = (slice(0, HALF), slice(HALF, CHUNK))
 
         def slot_start(c, t):
             if c < 2:
@@ -215,11 +221,11 @@ def tile_picked_winmax_silu_po_kernel(
                 SILU,
             )
 
-        def quantise_z(c, kinds):
+        def quantise_z(c, kinds, cols=whole):
             nc.vector.quantize_mx(
-                out=z_codes[c][:, kinds].rearrange("p w v -> p (w v)").bitcast(FP8X4),
-                scales=z_scales[c][:, kinds].rearrange("p w v -> p (w v)"),
-                in_=z[c][:, kinds].rearrange("p w v t -> p (w v t)"),
+                out=z_codes[c][:, kinds, cols].rearrange("p w v -> p (w v)").bitcast(FP8X4),
+                scales=z_scales[c][:, kinds, cols].rearrange("p w v -> p (w v)"),
+                in_=z[c][:, kinds, cols].rearrange("p w v t -> p (w v t)"),
             )
 
         def multiply(c, t, w, into, start, stop):
@@ -268,7 +274,7 @@ def tile_picked_winmax_silu_po_kernel(
             fetch(c, 3, False)
 
         def pool_and_silu(c, w):
-            at, op = ((LARGER[c], MAX), (SMALLER[c], MIN))[w]
+            at, op = (LARGER, SMALLER)[w][c], (MAX, MIN)[w]
             pool(pooled(at), c, op)
             silu(c, w, pooled(at))
 
@@ -279,6 +285,7 @@ def tile_picked_winmax_silu_po_kernel(
         fetch(2, 3, True)
         fetch(3, 0, True)
         bank1 = second_product(1)
+        warm_pass(z_codes[1][:, 0, 0:WARM_ROWS], z_scales[1][:, 0, 0:WARM_ROWS], BANK, xq_scales)
         for t in (1, 2):
             fetch(3, t, False)
         result0 = held.tile([P, PACK, CHUNK], F32)
@@ -292,7 +299,13 @@ def tile_picked_winmax_silu_po_kernel(
 
         bank2 = psum.tile([P, PACK, CHUNK], F32, tag="bank", name="bank")
         for w, kind in enumerate((larger_kind, smaller_kind)):
-            pool_and_silu(3, w)
+            if w == 0:
+                pool_and_silu(3, w)
+            else:
+                for h in range(2):
+                    values = pooled(SMALLER[3] + h * PACK * HALF, HALF)
+                    pool(values, 3, MIN, halves[h])
+                    silu(3, 1, values, halves[h])
             quantise_z(2, kind)
             for t in range(PACK):
                 multiply(2, t, w, bank2[:, t, :], w == 0 and t == 0, w == 1 and t == PACK - 1)
@@ -302,7 +315,8 @@ def tile_picked_winmax_silu_po_kernel(
         rounded01 = arena[:, ROUNDED01 : ROUNDED01 + 2 * SPAN].bitcast(BF16).rearrange("p (v t) -> p v t", t=PACK)
         last_banks = [psum.tile([P, CHUNK], F32, tag="bank", name="bank") for t in range(PACK)]
         for w, kind in enumerate((larger_kind, smaller_kind)):
-            quantise_z(3, kind)
+            for cols in (whole,) if w == 0 else halves:
+                quantise_z(3, kind, cols)
             for t in range(PACK):
                 multiply(3, t, w, last_banks[t][:], w == 0, w == 1)
         for c in range(2):

@@ -21,6 +21,8 @@ P = 128
 PACK = 4
 BANK = 512
 CHUNK = 128
+CHUNKS = V // CHUNK
+LAST = CHUNKS - 1
 SPAN = 2 * CHUNK
 HALF = CHUNK // 2
 X_AHEAD = T // 8
@@ -29,17 +31,29 @@ WARM_ROWS = 32
 WARM_WIDTHS = (CHUNK, CHUNK, BANK, BANK, BANK)
 
 XS_WINDOW_AT = 2048
-W2_RAW_AT, WS_RAW_AT, W3_RAW_AT = 256, 2304, 2816
-W1_BF_AT = (8192, 8192)
+W2_RAW_AT, W3_ROWS_AT, W3_RAW_AT = 256, 2304, 2816
+W1_BF_AT = 8192
 W23_CODES_AT = (7168, 9216)
+W23_SCALES_AT = (11264, W3_RAW_AT)
 
-SLOTS01, SLOTS2, SLOTS3 = 0, 2048, 3072
-LARGER = (6144, 3328, 4352, 4864)
-SMALLER = (2816, 4096, 5632, 6656)
-RESULT1 = 5376
-ROUNDED01 = 4352
-RESULT2 = 4864
-ARENA = 7168
+SLOTS01 = 0
+SLOTS2 = SLOTS01 + 2 * PACK * SPAN
+SLOTS3 = SLOTS2 + PACK * SPAN
+POOLED = PACK * CHUNK
+SMALLER0 = SLOTS2 + 3 * SPAN
+LARGER1 = SLOTS3 + SPAN
+SMALLER1 = SLOTS3 + PACK * SPAN
+LARGER2 = SMALLER1 + POOLED // 2
+LARGER3 = LARGER2 + POOLED
+RESULT1 = LARGER3 + POOLED
+SMALLER2 = RESULT1 + POOLED // 2
+LARGER0 = SMALLER2 + POOLED
+SMALLER3 = LARGER0 + POOLED
+LARGER = (LARGER0, LARGER1, LARGER2, LARGER3)
+SMALLER = (SMALLER0, SMALLER1, SMALLER2, SMALLER3)
+ROUNDED01 = LARGER2
+RESULT2 = LARGER3
+ARENA = SMALLER3 + POOLED
 
 
 def tile_picked_winmax_silu_po_kernel(
@@ -64,6 +78,15 @@ def tile_picked_winmax_silu_po_kernel(
         nc.sync.dma_start(xw_window[:, 0:X_AHEAD].bitcast(I32), x_rows[:, 0:X_AHEAD])
         nc.sync.dma_start(xs_window[0:P:8, :].bitcast(I32), x_scales[0].bitcast(I32))
         nc.sync.dma_start(xw_window[:, X_AHEAD:T].bitcast(I32), x_rows[:, X_AHEAD:T])
+        w2_rows = held.tile([P, N], U8, align_bytes=64)
+        nc.vector.memset(w2_rows[:].bitcast(I32), 0)
+
+        def load_scale_rows(into, scales):
+            rows = scales[0].bitcast(I32)
+            for q in range(4):
+                nc.sync.dma_start(into[32 * q : 32 * q + 4, :].bitcast(I32), rows[4 * q : 4 * q + 4, :])
+
+        load_scale_rows(w2_rows, w2_scales)
         w1_rows = w1.rearrange("(p j) h -> p j h", j=PACK)
         for half in range(2):
             nc.sync.dma_start(w1_raw[half][:], w1_rows[:, :, half * (H // 2) : (half + 1) * (H // 2)])
@@ -83,36 +106,29 @@ def tile_picked_winmax_silu_po_kernel(
         for first, last in zip(X_EDGES, X_EDGES[1:]):
             nc.vector.tensor_copy(xq_words[:, first:last], xw_window[:].indirect(offs_sb[:, first // 16 : last // 16]))
 
-        def warm_pass(codes, scales, width, moving_scales):
-            idle = psum.tile([WARM_ROWS, width], F32, tag="bank", name="idle")
+        for width in WARM_WIDTHS:
+            idle = psum.tile([WARM_ROWS, width], F32, tag="bank")
             nc.tensor.matmul_mx(
                 out=idle[:],
-                lhsT=codes.bitcast(FP8X4),
-                lhsT_scale=scales,
+                lhsT=xq_words[:, 0:WARM_ROWS].bitcast(FP8X4),
+                lhsT_scale=w2_rows[:, 0:WARM_ROWS],
                 rhs=xq_words[:, 0:width].bitcast(FP8X4),
-                rhs_scale=moving_scales[:, 0:width],
+                rhs_scale=w2_rows[:, 0:width],
                 start=True,
                 stop=True,
             )
-
-        for width in WARM_WIDTHS:
-            warm_pass(xq_words[:, 0:WARM_ROWS], xs_picked[:, 0:WARM_ROWS], width, xs_picked)
 
         w23_raw = [
             early.tile([P, N], I32, name=f"w23_raw{w}", offset=at) for w, at in enumerate((W2_RAW_AT, W3_RAW_AT))
         ]
         for w, words in enumerate((w2_words, w3_words)):
             nc.sync.dma_start(w23_raw[w][:], words[0].rearrange("p c r -> p (c r)").bitcast(I32))
-        ws_raw = early.tile([P, N], U8, offset=WS_RAW_AT, align_bytes=64)
-        nc.gpsimd.memset(ws_raw[:].bitcast(I32), 0)
-        for w, scales in enumerate((w2_scales, w3_scales)):
-            rows = scales[0].bitcast(I32)
-            for q in range(4):
-                first = 32 * q + 4 * w
-                nc.sync.dma_start(ws_raw[first : first + 4, :].bitcast(I32), rows[4 * q : 4 * q + 4, :])
+        w3_rows = early.tile([P, N], U8, offset=W3_ROWS_AT, align_bytes=64)
+        nc.gpsimd.memset(w3_rows[:].bitcast(I32), 0)
+        load_scale_rows(w3_rows, w3_scales)
 
         w1_bf = [
-            early.tile([P, 2, P, PACK], BF16, offset=W1_BF_AT[pair], align_bytes=64, name=f"w1_bf{pair}")
+            early.tile([P, 2, P, PACK], BF16, offset=W1_BF_AT, align_bytes=64, name=f"w1_bf{pair}")
             for pair in range(2)
         ]
 
@@ -173,8 +189,12 @@ def tile_picked_winmax_silu_po_kernel(
                 else:
                     nc.scalar.copy(y[t][:, places], bank[:])
 
-        w23_scales = held.tile([P, PACK, P], U8, align_bytes=64)
-        nc.gpsimd.tensor_copy(w23_scales[:], ws_raw[:].rearrange("p (m t) -> p t m", t=PACK))
+        w23_scales = [
+            early.tile([P, PACK, P], U8, offset=at, align_bytes=64, name=f"w23_scales{w}")
+            for w, at in enumerate(W23_SCALES_AT)
+        ]
+        for w, rows in enumerate((w2_rows, w3_rows)):
+            nc.gpsimd.tensor_copy(w23_scales[w][:], rows[:].rearrange("p (m t) -> p t m", t=PACK))
 
         out_codes = held.tile([P, V], U32, align_bytes=64)
         out_scales = held.tile([P, V], U8, align_bytes=64)
@@ -182,12 +202,13 @@ def tile_picked_winmax_silu_po_kernel(
         out_words = out_1[0].rearrange("p v r -> p (v r)").bitcast(I32)
         arena = held.tile([P, ARENA], F32, align_bytes=64)
 
-        z = [held.tile([P, 2, CHUNK, PACK], BF16, align_bytes=64, name=f"z{c}") for c in range(4)]
-        z_codes = [held.tile([P, 2, CHUNK], U32, align_bytes=64, name=f"z_codes{c}") for c in range(4)]
-        z_scales = [held.tile([P, 2, CHUNK], U8, align_bytes=64, name=f"z_scales{c}") for c in range(4)]
+        z = [held.tile([P, 2, CHUNK, PACK], BF16, align_bytes=64, name=f"z{c}") for c in range(CHUNKS)]
+        z_codes = [held.tile([P, 2, CHUNK], U32, align_bytes=64, name=f"z_codes{c}") for c in range(CHUNKS)]
+        z_scales = [held.tile([P, 2, CHUNK], U8, align_bytes=64, name=f"z_scales{c}") for c in range(CHUNKS)]
         larger_kind, smaller_kind, both_kinds = slice(0, 1), slice(1, 2), slice(0, 2)
         whole = slice(0, CHUNK)
         halves = (slice(0, HALF), slice(HALF, CHUNK))
+        low, high = slice(0, 2), slice(2, PACK)
 
         def slot_start(c, t):
             if c < 2:
@@ -202,7 +223,7 @@ def tile_picked_winmax_silu_po_kernel(
             else:
                 nc.scalar.activation(into, picked, COPY)
 
-        def pooled(at, width=CHUNK):
+        def by_tile(at, width=CHUNK):
             return arena[:, at : at + PACK * width].rearrange("p (t v) -> p t v", t=PACK)
 
         def pool(into, c, op, cols=whole):
@@ -221,6 +242,11 @@ def tile_picked_winmax_silu_po_kernel(
                 SILU,
             )
 
+        def pool_and_silu(c, w):
+            values = by_tile((LARGER, SMALLER)[w][c])
+            pool(values, c, (MAX, MIN)[w])
+            silu(c, w, values)
+
         def quantise_z(c, kinds, cols=whole):
             nc.vector.quantize_mx(
                 out=z_codes[c][:, kinds, cols].rearrange("p w v -> p (w v)").bitcast(FP8X4),
@@ -232,7 +258,7 @@ def tile_picked_winmax_silu_po_kernel(
             nc.tensor.matmul_mx(
                 out=into,
                 lhsT=w23_codes[w][:, t, :].bitcast(FP8X4),
-                lhsT_scale=w23_scales[4 * w : P, t, :],
+                lhsT_scale=w23_scales[w][:, t, :],
                 rhs=z_codes[c][:, w, :].bitcast(FP8X4),
                 rhs_scale=z_scales[c][:, w, :],
                 start=start,
@@ -263,66 +289,60 @@ def tile_picked_winmax_silu_po_kernel(
                 in_=rounded.rearrange("p v t -> p (v t)"),
             )
 
-        fetch(0, 0, True, count=2)
-        fetch(2, 0, True)
-        fetch(0, 1, True, count=2)
-        fetch(2, 1, True)
+        for t in range(2):
+            fetch(0, t, True, count=2)
+            fetch(2, t, True)
         for c in range(2):
             fetch(c, 2, True)
         fetch(2, 2, False)
-        for c in (0, 1, 3):
+        for c in (0, 1, LAST):
             fetch(c, 3, False)
-
-        def pool_and_silu(c, w):
-            at, op = (LARGER, SMALLER)[w][c], (MAX, MIN)[w]
-            pool(pooled(at), c, op)
-            silu(c, w, pooled(at))
 
         for c in range(2):
             for w in range(2):
                 pool_and_silu(c, w)
         bank0 = second_product(0)
         fetch(2, 3, True)
-        fetch(3, 0, True)
+        fetch(LAST, 0, True)
         bank1 = second_product(1)
-        warm_pass(z_codes[1][:, 0, 0:WARM_ROWS], z_scales[1][:, 0, 0:WARM_ROWS], BANK, xq_scales)
         for t in (1, 2):
-            fetch(3, t, False)
+            fetch(LAST, t, False)
         result0 = held.tile([P, PACK, CHUNK], F32)
-        result1 = arena[:, RESULT1 : RESULT1 + PACK * CHUNK].rearrange("p (t v) -> p t v", t=PACK)
-        result01 = (result0[:], result1)
-        low, high = slice(0, 2), slice(2, PACK)
+        result1 = by_tile(RESULT1)
         store_result(0, result0[:], bank0)
+
         for w in range(2):
             pool_and_silu(2, w)
         nc.scalar.copy(result1[:, low], bank1[:, low])
 
         bank2 = psum.tile([P, PACK, CHUNK], F32, tag="bank", name="bank")
-        for w, kind in enumerate((larger_kind, smaller_kind)):
-            if w == 0:
-                pool_and_silu(3, w)
-            else:
-                for h in range(2):
-                    values = pooled(SMALLER[3] + h * PACK * HALF, HALF)
-                    pool(values, 3, MIN, halves[h])
-                    silu(3, 1, values, halves[h])
+
+        def multiply_chunk2(w, kind):
             quantise_z(2, kind)
             for t in range(PACK):
                 multiply(2, t, w, bank2[:, t, :], w == 0 and t == 0, w == 1 and t == PACK - 1)
+
+        pool_and_silu(LAST, 0)
+        multiply_chunk2(0, larger_kind)
+        for h in range(2):
+            values = by_tile(SMALLER3 + h * PACK * HALF, HALF)
+            pool(values, LAST, MIN, halves[h])
+            silu(LAST, 1, values, halves[h])
+        multiply_chunk2(1, smaller_kind)
         nc.vector.tensor_copy(result1[:, high], bank1[:, high])
         nc.sync.dma_start(out_rows[:, :, CHUNK : 2 * CHUNK], result1)
 
-        rounded01 = arena[:, ROUNDED01 : ROUNDED01 + 2 * SPAN].bitcast(BF16).rearrange("p (v t) -> p v t", t=PACK)
         last_banks = [psum.tile([P, CHUNK], F32, tag="bank", name="bank") for t in range(PACK)]
-        for w, kind in enumerate((larger_kind, smaller_kind)):
-            for cols in (whole,) if w == 0 else halves:
-                quantise_z(3, kind, cols)
+        for w, (kind, steps) in enumerate(((larger_kind, (whole,)), (smaller_kind, halves))):
+            for cols in steps:
+                quantise_z(LAST, kind, cols)
             for t in range(PACK):
-                multiply(3, t, w, last_banks[t][:], w == 0, w == 1)
-        for c in range(2):
-            round_result(rounded01[:, c * CHUNK : (c + 1) * CHUNK], result01[c])
+                multiply(LAST, t, w, last_banks[t][:], w == 0, w == 1)
 
-        result2 = pooled(RESULT2)
+        rounded01 = arena[:, ROUNDED01 : ROUNDED01 + POOLED].bitcast(BF16).rearrange("p (v t) -> p v t", t=PACK)
+        for c, result in enumerate((result0[:], result1)):
+            round_result(rounded01[:, c * CHUNK : (c + 1) * CHUNK], result)
+        result2 = by_tile(RESULT2)
         store_result(2, result2, bank2)
         quantise_result(slice(0, 2 * CHUNK), rounded01)
         nc.sync.dma_start(out_words[:, 0 : 2 * CHUNK], out_codes[:, 0 : 2 * CHUNK].bitcast(I32))
@@ -335,9 +355,9 @@ def tile_picked_winmax_silu_po_kernel(
         for tiles in (low, high):
             for t in range(tiles.start, tiles.stop):
                 nc.scalar.copy(result3[:, t, :], last_banks[t][:])
-            nc.sync.dma_start(out_rows[:, tiles, 3 * CHUNK : V], result3[:, tiles])
+            nc.sync.dma_start(out_rows[:, tiles, LAST * CHUNK : V], result3[:, tiles])
             nc.vector.tensor_copy(rounded3[:, :, tiles], result3[:, tiles].rearrange("p t v -> p v t"))
-        quantise_result(slice(3 * CHUNK, V), rounded3[:])
+        quantise_result(slice(LAST * CHUNK, V), rounded3[:])
         nc.sync.dma_start(out_words[:, 2 * CHUNK : V], out_codes[:, 2 * CHUNK : V].bitcast(I32))
 
         scale_rows = out_2[0].bitcast(I32)

@@ -24,6 +24,7 @@ CHUNK = 128
 CHUNKS = V // CHUNK
 LAST = CHUNKS - 1
 SPAN = 2 * CHUNK
+RUN = 2
 HALF = CHUNK // 2
 X_AHEAD = T // 8
 X_EDGES = (0, S // 4, S // 2, S)
@@ -237,8 +238,8 @@ def tile_picked_winmax_silu_po_kernel(
 
         def silu(c, w, values, cols=whole):
             nc.scalar.activation(
-                z[c][:, w, cols].rearrange("p (g i) t -> p g t i", i=PACK),
-                values.rearrange("p t (g i) -> p g t i", i=PACK),
+                z[c][:, w, cols].rearrange("p (g i) t -> p g t i", i=RUN),
+                values.rearrange("p t (g i) -> p g t i", i=RUN),
                 SILU,
             )
 
@@ -279,7 +280,7 @@ def tile_picked_winmax_silu_po_kernel(
 
         def round_result(rounded, result):
             nc.vector.tensor_copy(
-                rounded.rearrange("p (g i) t -> p g t i", i=PACK), result.rearrange("p t (g i) -> p g t i", i=PACK)
+                rounded.rearrange("p (g i) t -> p g t i", i=RUN), result.rearrange("p t (g i) -> p g t i", i=RUN)
             )
 
         def quantise_result(cols, rounded):

@@ -28,20 +28,22 @@ RUN = 2
 HALF = CHUNK // 2
 X_AHEAD = T // 8
 X_EDGES = (0, S // 4, S // 2, S)
+SCALAR_EARLY = 3 * P // 8
+VECTOR_SHARE = 320
+QUARTER = S // 4
 WARM_ROWS = 32
 WARM_WIDTHS = (CHUNK, CHUNK, BANK, BANK, BANK)
 
 XS_WINDOW_AT = 2048
 W2_RAW_AT, W3_ROWS_AT, W3_RAW_AT = 256, 2304, 2816
-W1_BF_AT = 8192
+W1_BF_AT = (6144, 8192)
 W23_CODES_AT = (7168, 9216)
 W23_SCALES_AT = (11264, W3_RAW_AT)
 
-SLOTS01 = 0
-SLOTS2 = SLOTS01 + 2 * PACK * SPAN
-SLOTS3 = SLOTS2 + PACK * SPAN
+SLOTS012 = 0
+SLOTS3 = SLOTS012 + LAST * PACK * SPAN
 POOLED = PACK * CHUNK
-SMALLER0 = SLOTS2 + 3 * SPAN
+SMALLER0 = SLOTS3 - SPAN
 LARGER1 = SLOTS3 + SPAN
 SMALLER1 = SLOTS3 + PACK * SPAN
 LARGER2 = SMALLER1 + POOLED // 2
@@ -129,7 +131,7 @@ def tile_picked_winmax_silu_po_kernel(
         load_scale_rows(w3_rows, w3_scales)
 
         w1_bf = [
-            early.tile([P, 2, P, PACK], BF16, offset=W1_BF_AT, align_bytes=64, name=f"w1_bf{pair}")
+            early.tile([P, 2, P, PACK], BF16, offset=W1_BF_AT[pair], align_bytes=64, name=f"w1_bf{pair}")
             for pair in range(2)
         ]
 
@@ -151,12 +153,13 @@ def tile_picked_winmax_silu_po_kernel(
             )
 
         round_w1(0, 0, nc.scalar.copy)
+        round_w1(0, 1, nc.scalar.copy, 0, SCALAR_EARLY)
         round_w1(1, 0, nc.scalar.copy, 0, P // 4)
         round_w1(1, 0, nc.vector.tensor_copy, P // 4, P // 4)
+        round_w1(1, 1, nc.scalar.copy)
         for first in range(2):
             quantise_w1(0, first, 1)
-        for half in range(2):
-            round_w1(half, 1, nc.vector.tensor_copy)
+        round_w1(0, 1, nc.vector.tensor_copy, SCALAR_EARLY, P // 2 - SCALAR_EARLY)
         quantise_w1(1, 0, 2)
 
         w23_codes = [
@@ -170,25 +173,33 @@ def tile_picked_winmax_silu_po_kernel(
             )
 
         y = [held.tile([P, S], F32, name=f"y{t}") for t in range(PACK)]
-        for t in range(PACK):
+
+        def first_product(t, first, width, on_vector):
             cols = slice(t * P, (t + 1) * P)
-            width = BANK // 2 if t == 0 else BANK
-            for part in range(S // width):
-                places = slice(part * width, (part + 1) * width)
-                bank = psum.tile([P, width], F32, tag="bank")
-                nc.tensor.matmul_mx(
-                    out=bank[:],
-                    lhsT=w1_codes[:, cols].bitcast(FP8X4),
-                    lhsT_scale=w1_scales[:, cols],
-                    rhs=xq_words[:, places].bitcast(FP8X4),
-                    rhs_scale=xq_scales[:, places],
-                    start=True,
-                    stop=True,
-                )
-                if t == 0 and part == 1:
-                    nc.vector.tensor_copy(y[t][:, places], bank[:])
-                else:
-                    nc.scalar.copy(y[t][:, places], bank[:])
+            places = slice(first, first + width)
+            bank = psum.tile([P, width], F32, tag="bank", name="bank")
+            nc.tensor.matmul_mx(
+                out=bank[:],
+                lhsT=w1_codes[:, cols].bitcast(FP8X4),
+                lhsT_scale=w1_scales[:, cols],
+                rhs=xq_words[:, places].bitcast(FP8X4),
+                rhs_scale=xq_scales[:, places],
+                start=True,
+                stop=True,
+            )
+            if on_vector:
+                nc.vector.tensor_copy(y[t][:, places], bank[:])
+            else:
+                nc.scalar.copy(y[t][:, places], bank[:])
+
+        for part in range(4):
+            first_product(0, part * QUARTER, QUARTER, part % 2 == 1)
+        first_product(1, 0, QUARTER, True)
+        first_product(1, QUARTER, QUARTER, False)
+        first_product(1, BANK, BANK, False)
+        for t in (2, 3):
+            for part in range(2):
+                first_product(t, part * BANK, BANK, False)
 
         w23_scales = [
             early.tile([P, PACK, P], U8, offset=at, align_bytes=64, name=f"w23_scales{w}")
@@ -211,14 +222,10 @@ def tile_picked_winmax_silu_po_kernel(
         halves = (slice(0, HALF), slice(HALF, CHUNK))
         low, high = slice(0, 2), slice(2, PACK)
 
-        def slot_start(c, t):
-            if c < 2:
-                return SLOTS01 + t * 2 * SPAN + c * SPAN
-            return (SLOTS2 if c == 2 else SLOTS3) + t * SPAN
-
-        def fetch(c, t, on_vector, count=1):
-            picked = y[t][:].indirect(order_sb[:, c * (SPAN // 16) : (c + count) * (SPAN // 16)])
-            into = arena[:, slot_start(c, t) : slot_start(c, t) + count * SPAN]
+        def fetch(t, first, count, on_vector):
+            picked = y[t][:].indirect(order_sb[:, first // 16 : (first + count) // 16])
+            at = SLOTS012 + t * LAST * SPAN + first if first < LAST * SPAN else SLOTS3 + t * SPAN
+            into = arena[:, at : at + count]
             if on_vector:
                 nc.vector.tensor_copy(into, picked)
             else:
@@ -228,12 +235,11 @@ def tile_picked_winmax_silu_po_kernel(
             return arena[:, at : at + PACK * width].rearrange("p (t v) -> p t v", t=PACK)
 
         def pool(into, c, op, cols=whole):
-            if c < 2:
-                both = arena[:, SLOTS01 : SLOTS01 + PACK * 2 * SPAN]
-                pairs = both.rearrange("p (t s v e) -> p t s v e", t=PACK, s=2, e=2)[:, :, c]
+            if c < LAST:
+                three = arena[:, SLOTS012:SLOTS3]
+                pairs = three.rearrange("p (t s v e) -> p t s v e", t=PACK, s=LAST, e=2)[:, :, c]
             else:
-                first = slot_start(c, 0)
-                pairs = arena[:, first : first + PACK * SPAN].rearrange("p (t v e) -> p t v e", t=PACK, e=2)
+                pairs = arena[:, SLOTS3 : SLOTS3 + PACK * SPAN].rearrange("p (t v e) -> p t v e", t=PACK, e=2)
             nc.vector.tensor_tensor(into, pairs[:, :, cols, 0], pairs[:, :, cols, 1], op)
 
         def silu(c, w, values, cols=whole):
@@ -291,23 +297,21 @@ def tile_picked_winmax_silu_po_kernel(
             )
 
         for t in range(2):
-            fetch(0, t, True, count=2)
-            fetch(2, t, True)
-        for c in range(2):
-            fetch(c, 2, True)
-        fetch(2, 2, False)
+            fetch(t, 0, LAST * SPAN, True)
+        fetch(2, 0, VECTOR_SHARE, True)
+        fetch(2, VECTOR_SHARE, LAST * SPAN - VECTOR_SHARE, False)
         for c in (0, 1, LAST):
-            fetch(c, 3, False)
+            fetch(3, c * SPAN, SPAN, False)
 
         for c in range(2):
             for w in range(2):
                 pool_and_silu(c, w)
         bank0 = second_product(0)
-        fetch(2, 3, True)
-        fetch(LAST, 0, True)
+        fetch(3, 2 * SPAN, SPAN, True)
+        fetch(0, LAST * SPAN, SPAN, True)
         bank1 = second_product(1)
         for t in (1, 2):
-            fetch(LAST, t, False)
+            fetch(t, LAST * SPAN, SPAN, False)
         result0 = held.tile([P, PACK, CHUNK], F32)
         result1 = by_tile(RESULT1)
         store_result(0, result0[:], bank0)

@@ -31,8 +31,7 @@ X_EDGES = (0, S // 4, S // 2, S)
 SCALAR_EARLY = 3 * P // 8
 VECTOR_SHARE = 320
 QUARTER = S // 4
-WARM_ROWS = 32
-WARM_WIDTHS = (CHUNK, CHUNK, BANK, BANK, BANK)
+WARM_SHAPES = ((P, QUARTER), (P, QUARTER), (32, BANK), (32, BANK))
 
 XS_WINDOW_AT = 2048
 W2_RAW_AT, W3_ROWS_AT, W3_RAW_AT = 256, 2304, 2816
@@ -109,12 +108,12 @@ def tile_picked_winmax_silu_po_kernel(
         for first, last in zip(X_EDGES, X_EDGES[1:]):
             nc.vector.tensor_copy(xq_words[:, first:last], xw_window[:].indirect(offs_sb[:, first // 16 : last // 16]))
 
-        for width in WARM_WIDTHS:
-            idle = psum.tile([WARM_ROWS, width], F32, tag="bank")
+        for rows, width in WARM_SHAPES:
+            idle = psum.tile([rows, width], F32, tag="bank")
             nc.tensor.matmul_mx(
                 out=idle[:],
-                lhsT=xq_words[:, 0:WARM_ROWS].bitcast(FP8X4),
-                lhsT_scale=w2_rows[:, 0:WARM_ROWS],
+                lhsT=xq_words[:, 0:rows].bitcast(FP8X4),
+                lhsT_scale=w2_rows[:, 0:rows],
                 rhs=xq_words[:, 0:width].bitcast(FP8X4),
                 rhs_scale=w2_rows[:, 0:width],
                 start=True,

@@ -356,11 +356,10 @@ def tile_picked_winmax_silu_po_kernel(
 
         result3 = held.tile([P, PACK, CHUNK], F32)
         rounded3 = held.tile([P, CHUNK, PACK], BF16, align_bytes=64)
-        for tiles in (low, high):
-            for t in range(tiles.start, tiles.stop):
-                nc.scalar.copy(result3[:, t, :], last_banks[t][:])
-            nc.sync.dma_start(out_rows[:, tiles, LAST * CHUNK : V], result3[:, tiles])
-            nc.vector.tensor_copy(rounded3[:, :, tiles], result3[:, tiles].rearrange("p t v -> p v t"))
+        for t in range(PACK):
+            nc.scalar.copy(result3[:, t, :], last_banks[t][:])
+        round_result(rounded3[:], result3[:])
+        nc.sync.dma_start(out_rows[:, :, LAST * CHUNK : V], result3[:])
         quantise_result(slice(LAST * CHUNK, V), rounded3[:])
         nc.sync.dma_start(out_words[:, 2 * CHUNK : V], out_codes[:, 2 * CHUNK : V].bitcast(I32))
 

@@ -16,6 +16,8 @@ SILU = mybir.ActivationFunctionType.Silu
 COPY = mybir.ActivationFunctionType.Copy
 MAX = mybir.AluOpType.max
 MIN = mybir.AluOpType.min
+MULT = mybir.AluOpType.mult
+ADD = mybir.AluOpType.add
 
 P = 128
 PACK = 4
@@ -29,6 +31,7 @@ HALF = CHUNK // 2
 X_AHEAD = T // 8
 X_EDGES = (0, S // 4, S // 2, S)
 SCALAR_EARLY = 3 * P // 8
+GPSIMD_PAIRS = 3 * CHUNK // 4
 VECTOR_SHARE = 320
 QUARTER = S // 4
 WARM_SHAPES = ((P, QUARTER), (P, QUARTER), (32, BANK), (32, BANK))
@@ -53,7 +56,7 @@ LARGER0 = SMALLER2 + POOLED
 SMALLER3 = LARGER0 + POOLED
 LARGER = (LARGER0, LARGER1, LARGER2, LARGER3)
 SMALLER = (SMALLER0, SMALLER1, SMALLER2, SMALLER3)
-ROUNDED01 = LARGER2
+ROUNDED01 = SLOTS3
 RESULT2 = LARGER3
 ARENA = SMALLER3 + POOLED
 
@@ -317,7 +320,6 @@ def tile_picked_winmax_silu_po_kernel(
 
         for w in range(2):
             pool_and_silu(2, w)
-        nc.scalar.copy(result1[:, low], bank1[:, low])
 
         bank2 = psum.tile([P, PACK, CHUNK], F32, tag="bank", name="bank")
 
@@ -333,7 +335,7 @@ def tile_picked_winmax_silu_po_kernel(
             pool(values, LAST, MIN, halves[h])
             silu(LAST, 1, values, halves[h])
         multiply_chunk2(1, smaller_kind)
-        nc.vector.tensor_copy(result1[:, high], bank1[:, high])
+        nc.vector.tensor_copy(result1, bank1[:])
         nc.sync.dma_start(out_rows[:, :, CHUNK : 2 * CHUNK], result1)
 
         last_banks = [psum.tile([P, CHUNK], F32, tag="bank", name="bank") for t in range(PACK)]
@@ -344,23 +346,25 @@ def tile_picked_winmax_silu_po_kernel(
                 multiply(LAST, t, w, last_banks[t][:], w == 0, w == 1)
 
         rounded01 = arena[:, ROUNDED01 : ROUNDED01 + POOLED].bitcast(BF16).rearrange("p (v t) -> p v t", t=PACK)
-        for c, result in enumerate((result0[:], result1)):
-            round_result(rounded01[:, c * CHUNK : (c + 1) * CHUNK], result)
+        nc.gpsimd.tensor_scalar(
+            rounded01[:, 0:GPSIMD_PAIRS], result0[:, :, 0:GPSIMD_PAIRS].rearrange("p t v -> p v t"), 1.0, -0.0, MULT, ADD
+        )
+        round_result(rounded01[:, GPSIMD_PAIRS:CHUNK], result0[:, :, GPSIMD_PAIRS:CHUNK])
+        round_result(rounded01[:, CHUNK : 2 * CHUNK], result1)
         result2 = by_tile(RESULT2)
         store_result(2, result2, bank2)
         quantise_result(slice(0, 2 * CHUNK), rounded01)
         nc.sync.dma_start(out_words[:, 0 : 2 * CHUNK], out_codes[:, 0 : 2 * CHUNK].bitcast(I32))
-        rounded2 = held.tile([P, CHUNK, PACK], BF16, align_bytes=64)
-        round_result(rounded2[:], result2)
-        quantise_result(slice(2 * CHUNK, 3 * CHUNK), rounded2[:])
+        rounded2, rounded3 = rounded01[:, 0:CHUNK], rounded01[:, CHUNK : 2 * CHUNK]
+        round_result(rounded2, result2)
+        quantise_result(slice(2 * CHUNK, 3 * CHUNK), rounded2)
 
         result3 = held.tile([P, PACK, CHUNK], F32)
-        rounded3 = held.tile([P, CHUNK, PACK], BF16, align_bytes=64)
         for t in range(PACK):
             nc.scalar.copy(result3[:, t, :], last_banks[t][:])
-        round_result(rounded3[:], result3[:])
+        round_result(rounded3, result3[:])
         nc.sync.dma_start(out_rows[:, :, LAST * CHUNK : V], result3[:])
-        quantise_result(slice(LAST * CHUNK, V), rounded3[:])
+        quantise_result(slice(LAST * CHUNK, V), rounded3)
         nc.sync.dma_start(out_words[:, 2 * CHUNK : V], out_codes[:, 2 * CHUNK : V].bitcast(I32))
 
         scale_rows = out_2[0].bitcast(I32)

@@ -28,9 +28,9 @@ LAST = CHUNKS - 1
 SPAN = 2 * CHUNK
 RUN = 2
 HALF = CHUNK // 2
-X_AHEAD = T // 8
+X_AHEAD = 3 * T // 16
 X_EDGES = (0, S // 4, S // 2, S)
-SCALAR_EARLY = 3 * P // 8
+SCALAR_LATE = 3 * P // 16
 GPSIMD_PAIRS = 3 * CHUNK // 4
 VECTOR_SHARE = 320
 QUARTER = S // 4
@@ -77,7 +77,6 @@ def tile_picked_winmax_silu_po_kernel(
         w1_raw = [held.tile([P, PACK, H // 2], F32, name=f"w1_raw{half}") for half in range(2)]
 
         nc.sync.dma_start(offs_sb[:], offs)
-        nc.sync.dma_start(order_sb[:], order)
         nc.vector.memset(xs_window[:].bitcast(I32), 0)
         x_rows = x_words[0].rearrange("p c r -> p (c r)").bitcast(I32)
         nc.sync.dma_start(xw_window[:, 0:X_AHEAD].bitcast(I32), x_rows[:, 0:X_AHEAD])
@@ -95,6 +94,7 @@ def tile_picked_winmax_silu_po_kernel(
         w1_rows = w1.rearrange("(p j) h -> p j h", j=PACK)
         for half in range(2):
             nc.sync.dma_start(w1_raw[half][:], w1_rows[:, :, half * (H // 2) : (half + 1) * (H // 2)])
+        nc.sync.dma_start(order_sb[:], order)
 
         warm = held.tile([P, 2], F32)
         nc.vector.memset(warm[:, 0:1], 0.0)
@@ -105,8 +105,7 @@ def tile_picked_winmax_silu_po_kernel(
         xs_picked = held.tile([P, S], U8, align_bytes=64)
         nc.vector.tensor_copy(xs_picked[:], xs_window[:].indirect(offs_sb[:]))
         for b in range(4):
-            queue = nc.sync if b % 2 == 0 else nc.scalar
-            queue.dma_start(xq_scales[b:P:32, :].bitcast(I32), xs_picked[8 * b : P : 32, :].bitcast(I32))
+            nc.sync.dma_start(xq_scales[b:P:32, :].bitcast(I32), xs_picked[8 * b : P : 32, :].bitcast(I32))
         xq_words = held.tile([P, S], U32, align_bytes=64)
         for first, last in zip(X_EDGES, X_EDGES[1:]):
             nc.vector.tensor_copy(xq_words[:, first:last], xw_window[:].indirect(offs_sb[:, first // 16 : last // 16]))
@@ -155,13 +154,12 @@ def tile_picked_winmax_silu_po_kernel(
             )
 
         round_w1(0, 0, nc.scalar.copy)
-        round_w1(0, 1, nc.scalar.copy, 0, SCALAR_EARLY)
-        round_w1(1, 0, nc.scalar.copy, 0, P // 4)
-        round_w1(1, 0, nc.vector.tensor_copy, P // 4, P // 4)
+        round_w1(0, 1, nc.scalar.copy)
+        round_w1(1, 0, nc.scalar.copy, 0, SCALAR_LATE)
+        round_w1(1, 0, nc.vector.tensor_copy, SCALAR_LATE, P // 2 - SCALAR_LATE)
         round_w1(1, 1, nc.scalar.copy)
         for first in range(2):
             quantise_w1(0, first, 1)
-        round_w1(0, 1, nc.vector.tensor_copy, SCALAR_EARLY, P // 2 - SCALAR_EARLY)
         quantise_w1(1, 0, 2)
 
         w23_codes = [

@@ -29,7 +29,7 @@ SPAN = 2 * CHUNK
 RUN = 2
 HALF = CHUNK // 2
 X_AHEAD = 3 * T // 16
-X_EDGES = (0, S // 4, S // 2, S)
+X_EDGES = (0, S // 4, S // 2, 3 * S // 4)
 SCALAR_LATE = 3 * P // 16
 GPSIMD_PAIRS = 3 * CHUNK // 4
 VECTOR_SHARE = 320
@@ -106,7 +106,7 @@ def tile_picked_winmax_silu_po_kernel(
         nc.vector.tensor_copy(xs_picked[:], xs_window[:].indirect(offs_sb[:]))
         for b in range(4):
             nc.sync.dma_start(xq_scales[b:P:32, :].bitcast(I32), xs_picked[8 * b : P : 32, :].bitcast(I32))
-        xq_words = held.tile([P, S], U32, align_bytes=64)
+        xq_words = held.tile([P, S - QUARTER], U32, align_bytes=64)
         for first, last in zip(X_EDGES, X_EDGES[1:]):
             nc.vector.tensor_copy(xq_words[:, first:last], xw_window[:].indirect(offs_sb[:, first // 16 : last // 16]))
 
@@ -160,6 +160,8 @@ def tile_picked_winmax_silu_po_kernel(
         round_w1(1, 1, nc.scalar.copy)
         for first in range(2):
             quantise_w1(0, first, 1)
+        xq_last = early.tile([P, QUARTER], U32, offset=W1_BF_AT[0], align_bytes=64)
+        nc.vector.tensor_copy(xq_last[:], xw_window[:].indirect(offs_sb[:, (S - QUARTER) // 16 : S // 16]))
         quantise_w1(1, 0, 2)
 
         w23_codes = [
@@ -178,25 +180,29 @@ def tile_picked_winmax_silu_po_kernel(
             cols = slice(t * P, (t + 1) * P)
             places = slice(first, first + width)
             bank = psum.tile([P, width], F32, tag="bank", name="bank")
-            nc.tensor.matmul_mx(
-                out=bank[:],
-                lhsT=w1_codes[:, cols].bitcast(FP8X4),
-                lhsT_scale=w1_scales[:, cols],
-                rhs=xq_words[:, places].bitcast(FP8X4),
-                rhs_scale=xq_scales[:, places],
-                start=True,
-                stop=True,
-            )
+            step = width if first + width <= BANK else QUARTER
+            for at in range(first, first + width, step):
+                words = xq_words[:, at : at + step] if at < S - QUARTER else xq_last[:]
+                nc.tensor.matmul_mx(
+                    out=bank[:, at - first : at - first + step],
+                    lhsT=w1_codes[:, cols].bitcast(FP8X4),
+                    lhsT_scale=w1_scales[:, cols],
+                    rhs=words.bitcast(FP8X4),
+                    rhs_scale=xq_scales[:, at : at + step],
+                    start=True,
+                    stop=True,
+                )
             if on_vector:
                 nc.vector.tensor_copy(y[t][:, places], bank[:])
             else:
                 nc.scalar.copy(y[t][:, places], bank[:])
 
-        for part in range(4):
-            first_product(0, part * QUARTER, QUARTER, part % 2 == 1)
-        first_product(1, 0, QUARTER, True)
-        first_product(1, QUARTER, QUARTER, False)
-        first_product(1, BANK, BANK, False)
+        for part in range(3):
+            first_product(0, part * QUARTER, QUARTER, False)
+        first_product(1, BANK, QUARTER, False)
+        first_product(1, 0, BANK, True)
+        first_product(0, 3 * QUARTER, QUARTER, False)
+        first_product(1, 3 * QUARTER, QUARTER, True)
         for t in (2, 3):
             for part in range(2):
                 first_product(t, part * BANK, BANK, False)

@@ -32,7 +32,7 @@ X_AHEAD = 3 * T // 16
 X_EDGES = (0, S // 4, S // 2, 3 * S // 4)
 SCALAR_LATE = 3 * P // 16
 GPSIMD_PAIRS = 3 * CHUNK // 4
-VECTOR_SHARE = 320
+VECTOR_SHARE = 256
 QUARTER = S // 4
 WARM_SHAPES = ((P, QUARTER), (P, QUARTER), (32, BANK), (32, BANK))
 

from contextlib import ExitStack

import concourse.mybir as mybir

K, T, S, V, N, H = 512, 2048, 1024, 512, 512, 512
FLOPS = 2 * K * H * S + 2 * 2 * H * N * V

F32 = mybir.dt.float32
BF16 = mybir.dt.bfloat16
I32 = mybir.dt.int32
U32 = mybir.dt.uint32
U16 = mybir.dt.uint16
U8 = mybir.dt.uint8
FP8X4 = mybir.dt.float8_e4m3fn_x4
SILU = mybir.ActivationFunctionType.Silu
COPY = mybir.ActivationFunctionType.Copy
MAX = mybir.AluOpType.max
MIN = mybir.AluOpType.min
MULT = mybir.AluOpType.mult
ADD = mybir.AluOpType.add

P = 128
PACK = 4
BANK = 512
CHUNK = 128
CHUNKS = V // CHUNK
LAST = CHUNKS - 1
SPAN = 2 * CHUNK
RUN = 2
HALF = CHUNK // 2
X_AHEAD = 3 * T // 16
X_EDGES = (0, S // 4, S // 2, 3 * S // 4)
SCALAR_LATE = 3 * P // 16
GPSIMD_PAIRS = 3 * CHUNK // 4
VECTOR_SHARE = 256
QUARTER = S // 4
WARM_SHAPES = ((P, QUARTER), (P, QUARTER), (32, BANK), (32, BANK))

XS_WINDOW_AT = 2048
W2_RAW_AT, W3_ROWS_AT, W3_RAW_AT = 256, 2304, 2816
W1_BF_AT = (6144, 8192)
W23_CODES_AT = (7168, 9216)
W23_SCALES_AT = (11264, W3_RAW_AT)

SLOTS012 = 0
SLOTS3 = SLOTS012 + LAST * PACK * SPAN
POOLED = PACK * CHUNK
SMALLER0 = SLOTS3 - SPAN
LARGER1 = SLOTS3 + SPAN
SMALLER1 = SLOTS3 + PACK * SPAN
LARGER2 = SMALLER1 + POOLED // 2
LARGER3 = LARGER2 + POOLED
RESULT1 = LARGER3 + POOLED
SMALLER2 = RESULT1 + POOLED // 2
LARGER0 = SMALLER2 + POOLED
SMALLER3 = LARGER0 + POOLED
LARGER = (LARGER0, LARGER1, LARGER2, LARGER3)
SMALLER = (SMALLER0, SMALLER1, SMALLER2, SMALLER3)
ROUNDED01 = SLOTS3
RESULT2 = LARGER3
ARENA = SMALLER3 + POOLED


def tile_picked_winmax_silu_po_kernel(
    tc, x_words, x_scales, w1, w2_words, w2_scales, w3_words, w3_scales, offs, order, out_0, out_1, out_2
):
    nc = tc.nc
    with ExitStack() as ctx:
        held = ctx.enter_context(tc.tile_pool(name="held", bufs=1))
        early = ctx.enter_context(tc.tile_pool(name="early", bufs=1))
        psum = ctx.enter_context(tc.psum_pool(name="psum", bufs=8))

        offs_sb = held.tile([P, S // 16], U16)
        order_sb = held.tile([P, S // 16], U16)
        xs_window = early.tile([P, T], U8, offset=XS_WINDOW_AT, align_bytes=64)
        xw_window = held.tile([P, T], U32, align_bytes=64)
        w1_raw = [held.tile([P, PACK, H // 2], F32, name=f"w1_raw{half}") for half in range(2)]

        nc.sync.dma_start(offs_sb[:], offs)
        nc.vector.memset(xs_window[:].bitcast(I32), 0)
        x_rows = x_words[0].rearrange("p c r -> p (c r)").bitcast(I32)
        nc.sync.dma_start(xw_window[:, 0:X_AHEAD].bitcast(I32), x_rows[:, 0:X_AHEAD])
        nc.sync.dma_start(xs_window[0:P:8, :].bitcast(I32), x_scales[0].bitcast(I32))
        nc.sync.dma_start(xw_window[:, X_AHEAD:T].bitcast(I32), x_rows[:, X_AHEAD:T])
        w2_rows = held.tile([P, N], U8, align_bytes=64)
        nc.vector.memset(w2_rows[:].bitcast(I32), 0)

        def load_scale_rows(into, scales):
            rows = scales[0].bitcast(I32)
            for q in range(4):
                nc.sync.dma_start(into[32 * q : 32 * q + 4, :].bitcast(I32), rows[4 * q : 4 * q + 4, :])

        load_scale_rows(w2_rows, w2_scales)
        w1_rows = w1.rearrange("(p j) h -> p j h", j=PACK)
        for half in range(2):
            nc.sync.dma_start(w1_raw[half][:], w1_rows[:, :, half * (H // 2) : (half + 1) * (H // 2)])
        nc.sync.dma_start(order_sb[:], order)

        warm = held.tile([P, 2], F32)
        nc.vector.memset(warm[:, 0:1], 0.0)
        nc.scalar.activation(warm[:, 1:2], warm[:, 0:1], SILU)

        xq_scales = held.tile([P, S], U8, align_bytes=64)
        nc.vector.memset(xq_scales[:].bitcast(I32), 0)
        xs_picked = held.tile([P, S], U8, align_bytes=64)
        nc.vector.tensor_copy(xs_picked[:], xs_window[:].indirect(offs_sb[:]))
        for b in range(4):
            nc.sync.dma_start(xq_scales[b:P:32, :].bitcast(I32), xs_picked[8 * b : P : 32, :].bitcast(I32))
        xq_words = held.tile([P, S - QUARTER], U32, align_bytes=64)
        for first, last in zip(X_EDGES, X_EDGES[1:]):
            nc.vector.tensor_copy(xq_words[:, first:last], xw_window[:].indirect(offs_sb[:, first // 16 : last // 16]))

        for rows, width in WARM_SHAPES:
            idle = psum.tile([rows, width], F32, tag="bank")
            nc.tensor.matmul_mx(
                out=idle[:],
                lhsT=xq_words[:, 0:rows].bitcast(FP8X4),
                lhsT_scale=w2_rows[:, 0:rows],
                rhs=xq_words[:, 0:width].bitcast(FP8X4),
                rhs_scale=w2_rows[:, 0:width],
                start=True,
                stop=True,
            )

        w23_raw = [
            early.tile([P, N], I32, name=f"w23_raw{w}", offset=at) for w, at in enumerate((W2_RAW_AT, W3_RAW_AT))
        ]
        for w, words in enumerate((w2_words, w3_words)):
            nc.sync.dma_start(w23_raw[w][:], words[0].rearrange("p c r -> p (c r)").bitcast(I32))
        w3_rows = early.tile([P, N], U8, offset=W3_ROWS_AT, align_bytes=64)
        nc.gpsimd.memset(w3_rows[:].bitcast(I32), 0)
        load_scale_rows(w3_rows, w3_scales)

        w1_bf = [
            early.tile([P, 2, P, PACK], BF16, offset=W1_BF_AT[pair], align_bytes=64, name=f"w1_bf{pair}")
            for pair in range(2)
        ]

        def round_w1(half, pair, copy, first=0, count=P // 2):
            source = w1_raw[half][:].rearrange("p j (m t) -> p m j t", t=PACK)
            places = slice(half * (P // 2) + first, half * (P // 2) + first + count)
            dealt = w1_bf[pair][:].rearrange("p u m j -> p m j u")
            copy(dealt[:, places], source[:, first : first + count, :, 2 * pair : 2 * pair + 2])

        w1_codes = held.tile([P, H], U32, align_bytes=64)
        w1_scales = held.tile([P, H], U8, align_bytes=64)

        def quantise_w1(pair, first, count):
            cols = slice((2 * pair + first) * P, (2 * pair + first + count) * P)
            nc.vector.quantize_mx(
                out=w1_codes[:, cols].bitcast(FP8X4),
                scales=w1_scales[:, cols],
                in_=w1_bf[pair][:, first : first + count].rearrange("p u m j -> p (u m j)"),
            )

        round_w1(0, 0, nc.scalar.copy)
        round_w1(0, 1, nc.scalar.copy)
        round_w1(1, 0, nc.scalar.copy, 0, SCALAR_LATE)
        round_w1(1, 0, nc.vector.tensor_copy, SCALAR_LATE, P // 2 - SCALAR_LATE)
        round_w1(1, 1, nc.scalar.copy)
        for first in range(2):
            quantise_w1(0, first, 1)
        xq_last = early.tile([P, QUARTER], U32, offset=W1_BF_AT[0], align_bytes=64)
        nc.vector.tensor_copy(xq_last[:], xw_window[:].indirect(offs_sb[:, (S - QUARTER) // 16 : S // 16]))
        quantise_w1(1, 0, 2)

        w23_codes = [
            early.tile([P, PACK, P], I32, offset=at, align_bytes=64, name=f"w23_codes{w}")
            for w, at in enumerate(W23_CODES_AT)
        ]
        for w in range(2):
            nc.gpsimd.tensor_copy(
                w23_codes[w][:].rearrange("p t (g i) -> p g t i", i=PACK),
                w23_raw[w][:].rearrange("p (g i t) -> p g t i", i=PACK, t=PACK),
            )

        y = [held.tile([P, S], F32, name=f"y{t}") for t in range(PACK)]

        def first_product(t, first, width, on_vector):
            cols = slice(t * P, (t + 1) * P)
            places = slice(first, first + width)
            bank = psum.tile([P, width], F32, tag="bank", name="bank")
            step = width if first + width <= BANK else QUARTER
            for at in range(first, first + width, step):
                words = xq_words[:, at : at + step] if at < S - QUARTER else xq_last[:]
                nc.tensor.matmul_mx(
                    out=bank[:, at - first : at - first + step],
                    lhsT=w1_codes[:, cols].bitcast(FP8X4),
                    lhsT_scale=w1_scales[:, cols],
                    rhs=words.bitcast(FP8X4),
                    rhs_scale=xq_scales[:, at : at + step],
                    start=True,
                    stop=True,
                )
            if on_vector:
                nc.vector.tensor_copy(y[t][:, places], bank[:])
            else:
                nc.scalar.copy(y[t][:, places], bank[:])

        for part in range(3):
            first_product(0, part * QUARTER, QUARTER, False)
        first_product(1, BANK, QUARTER, False)
        first_product(1, 0, BANK, True)
        first_product(0, 3 * QUARTER, QUARTER, False)
        first_product(1, 3 * QUARTER, QUARTER, True)
        for t in (2, 3):
            for part in range(2):
                first_product(t, part * BANK, BANK, False)

        w23_scales = [
            early.tile([P, PACK, P], U8, offset=at, align_bytes=64, name=f"w23_scales{w}")
            for w, at in enumerate(W23_SCALES_AT)
        ]
        for w, rows in enumerate((w2_rows, w3_rows)):
            nc.gpsimd.tensor_copy(w23_scales[w][:], rows[:].rearrange("p (m t) -> p t m", t=PACK))

        out_codes = held.tile([P, V], U32, align_bytes=64)
        out_scales = held.tile([P, V], U8, align_bytes=64)
        out_rows = out_0.rearrange("(p t) v -> p t v", t=PACK)
        out_words = out_1[0].rearrange("p v r -> p (v r)").bitcast(I32)
        arena = held.tile([P, ARENA], F32, align_bytes=64)

        z = [held.tile([P, 2, CHUNK, PACK], BF16, align_bytes=64, name=f"z{c}") for c in range(CHUNKS)]
        z_codes = [held.tile([P, 2, CHUNK], U32, align_bytes=64, name=f"z_codes{c}") for c in range(CHUNKS)]
        z_scales = [held.tile([P, 2, CHUNK], U8, align_bytes=64, name=f"z_scales{c}") for c in range(CHUNKS)]
        larger_kind, smaller_kind, both_kinds = slice(0, 1), slice(1, 2), slice(0, 2)
        whole = slice(0, CHUNK)
        halves = (slice(0, HALF), slice(HALF, CHUNK))
        low, high = slice(0, 2), slice(2, PACK)

        def fetch(t, first, count, on_vector):
            picked = y[t][:].indirect(order_sb[:, first // 16 : (first + count) // 16])
            at = SLOTS012 + t * LAST * SPAN + first if first < LAST * SPAN else SLOTS3 + t * SPAN
            into = arena[:, at : at + count]
            if on_vector:
                nc.vector.tensor_copy(into, picked)
            else:
                nc.scalar.activation(into, picked, COPY)

        def by_tile(at, width=CHUNK):
            return arena[:, at : at + PACK * width].rearrange("p (t v) -> p t v", t=PACK)

        def pool(into, c, op, cols=whole):
            if c < LAST:
                three = arena[:, SLOTS012:SLOTS3]
                pairs = three.rearrange("p (t s v e) -> p t s v e", t=PACK, s=LAST, e=2)[:, :, c]
            else:
                pairs = arena[:, SLOTS3 : SLOTS3 + PACK * SPAN].rearrange("p (t v e) -> p t v e", t=PACK, e=2)
            nc.vector.tensor_tensor(into, pairs[:, :, cols, 0], pairs[:, :, cols, 1], op)

        def silu(c, w, values, cols=whole):
            nc.scalar.activation(
                z[c][:, w, cols].rearrange("p (g i) t -> p g t i", i=RUN),
                values.rearrange("p t (g i) -> p g t i", i=RUN),
                SILU,
            )

        def pool_and_silu(c, w):
            values = by_tile((LARGER, SMALLER)[w][c])
            pool(values, c, (MAX, MIN)[w])
            silu(c, w, values)

        def quantise_z(c, kinds, cols=whole):
            nc.vector.quantize_mx(
                out=z_codes[c][:, kinds, cols].rearrange("p w v -> p (w v)").bitcast(FP8X4),
                scales=z_scales[c][:, kinds, cols].rearrange("p w v -> p (w v)"),
                in_=z[c][:, kinds, cols].rearrange("p w v t -> p (w v t)"),
            )

        def multiply(c, t, w, into, start, stop):
            nc.tensor.matmul_mx(
                out=into,
                lhsT=w23_codes[w][:, t, :].bitcast(FP8X4),
                lhsT_scale=w23_scales[w][:, t, :],
                rhs=z_codes[c][:, w, :].bitcast(FP8X4),
                rhs_scale=z_scales[c][:, w, :],
                start=start,
                stop=stop,
            )

        def second_product(c):
            quantise_z(c, both_kinds)
            bank = psum.tile([P, PACK, CHUNK], F32, tag="bank", name="bank")
            for t in range(PACK):
                for w in range(2):
                    multiply(c, t, w, bank[:, t, :], w == 0, w == 1)
            return bank

        def store_result(c, result, bank):
            nc.scalar.copy(result, bank[:])
            nc.sync.dma_start(out_rows[:, :, c * CHUNK : (c + 1) * CHUNK], result)

        def round_result(rounded, result):
            nc.vector.tensor_copy(
                rounded.rearrange("p (g i) t -> p g t i", i=RUN), result.rearrange("p t (g i) -> p g t i", i=RUN)
            )

        def quantise_result(cols, rounded):
            nc.vector.quantize_mx(
                out=out_codes[:, cols].bitcast(FP8X4),
                scales=out_scales[:, cols],
                in_=rounded.rearrange("p v t -> p (v t)"),
            )

        for t in range(2):
            fetch(t, 0, LAST * SPAN, True)
        fetch(2, 0, VECTOR_SHARE, True)
        fetch(2, VECTOR_SHARE, LAST * SPAN - VECTOR_SHARE, False)
        for c in (0, 1, LAST):
            fetch(3, c * SPAN, SPAN, False)

        for c in range(2):
            for w in range(2):
                pool_and_silu(c, w)
        bank0 = second_product(0)
        fetch(3, 2 * SPAN, SPAN, True)
        fetch(0, LAST * SPAN, SPAN, True)
        bank1 = second_product(1)
        for t in (1, 2):
            fetch(t, LAST * SPAN, SPAN, False)
        result0 = held.tile([P, PACK, CHUNK], F32)
        result1 = by_tile(RESULT1)
        store_result(0, result0[:], bank0)

        for w in range(2):
            pool_and_silu(2, w)

        bank2 = psum.tile([P, PACK, CHUNK], F32, tag="bank", name="bank")

        def multiply_chunk2(w, kind):
            quantise_z(2, kind)
            for t in range(PACK):
                multiply(2, t, w, bank2[:, t, :], w == 0 and t == 0, w == 1 and t == PACK - 1)

        pool_and_silu(LAST, 0)
        multiply_chunk2(0, larger_kind)
        for h in range(2):
            values = by_tile(SMALLER3 + h * PACK * HALF, HALF)
            pool(values, LAST, MIN, halves[h])
            silu(LAST, 1, values, halves[h])
        multiply_chunk2(1, smaller_kind)
        nc.vector.tensor_copy(result1, bank1[:])
        nc.sync.dma_start(out_rows[:, :, CHUNK : 2 * CHUNK], result1)

        last_banks = [psum.tile([P, CHUNK], F32, tag="bank", name="bank") for t in range(PACK)]
        for w, (kind, steps) in enumerate(((larger_kind, (whole,)), (smaller_kind, halves))):
            for cols in steps:
                quantise_z(LAST, kind, cols)
            for t in range(PACK):
                multiply(LAST, t, w, last_banks[t][:], w == 0, w == 1)

        rounded01 = arena[:, ROUNDED01 : ROUNDED01 + POOLED].bitcast(BF16).rearrange("p (v t) -> p v t", t=PACK)
        nc.gpsimd.tensor_scalar(
            rounded01[:, 0:GPSIMD_PAIRS], result0[:, :, 0:GPSIMD_PAIRS].rearrange("p t v -> p v t"), 1.0, -0.0, MULT, ADD
        )
        round_result(rounded01[:, GPSIMD_PAIRS:CHUNK], result0[:, :, GPSIMD_PAIRS:CHUNK])
        round_result(rounded01[:, CHUNK : 2 * CHUNK], result1)
        result2 = by_tile(RESULT2)
        store_result(2, result2, bank2)
        quantise_result(slice(0, 2 * CHUNK), rounded01)
        nc.sync.dma_start(out_words[:, 0 : 2 * CHUNK], out_codes[:, 0 : 2 * CHUNK].bitcast(I32))
        rounded2, rounded3 = rounded01[:, 0:CHUNK], rounded01[:, CHUNK : 2 * CHUNK]
        round_result(rounded2, result2)
        quantise_result(slice(2 * CHUNK, 3 * CHUNK), rounded2)

        result3 = held.tile([P, PACK, CHUNK], F32)
        for t in range(PACK):
            nc.scalar.copy(result3[:, t, :], last_banks[t][:])
        round_result(rounded3, result3[:])
        nc.sync.dma_start(out_rows[:, :, LAST * CHUNK : V], result3[:])
        quantise_result(slice(LAST * CHUNK, V), rounded3)
        nc.sync.dma_start(out_words[:, 2 * CHUNK : V], out_codes[:, 2 * CHUNK : V].bitcast(I32))

        scale_rows = out_2[0].bitcast(I32)
        for q in range(4):
            queue = nc.scalar if q % 2 == 0 else nc.sync
            queue.dma_start(scale_rows[4 * q : 4 * q + 4, :], out_scales[32 * q : 32 * q + 4, :].bitcast(I32))
